import numpy as np, ml_dtypes
CORES = [16,18,20,22]
N = 4
BF = ml_dtypes.bfloat16
W, I, C, V, ST = 4096, 256, 1024, 5, 1
def legs(v):
    return np.ascontiguousarray(np.swapaxes(v.reshape(N, 8, 16, I), 2, 3)).astype(np.int32)
def unlegs(v):
    return np.ascontiguousarray(np.swapaxes(v, 2, 3)).reshape(N, 128, I)
def spot(n, al):
    return (((n * (2 * al + 1)) >> 3) + n + 37 * al) & (W - 1)
def pick(x, ix):
    return np.take_along_axis(x, ix.reshape(N, 8, 1, I * 16), 3).reshape(N, 8, 16, I, 16)
def look(x, s, e, l, t, a, b, am):
    run = np.add.accumulate(t, axis=3); tot = run[..., 15:]
    al = (a[..., None] + run) & 255
    be = (b[..., None] + am[:, None, None, None] - (tot - run)) & 255
    f = pick(x, spot(l, al)); g = pick(x, spot(l, be))
    p = s[..., None] + np.add.accumulate(f, axis=4) - f
    q = e[..., None] - (np.add.reduce(g, axis=4, keepdims=True) - np.add.accumulate(g, axis=4) + g)
    d = np.add.reduce(np.minimum(np.abs(p - q), 255), axis=2)
    return f, g, p, tot, d
def parts(rng):
    x = rng.integers(0, 16, (N, 8, 16, W), dtype=np.int32); l = rng.integers(0, W, (N, 8, I, 16), dtype=np.int32); t = rng.integers(0, 256, (N, 8, I, 16), dtype=np.int32)
    a = rng.integers(0, 256, (N, 8, I), dtype=np.int32); c = rng.integers(0, W, (N, 8, 16, C), dtype=np.int32)
    w = rng.integers(0, 256, (N, 8, 16, 1), dtype=np.int32); th = rng.integers(60, 421, (N, 8, I), dtype=np.int32)
    s = rng.integers(0, 136, (N, 8, 16, I), dtype=np.int32)
    closed = rng.random((N, 8, I)) < 0.4
    b = np.where(closed, (a + np.add.reduce(t, axis=3)) & 255, rng.integers(0, 256, (N, 8, I))).astype(np.int32)
    f = look(x, s, s, l, t, a, b, np.zeros(N, np.int32))[0]
    noise = np.rint(rng.standard_normal((N, 8, 16, I)) * rng.choice(np.array([0, 4, 12, 30]), (N, 8, 1, I)))
    e = np.clip(s + np.where(closed[:, :, None, :], np.add.reduce(f, axis=4), 120) + noise, 0, 255).astype(np.int32)
    hit = (rng.random((N, 8, I, 1)) < 0.6) & (np.arange(16) == rng.integers(0, 16, (N, 8, I, 1)))
    t = np.where(hit, (t + rng.integers(1, 256, (N, 8, I, 1))) & 255, t).astype(np.int32)
    return x, s, e, l, t, a, b, c, w, th
def pack(x, s, e, l, t, a, b, c, w, th):
    return {"xt": np.asarray(x, np.float32).reshape(N, 128, W).astype(BF), "sp": np.asarray(s, np.float32).reshape(N, 128, I).astype(BF), "ep": np.asarray(e, np.float32).reshape(N, 128, I).astype(BF),
            "lg": unlegs(np.asarray(l, np.int32)), "tn": unlegs(np.asarray(t, np.int32)), "aa": np.asarray(a, np.int32), "bb": np.asarray(b, np.int32),
            "ct": np.ascontiguousarray(np.asarray(c, np.int32).reshape(N, 128, C)), "wt": np.ascontiguousarray(np.asarray(w, np.int32).reshape(N, 128, 1)), "th": np.asarray(th, np.int32)}
def setup_inputs(rng):
    return pack(*parts(rng))
def setup_inputs_spread(rng):
    x = np.minimum(16 * rng.random((N, 8, 1, W)) ** 0.5 * rng.random((N, 8, 16, W)) ** 0.7, 15).astype(np.int32)
    s = np.minimum(256 * rng.random((N, 8, 1, I)) * rng.random((N, 8, 16, I)) ** 0.5, 255).astype(np.int32)
    e = np.minimum(256 * rng.random((N, 8, 1, I)) ** 0.3 * rng.random((N, 8, 16, I)) ** 0.5, 255).astype(np.int32)
    l = np.minimum(W * rng.random((N, 8, I, 16)) ** rng.choice(np.array([0.25, 1.0, 3.0]), (N, 8, 1, 1)), W - 1).astype(np.int32)
    t = np.minimum(256 * rng.random((N, 8, I, 1)) * rng.random((N, 8, I, 16)), 255).astype(np.int32)
    a = np.minimum(256 * rng.random((N, 8, I)) ** 2, 255).astype(np.int32); b = rng.integers(0, 256, (N, 8, I))
    c = np.minimum(W * rng.random((N, 8, 16, C)) ** rng.choice(np.array([0.25, 1.0, 3.0]), (N, 8, 1, C)), W - 1).astype(np.int32)
    w = np.exp2(8 * rng.random((N, 8, 16, 1))).astype(np.int32) - 1; th = np.minimum(np.exp2(4 + 8 * rng.random((N, 8, I))).astype(np.int32) - 1, 4080)
    return pack(x, s, e, l, t, a, b, c, w, th)
def setup_inputs_ends(rng):
    share = rng.choice(np.array([0.03, 0.3, 0.5, 0.7, 0.97]), (N, 8, 1, 1)); share[0, 0] = 0.0; share[N - 1, 7] = 1.0
    x = 15 * (np.where(rng.random((N, 8, 1, W)) < 0.3, rng.random((N, 8, 16, W)), rng.random((N, 8, 1, W))) < share)
    alike = rng.random((N, 8, 1, I)) < 0.5
    s = 255 * np.where(alike, rng.integers(0, 2, (N, 8, 1, I)), rng.integers(0, 2, (N, 8, 16, I)))
    e = 255 * np.where(alike, rng.integers(0, 2, (N, 8, 1, I)), rng.integers(0, 2, (N, 8, 16, I)))
    for i, lo, hi in ((0, 255, 0), (1, 0, 255), (2, 0, 0), (I - 3, 0, 0), (I - 2, 0, 255), (I - 1, 255, 0)): s[..., i] = lo; e[..., i] = hi
    l = (W - 1) * rng.integers(0, 2, (N, 8, I, 16)); t = 255 * rng.integers(0, 2, (N, 8, I, 16)); l[:, :, I - 1] = W - 1; t[:, :, I - 1] = 255; l[:, :, 0] = 0; t[:, :, 0] = 0
    a = 255 * rng.integers(0, 2, (N, 8, I)); b = 255 * rng.integers(0, 2, (N, 8, I)); c = (W - 1) * rng.integers(0, 2, (N, 8, 16, C))
    w = 255 * rng.integers(0, 2, (N, 8, 16, 1)); w[:, 7] = 255; w[:, 3] = 0
    th = 4080 * rng.integers(0, 2, (N, 8, I)); th[:, ::2, I - 1] = 4080; th[:, 1::2, I - 1] = 0; th[:, 7, I - 1] = 4080 * (np.arange(N) & 1); th[:, 7, 0] = 4080 - th[:, 7, I - 1]
    return pack(x, s, e, l, t, a, b, c, w, th)
def setup_inputs_corners(rng):
    x, s, e, l, t, a, b, c, w, th = parts(rng)
    x[:, 1] = 7; e[:, 1, :, ::2] = np.minimum(s[:, 1, :, ::2] + 112, 255)
    x[:, 3] = 15 * (rng.random((N, 1, W)) < 0.5)
    l[:, 2] = rng.choice(np.array([0, W - 1, W // 2]), (N, I, 16)); c[:, 2] = rng.choice(np.array([0, W - 1, 1]), (N, 16, C)); l[:, 4] = rng.choice(np.array([0, W - 1, 5]), (N, I, 1))
    w[:, 5] = 0; w[:, 6] = 255; w[:, 0] = 255 * rng.integers(0, 2, (N, 16, 1))
    t[:, :, ::8, 0] = (t[:, :, ::8, 0] + 1) & 255; t[:, :, 4::8, 15] = (t[:, :, 4::8, 15] + 255) & 255
    m = np.min(look(x, s, e, l, t, a, b, np.zeros(N, np.int32))[4], axis=3)
    th = np.clip(m + rng.integers(-1, 2, m.shape), 0, 4080)
    return pack(x, s, e, l, t, a, b, c, w, th)
def setup_inputs_crowd(rng):
    x, s, e, l, t, a, b, c, w, th = parts(rng)
    w[:, 0] = 0; w[:, 1] = 255; s[:, 1] = 255
    w[:, 2] = 0; w[:, 2, 0] = 1; s[:, 2, 0] = 254 + rng.integers(0, 2, (N, I))
    w[:, 3] = 0; w[:, 3, 0] = 255; s[:, 3, 0] = 255
    for q in range(N): s[q, 3, 0, rng.integers(0, I)] = 1
    s[:, :, 0] = np.maximum(s[:, :, 0], 1); e[:, :, 0] = np.minimum(e[:, :, 0], s[:, :, 0] - 1)
    for q in range(N):
        g = int(rng.integers(0, 8)); i = int(rng.integers(0, I))
        if q < 4:
            th[q] = (0, 0, 4080, 4080)[q]
            if q & 1: th[q, g, i] = 4080 - th[q, g, i]
        else:
            th[q] = 4080 * rng.integers(0, 2, (8, 1)); th[q, g, i] = 4080 - th[q, g, i]; th[q, (g + 3) % 8, I - 1] = 4080 - th[q, (g + 3) % 8, I - 1]
    return pack(x, s, e, l, t, a, b, c, w, th)
def setup_inputs_falls(rng):
    x, s, e, l, t, a, b, c, w, th = parts(rng)
    e = np.minimum(np.maximum(e, s), s + 200)
    th[:] = 4079; x[:, 5, 0] = 0
    x[:, 6] = 15 - ((rng.integers(0, 16, (N, 1, W)) == np.arange(16)[:, None]) & (rng.random((N, 1, W)) < 0.03125)).astype(np.int32)
    z = rng.random((N, 1, I)) < 0.5; s[:, 6] = np.where(z, 0, s[:, 6]); e[:, 6] = np.where(z, 0, e[:, 6])
    q = int(rng.integers(0, N))
    for i in range(N):
        o = (q - ST * i) % N; n = 32 * int(rng.integers(0, I // 8)) + int(rng.integers(1, 32))
        n = (n, 0, n, 8 * I)[i & 3]
        m = (rng.permutation(8 * I) < n).reshape(8, 1, I)
        s[o] = np.where(m, 255, s[o]); e[o] = np.where(m, 0, e[o])
        near = ~m[5, 0] & (rng.random(I) < 0.25)
        s[o, 5] = np.where(near, 255, s[o, 5]); e[o, 5] = np.where(near, 0, e[o, 5]); s[o, 5, 0] = np.where(near, 254, s[o, 5, 0])
    return pack(x, s, e, l, t, a, b, c, w, th)
def check_inputs(d):
    bad = []
    for k, hi in (("xt", 15), ("sp", 255), ("ep", 255), ("lg", W - 1), ("tn", 255), ("aa", 255), ("bb", 255), ("ct", W - 1), ("wt", 255), ("th", 4080)):
        v = np.asarray(d[k]).astype(np.float64)
        if not (np.min(v) >= 0 and np.max(v) <= hi): bad.append("range of " + k)
        elif np.any(v != np.floor(v)): bad.append("whole numbers in " + k)
    return bad
def reference(xt, sp, ep, lg, tn, aa, bb, ct, wt, th):
    x = xt.astype(np.float32).astype(np.int32).reshape(N, 8, 16, W)
    s = sp.astype(np.float32).astype(np.int32).reshape(N, 8, 16, I); e = ep.astype(np.float32).astype(np.int32).reshape(N, 8, 16, I)
    l = legs(lg); t = legs(tn); a = aa.astype(np.int32); b = bb.astype(np.int32)
    c = ct.astype(np.int32).reshape(N, 8, 16, C); w = wt.astype(np.int32).reshape(N, 8, 16, 1)
    am = np.zeros(N, np.int32); leg = np.arange(16); slot = np.arange(I)
    for v in range(V):
        h = (np.arange(N) - ST * v) % N
        l0, t0, a0, b0 = l[h], t[h], a[h], b[h]
        f, g, p, tot, d = look(x, s[h], e[h], l0, t0, a0, b0, am)
        k = np.argmin(d, axis=3); ok = np.min(d, axis=3) <= th
        at = k[:, :, None, :, None]
        pk, fk, gk = [np.take_along_axis(z, at, 4)[..., 0] for z in (p, f, g)]
        u = np.add.reduce(w * np.minimum(pk, 255), axis=2)
        got = np.swapaxes(np.take_along_axis(c, (u % C)[:, :, None, :], 3), 2, 3)
        t[h] = np.where(ok[..., None] & (leg == k[..., None]), (t0 + (b0 + am[:, None, None] - a0)[..., None] - tot) & 255, t0)
        l[h] = np.where(~ok[..., None] & (leg >= k[..., None]), got, l0)
        pc = np.broadcast_to(((C // I) * slot + u % (C // I))[:, :, None, :], (N, 8, 16, I))
        np.put_along_axis(c, pc, np.where(ok[:, :, None, :], np.take_along_axis(c, pc, 3), np.swapaxes(l0, 2, 3)), 3)
        px = np.broadcast_to(((W // I) * slot + u % (W // I))[:, :, None, :], (N, 8, 16, I))
        np.put_along_axis(x, px, (fk + gk) >> 1, 3)
        am = (np.add.reduce((~ok).astype(np.int32), axis=(1, 2)) & 31).astype(np.int32)
    return {"yx": x.reshape(N, 128, W).astype(np.float32).astype(BF), "yl": unlegs(l).astype(np.float32), "yt": unlegs(t).astype(np.float32), "yc": c.reshape(N, 128, C).astype(np.float32)}

@@ -1,0 +1,447 @@
+from concourse.bass import DstId, RemoteDMATransfer
+from concourse.mybir import AluOpType as A, ActivationFunctionType as AF
+
+NV = 5
+CHUNKS = [(192, 256), (128, 192), (64, 128), (0, 64)]
+BATCHES = [(128, 256), (0, 128)]
+FR = [(192, 256), (128, 192), (0, 128)]
+ROT, EPS, M2 = 167, 2.0 ** -13, 1.5 * 2.0 ** 32
+CYC, GATH, SCAT, HOP, REMOTE = 1.0, 1.55, 3.5, 60.0, 2200.0
+ROUNDS = 5
+BANKS = ["ba", "bb_", "bd", "bu", "bk0", "bk1", "bj0", "bj1"]
+SIZES = {
+    "bfloat16": "xw 4096 ff 4096 nd 4096 sf 4096 vv 4096 mk 1024 dw 2048 ib 128 inb 128 hib 128 onb 256 uw 128 l1 128 l2 128 lda 128 ldb 128 la 128 ka 256 "
+                "kb 256 m128 256 epb 256 qa 256 qb 256 s15 256 s14 256 mp 256 fk 256 ndk 256 rr 256 loc 16 st0 1024 st1 1024 st2 1024 st3 1024",
+    "float32": "cw 2048 ktab 1040 mtab 1040 otab 1040 wf 1 th2 16 onef 128 t1 128 blk 128 idf 128 upf 128 b8 128 diag 256 rst 256 mfw 256 m8 256 "
+               "d2 256 ss 256 ud 256 mg 256 acol 1 qt 512 lb0 256 lb1 256 lb2 256 lb3 256 lb4 256 lo0 256 lo1 256 lo2 256 lo3 256 lo4 256 "
+               "lk0 256 lk1 256 lk2 256 lk3 256 lk4 256",
+    "float16": "ta 128 tb 128 td 128 np 256 tb0 256 tb1 256 tb2 256 tb3 256 tb4 256 td0 256 td1 256 td2 256 td3 256 td4 256",
+    "int32": "cti 1024 lgi 256 tni 256 aai 256 bbi 256 wti 1 p15 256 ei 256 kai 256 rb 16 cb 16 pia 256 pib 256 kint 256 posi 16 us 256 r1 16 "
+             "cg 16 c3 16 n1k 16 k15 16 cod 16 cbv 16 cnt 16 c31 1",
+    "uint16": "fo 256 bo 256 posu 16 ru 16 cgu 16 c3u 16 codu 16"}
+SCRATCH = {n: ("psum", [128, 512], "float32") for n in BANKS}
+for _d in SIZES:
+    _l = SIZES[_d].split()
+    for _i in range(0, len(_l), 2):
+        SCRATCH[_l[_i]] = ("sbuf", [128, int(_l[_i + 1])], _d)
+SCRATCH["ab"] = ("sbuf", [128, 16, 16, 16], "bfloat16")
+SEMAPHORES = ["qV", "qS", "qP", "qG", "loc"] + ["dm%d" % i for i in range(20)] + ["ar%d" % i for i in range(20)]
+CACHE = {}
+
+
+def program():
+    ops, acc, num = [], {}, {"d": 0, "a": 0}
+
+    def add(q, cost, rd, wr, emit, kind="c", dep=()):
+        deps, k = set(dep), len(ops)
+        for w, lst in ((0, rd), (1, wr)):
+            for b, lo, hi in lst:
+                for o, l, h, ow in acc.get(b, ()):
+                    if b in BANKS:
+                        if ops[o]["q"] != q or w or ow:
+                            deps.add(o)
+                    elif (w or ow) and l < hi and lo < h:
+                        deps.add(o)
+        for b, lo, hi in wr:
+            acc[b] = [e for e in acc.get(b, ()) if not (b in BANKS or (lo <= e[1] and e[2] <= hi))] + [(k, lo, hi, 1)]
+        for b, lo, hi in rd:
+            acc.setdefault(b, []).append((k, lo, hi, 0))
+        deps.discard(k)
+        sem = None
+        if kind in num:
+            sem = ("dm%d" if kind == "d" else "ar%d") % num[kind]
+            num[kind] += 1
+        ops.append({"q": q, "cost": cost, "deps": deps, "emit": emit, "kind": kind, "sem": sem})
+        return k
+
+    def vc(n, f=1.0):
+        return max(64.0, n * f) * CYC
+
+    def ln(a):
+        return -(-(a[2] - a[1]) // abs(a[3] if len(a) > 3 else 1))
+
+    def view(T, a):
+        if len(a) == 5:
+            return T[a[0]][0:a[4], a[1]:a[2]]
+        if len(a) == 4 and a[3] == -1:
+            return T[a[0]][:, a[2] - 1:(a[1] - 1 if a[1] else None):-1]
+        return T[a[0]][:, a[1]:a[2]:a[3]] if len(a) == 4 else T[a[0]][:, a[1]:a[2]]
+
+    def reg(*vs):
+        return [a[:3] for a in vs]
+
+    def ind(T, win, off):
+        return view(T, win).indirect(view(T, off))
+
+    def tt(out, a, b, op):
+        add("V", vc(ln(out), 1.0 if a[0] in BANKS or b[0] in BANKS else 2.0), reg(a, b), reg(out), lambda g, T, X: g.vector.tensor_tensor(view(T, out), view(T, a), view(T, b), op))
+
+    def gtt(out, win, off, b, op):
+        add("V", 50 + ln(out) * GATH * CYC, reg(win, off, b), reg(out), lambda g, T, X: g.vector.tensor_tensor(view(T, out), ind(T, win, off), view(T, b), op))
+
+    def ts(out, a, s1, o1, s2=None, o2=None, f=1.0):
+        def em(g, T, X):
+            x1 = T[s1][:, 0:1] if isinstance(s1, str) else s1
+            return g.vector.tensor_scalar(view(T, out), view(T, a), x1, s2, o1, o2) if o2 else g.vector.tensor_scalar(view(T, out), view(T, a), x1, None, o1)
+        add("V", vc(ln(out), f), reg(a) + ([(s1, 0, 1)] if isinstance(s1, str) else []), reg(out), em)
+
+    def cp(out, a):
+        add("V", vc(ln(out)), reg(a), reg(out), lambda g, T, X: g.vector.tensor_copy(view(T, out), view(T, a)))
+
+    def ms(out, c, f=1.0):
+        add("V", vc(ln(out), f), [], reg(out), lambda g, T, X: g.vector.memset(view(T, out), c))
+
+    def scan(out, d0, d1, o0, o1, f=1.0):
+        add("V", vc(ln(out), f), reg(d0, d1), reg(out), lambda g, T, X: g.vector.tensor_tensor_scan(view(T, out), view(T, d0), view(T, d1), 0.0, o0, o1))
+
+    def act(out, a, scale=1.0, bias=0.0):
+        add("S", 20 + vc(ln(out)), reg(a), reg(out), lambda g, T, X: g.scalar.activation(view(T, out), view(T, a), AF.Identity, bias=bias, scale=scale))
+
+    def gact(out, win, off):
+        add("S", 65 + ln(out) * GATH * CYC, reg(win, off), reg(out), lambda g, T, X: g.scalar.activation(view(T, out), ind(T, win, off), AF.Identity))
+
+    def mm(bank, terms):
+        def em(g, T, X):
+            for i, (o, lt, rh) in enumerate(terms):
+                last = g.tensor.matmul(view(T, o), view(T, lt), rh[1](T) if len(rh) == 2 else view(T, rh), i == 0, i == len(terms) - 1)
+            return last
+        rd = []
+        for o, lt, rh in terms:
+            rd += reg(lt) + (rh[0] if len(rh) == 2 else reg(rh))
+        add("P", sum(max(64, ln(o)) * CYC * (4 if lt[0] == "b8" else 1) for o, lt, _ in terms), rd, [(bank, 0, 512)], em)
+
+    def sel(out, src, pattern, cmp, base, cm, parts=128):
+        add("G", 170 + 256 * CYC, reg(src), reg(out), lambda g, T, X: g.affine_select(T[out[0]][0:parts, 0:128], T[src[0]][0:parts, 0:128], pattern, cmp, 0.0, base, cm))
+
+    def iota(out, pattern, base, cm, flag=False):
+        add("G", 130 + 2 * ln(out) * CYC, [], reg(out), lambda g, T, X: (g.iota(view(T, out), pattern, base, cm, allow_small_or_imprecise_dtypes=True)
+                                                                     if flag else g.iota(view(T, out), pattern, base, cm)))
+
+    def dma(q, nbytes, rd, wr, fn):
+        add(q, 2000.0 + nbytes / 180.0, rd, wr, lambda g, T, X: fn(g.sync if q == "D" else g.scalar, T), kind="d")
+
+    def load(q, name, buf, lo, hi, c0, parts=128, size=4):
+        dma(q, parts * (hi - lo) * size, [], [(buf, lo, hi)], lambda e, T: e.dma_start(T[buf][0:parts, lo:hi], T[name][:, c0:c0 + hi - lo]))
+
+    def store(q, name, c0, buf, lo, hi):
+        dma(q, 128 * (hi - lo) * 3, [(buf, lo, hi)], [], lambda e, T: e.dma_start(T[name][:, c0:c0 + hi - lo], T[buf][:, lo:hi]))
+
+    load("D", "tn", "tni", 0, 256, 0)
+    load("S", "lg", "lgi", 0, 256, 0)
+    load("D", "aa", "aai", 0, 256, 0, 8)
+    load("S", "bb", "bbi", 0, 256, 0, 8)
+    load("D", "xt", "xw", ROT, 4096, 0, size=2)
+    load("S", "xt", "xw", 0, ROT, 4096 - ROT, size=2)
+    load("D", "sp", "st0", 0, 256, 0, size=2)
+    load("S", "ep", "epb", 0, 256, 0, size=2)
+    load("D", "th", "pib", 0, 256, 0, 8)
+    load("S", "wt", "wti", 0, 1, 0)
+    load("D", "ct", "cti", 0, 1024, 0)
+    ms(("onef", 0, 128), 1.0)
+    one, blk, idf, b8 = ("onef", 0, 128), ("blk", 0, 128), ("idf", 0, 128), ("b8", 0, 128, 1, 8)
+    sel(("t1", 0, 128), one, [[-16, 8], [0, 16]], A.is_ge, 0, 1)
+    sel(blk, ("t1", 0, 128), [[16, 8], [0, 16]], A.is_ge, 15, -1)
+    sel(("upf", 0, 128), blk, [[1, 128]], A.is_ge, 0, -1)
+    sel(("t1", 0, 128), one, [[1, 128]], A.is_ge, 0, -16, 8)
+    sel(b8[:3], ("t1", 0, 128), [[-1, 128]], A.is_ge, 15, 16, 8)
+    sel(("t1", 0, 128), blk, [[-1, 128]], A.is_gt, 0, 1)
+    sel(idf, one, [[-1, 128]], A.is_equal, 0, 1)
+    iota(("p15", 0, 256), [[0, 256]], 0, 1)
+    iota(("ei", 0, 256), [[0, 16], [1, 16]], 0, 0)
+    iota(("us", 0, 256), [[256, 16], [0, 16]], 0, 0)
+    ms(("st0", 512, 1024), 1.0, 0.5)
+    ms(("l1", 0, 128, 1, 9), -255.0)
+    ms(("l2", 0, 128, 1, 9), 9.0)
+    ts(("ta", 0, 128), ("upf", 0, 128), 2.0, A.mult)
+    for n, k in (("l1", 2.0), ("l2", 2.0), ("ldb", 2.0), ("lda", -2.0)):
+        act((n, 0, 128, 1, 8), b8, scale=k)
+    ts(("tb", 0, 128), ("t1", 0, 128), -2.0, A.mult)
+    ts(("td", 0, 128), blk, -2.0, A.mult)
+    for n, k in (("ib", 1.0), ("inb", -1.0), ("hib", 0.5)):
+        act((n, 0, 128), idf, scale=k)
+    cp(("tb0", 0, 256), ("tni", 0, 256))
+    cp(("lb0", 0, 256), ("lgi", 0, 256))
+    cp(("st0", 512, 768, 1, 8), ("aai", 0, 256, 1, 8))
+    cp(("st0", 768, 1024, 1, 8), ("bbi", 0, 256, 1, 8))
+    ms(("mk", 0, 1024), 1.0, 0.5)
+    ms(("mk", 15, 1024, 16), 0.0)
+    ms(("dw", 0, 2048), 0.0, 0.5)
+    for r in range(16):
+        act(("dw", r * 128 + r, (r + 1) * 128, 16), ("blk", r, 128, 16), scale=4096.0)
+    tt(("st0", 256, 512), ("st0", 0, 256), ("epb", 0, 256), A.subtract)
+    snd = add("G", 150.0, [("st0", 0, 1024)], [], lambda g, T, X: X["stat"](), kind="s")
+    for d in range(1, 4):
+        add("R", REMOTE + 2000, [], [("st%d" % d, 0, 1024)], None, kind="a", dep=(snd,))
+    ms(("onb", 0, 256), 1.0, 0.5)
+    ts(("p15", 0, 256), ("p15", 0, 256), 15, A.bitwise_and)
+    ts(("kai", 0, 256), ("p15", 0, 256), 16.0, A.mult)
+    tt(("kai", 0, 256), ("kai", 0, 256), ("us", 0, 256), A.add)
+    cp(("ka", 0, 256), ("kai", 0, 256))
+    cp(("kb", 0, 256), ("ei", 0, 256))
+    tt(("diag", 0, 256), ("p15", 0, 256), ("ei", 0, 256), A.is_equal)
+    ms(("rst", 0, 256), -1e9)
+    ms(("rst", 0, 256, 16), 1e9)
+    ms(("mfw", 0, 256), 1.0)
+    ms(("mfw", 0, 256, 16), 0.0)
+    ms(("m128", 0, 256), -128.0, 0.5)
+    for i, (lo, hi) in enumerate(BATCHES):
+        ts(("rb", lo // 16, hi // 16), ("kai", lo, hi, 16), float(ROT - 160 * (i > 0)), A.add)
+    ts(("cb", 0, 16), ("kai", 0, 256, 16), 0.25, A.mult)
+    for nm, c in (("otab", 0), ("mtab", 0), ("ktab", 1)):
+        iota((nm, 0, 1040), [[0, 1040]], c, 0, True)
+    tt(("mtab", 0, 16), ("p15", 0, 16), ("ei", 0, 16), A.is_ge)
+    ts(("ktab", 0, 16), ("mtab", 0, 16), -1.0, A.mult, 1.0, A.add)
+    tt(("otab", 1024, 1040), ("p15", 0, 16), ("ei", 0, 16), A.is_equal)
+    ts(("otab", 1024, 1040), ("otab", 1024, 1040), 0.5, A.mult)
+    cp(("wf", 0, 1), ("wti", 0, 1))
+    ts(("uw", 0, 128), blk, "wf", A.mult, -1.0, A.mult)
+    ts(("ss", 0, 256, 1, 8), ("pib", 0, 256, 1, 8), 4096.0, A.mult, 4095.0, A.add)
+    mm("bu", [(("bu", 0, 256), b8, ("ss", 0, 256, 1, 8))])
+    tt(("ud", 0, 256), ("bu", 0, 256), ("diag", 0, 256), A.mult)
+    scan(("mg", 0, 256), ("mfw", 0, 256), ("ud", 0, 256), A.mult, A.add)
+    cp(("th2", 0, 16), ("mg", 15, 256, 16))
+    cp(("cw", 0, 1024), ("cti", 0, 1024))
+    I, NI, HI, xw = ("ib", 0, 128), ("inb", 0, 128), ("hib", 0, 128), ("xw", 0, 4096)
+    for v in range(NV):
+        L, Tn, st, Lo, Lk, To = "lb%d" % v, "tb%d" % v, "st%d" % (v % 4), "lo%d" % v, "lk%d" % v, "td%d" % v
+        for lo, hi in FR:
+            act(("m8", lo, hi), (L, lo, hi), scale=0.125, bias=18.5 + EPS)
+        for nb, (bank, tri, q, pi, off, c0) in enumerate((("ba", "ta", "qa", "pia", "fo", 512), ("bb_", "tb", "qb", "pib", "bo", 768))):
+            for lo, hi in FR:
+                o1, o2, qt = (bank, lo, hi), (bank, 256 + lo, 256 + hi), ("qt", lo + 256 * nb, hi + 256 * nb)
+
+                def base(o, l):
+                    return ([(o, (tri, 0, 128), (Tn, lo, hi)), (o, (l, 0, 128, 1, 9), (st, c0 + lo, c0 + hi, 1, 9))]
+                            + ([(o, ("la", 0, 128, 1, 1), ("onb", lo, hi, 1, 1))] if nb and v else []))
+                mm(bank, base(o1, "l1"))
+                act(qt, o1, bias=M2)
+                act((q, lo, hi), qt, bias=-M2)
+                mm(bank, base(o2, "l2") + [(o2, NI, (q, lo, hi))])
+                tt((pi, lo, hi), o2, ("m8", lo, hi), A.mult)
+                ts((pi, lo, hi), (pi, lo, hi), 4095, A.bitwise_and)
+                cp((off, lo, hi), (pi, lo, hi))
+        o = ("bd", 0, 256)
+        mm("bd", [(o, ("td", 0, 128), (Tn, 0, 256)), (o, ("lda", 0, 128, 1, 8), (st, 512, 768, 1, 8)), (o, ("ldb", 0, 128, 1, 8), (st, 768, 1024, 1, 8))]
+           + ([(o, ("la", 0, 128, 1, 1), ("onb", 0, 256, 1, 1))] if v else []) + [(o, NI, ("qb", 0, 256)), (o, I, ("qa", 0, 256))])
+        act(("d2", 0, 256), o)
+        for ic, (lo, hi) in enumerate(CHUNKS):
+            a, b, n = 16 * lo, 16 * hi, hi - lo
+            gact(("ff", a, b), xw, ("fo", lo, hi))
+            scan(("sf", a, b, -1), ("mk", 0, b - a, -1), ("ff", a, b, -1), A.mult, A.add, 0.5)
+            gtt(("nd", a, b), xw, ("bo", lo, hi), ("ff", a, b), A.subtract)
+            bj = "bj%d" % (ic & 1)
+            n15, n14, s15, s14, f1, f2 = ("nd", a + 15, b, 16), ("nd", a + 14, b, 16), ("s15", lo, hi), ("s14", lo, hi), (bj, 0, n), (bj, 256, 256 + n)
+            act(s15, n15)
+            act(s14, n14)
+            mm(bj, [(f1, I, (st, 256 + lo, 256 + hi)), (f1, I, ("sf", a, b, 16)), (f1, I, s15)])
+            act(n15, f1)
+            mm(bj, [(f2, I, (st, 256 + lo, 256 + hi)), (f2, I, ("sf", a, b, 16)), (f2, I, s15), (f2, I, s14), (f2, NI, n15)])
+            act(n14, f2)
+            scan(("vv", a, b, -1), ("mk", 0, b - a, -1), ("nd", a, b, -1), A.mult, A.add, 0.5)
+            act(n15, s15)
+            act(n14, s14)
+            c0, c1, r_ab = lo // 16, hi // 16, [("ab", a, b)]
+            add("S", 20 + vc(b - a), [("vv", a, b)], r_ab, lambda g, T, X, c0=c0, c1=c1, a=a, b=b: g.scalar.activation(T.ab[:, c0:c1], T.vv[:, a:b], AF.Abs))
+            add("V", vc(b - a, 0.5), r_ab, r_ab, lambda g, T, X, c0=c0, c1=c1: g.vector.tensor_scalar(T.ab[:, c0:c1], T.ab[:, c0:c1], 255.0, None, A.min))
+            ib = [i for i, (x, y) in enumerate(BATCHES) if x <= lo < y][0]
+            bk, d0 = "bk%d" % ib, lo - BATCHES[ib][0]
+            od = (bk, d0, d0 + n)
+
+            def dterm(r, c0=c0, c1=c1, r_ab=r_ab):
+                return (r_ab, lambda T: T.ab[:, c0:c1, r, :])
+            mm(bk, [(od, ("dw", r * 128, (r + 1) * 128), dterm(r)) for r in range(16)] + [(od, I, ("ka", d0, d0 + n)), (od, I, ("kb", d0, d0 + n))])
+        for ib, (lo, hi) in enumerate(BATCHES):
+            a, b, n, c0, c1 = 16 * lo, 16 * hi, hi - lo, lo // 16, hi // 16
+
+            def sm(nm):
+                return (nm, c0, c1)
+            os_ = ("bd", 256 + lo, 256 + hi)
+            mm("bd", [(os_, I, (st, lo, hi)), (os_, I, ("sf", a, b, 16))])
+            act(("ss", lo, hi), os_)
+            scan(("kint", lo, hi), ("rst", 0, n), ("bk%d" % ib, 0, n), A.max, A.min)
+            key, u = ("kint", lo + 15, hi, 16), ("us", lo + 15, hi, 16)
+            ts(sm("posi"), key, 4095, A.bitwise_and)
+            cp(sm("posu"), sm("posi"))
+            gtt(("np", lo, hi), ("sf", a, b), sm("posu"), ("ss", lo, hi), A.subtract)
+            ts(("mp", lo, hi), ("np", lo, hi), -255.0, A.max, f=0.5)
+            mm("bu", [(("bu", 0, n), ("uw", 0, 128), ("mp", lo, hi))])
+            tt(("ud", lo, hi), ("bu", 0, n), ("diag", lo, hi), A.mult)
+            scan(("us", lo, hi), ("mfw", 0, n), ("ud", lo, hi), A.mult, A.add)
+            ts(sm("r1"), u, 15, A.bitwise_and)
+            tt(sm("r1"), sm("r1"), sm("rb"), A.add)
+            if ib == 0:
+                ts(sm("r1"), sm("r1"), 4095, A.bitwise_and)
+            cp(sm("ru"), sm("r1"))
+            tt(sm("loc"), key, sm("th2"), A.is_le)
+            ts(sm("n1k"), sm("loc"), 1024.0, A.mult)
+            ts(sm("k15"), key, 15, A.bitwise_and)
+            tt(sm("cod"), sm("k15"), sm("n1k"), A.add)
+            cp(sm("codu"), sm("cod"))
+
+            def pair(dst, s1, s2):
+                k = add("G", 150.0, [(s1, lo, hi), (s2, lo, hi)], [], lambda g, T, X, lo=lo, hi=hi: X["send"](dst, (s1, s2), lo, hi, X["ar"]), kind="s")
+                add("R", REMOTE, [], [(dst, lo, hi)], None, kind="a", dep=(k,))
+            gtt((To, lo, hi), ("otab", 0, 1040), sm("codu"), ("d2", lo, hi), A.mult)
+            if v == NV - 1:
+                tt((To, lo, hi), (Tn, lo, hi), (To, lo, hi), A.add)
+            else:
+                pair("tb%d" % (v + 1), Tn, To)
+            gtt((Lk, lo, hi), ("ktab", 0, 1040), sm("codu"), (L, lo, hi), A.mult)
+            gact(("mg", lo, hi), ("mtab", 0, 1040), sm("codu"))
+            ts(sm("cg"), u, 1023, A.bitwise_and)
+            cp(sm("cgu"), sm("cg"))
+            gtt((Lo, lo, hi), ("cw", 0, 1024), sm("cgu"), ("mg", lo, hi), A.mult)
+            if v == NV - 1:
+                tt((Lk, lo, hi), (Lk, lo, hi), (Lo, lo, hi), A.add)
+            else:
+                pair("lb%d" % (v + 1), Lk, Lo)
+            gact(("fk", lo, hi), ("ff", a, b), sm("posu"))
+            gact(("ndk", lo, hi), ("nd", a, b), sm("posu"))
+            mm("bd", [(os_, I, ("fk", lo, hi)), (os_, HI, ("ndk", lo, hi))])
+            act(("rr", lo, hi), os_, bias=127.875)
+            wl, wh = (0, 4096) if ib == 0 else (a + 160, b + 176)
+            add("V", 50 + n * SCAT * CYC, reg(("rr", lo, hi), sm("ru"), ("m128", 0, n)), [("xw", wl, wh)],
+                lambda g, T, X, lo=lo, hi=hi, c0=c0, c1=c1, wl=wl, wh=wh: g.vector.tensor_tensor(T.xw[:, wl:wh].indirect(T.ru[:, c0:c1]), T.rr[:, lo:hi], T.m128[:, 0:hi - lo], A.add))
+        tt(("cbv", 0, 16), ("cb", 0, 16), ("n1k", 0, 16), A.add)
+        ts(("c3", 0, 16), ("us", 15, 256, 16), 3, A.bitwise_and)
+        tt(("c3", 0, 16), ("c3", 0, 16), ("cbv", 0, 16), A.add)
+        cp(("c3u", 0, 16), ("c3", 0, 16))
+        add("V", 50 + 256 * SCAT * CYC, [(L, 0, 256), ("c3u", 0, 16)], [("cw", 0, 2048)],
+            lambda g, T, X, L=L: g.vector.tensor_copy(T.cw[:, 0:2048].indirect(T.c3u[:, 0:16]), T[L][:, 0:256]))
+        if v < NV - 1:
+            mm("bu", [(("bu", 0, 16), ("onb", 0, 128), ("loc", 0, 16))])
+            scan(("cnt", 0, 16), ("onb", 0, 16), ("bu", 0, 16), A.mult, A.subtract)
+            ts(("c31", 0, 1), ("cnt", 15, 16), 31, A.bitwise_and)
+            cp(("acol", 0, 1), ("c31", 0, 1))
+            add("V", vc(128), [("acol", 0, 1), ("onb", 0, 128)], [("la", 0, 128)],
+                lambda g, T, X: g.vector.tensor_scalar(T.la[0:1, 0:128], T.onb[0:1, 0:128], T.acol[0:1, 0:1], 2.0, A.mult, A.mult))
+    cp(("pia", 0, 256), ("td4", 0, 256))
+    ts(("pia", 0, 256), ("pia", 0, 256), 255, A.bitwise_and)
+    cp(("mg", 0, 256), ("pia", 0, 256))
+    wl, wh = 16 * BATCHES[1][0] + 160, 16 * BATCHES[1][1] + 176
+    store("D", "yx", wh - ROT, "xw", wh, 4096)
+    store("S", "yx", 4096 - ROT, "xw", 0, wl)
+    store("S", "yt", 0, "mg", 0, 256)
+    store("D", "yx", 4096 - ROT + wl, "xw", wl, ROT)
+    store("D", "yx", 0, "xw", ROT, wh)
+    store("S", "yl", 0, "lk4", 0, 256)
+    store("D", "yc", 0, "cw", 0, 1024)
+    return ops
+
+
+def schedule():
+    ops = program()
+    n = len(ops)
+    pred, succ = [sorted(o["deps"]) for o in ops], [[] for _ in ops]
+    for i in range(n):
+        for d in pred[i]:
+            succ[d].append(i)
+
+    def lay(before, after, prio):
+        left, ready, free, start, end, pend = [len(p) for p in before], [0.0] * n, {}, [0.0] * n, [0.0] * n, {}
+        for i in range(n):
+            if not left[i]:
+                pend.setdefault(ops[i]["q"], []).append(i)
+        for _ in range(n):
+            best = None
+            for q, lst in pend.items():
+                if lst:
+                    t = max(free.get(q, 0.0), min(ready[i] for i in lst))
+                    if best is None or t < best[0]:
+                        best = (t, q, max((j for j in lst if ready[j] <= t), key=lambda j: (prio[j], -j)))
+            t, q, i = best
+            pend[q].remove(i)
+            start[i], end[i] = t, t + ops[i]["cost"]
+            if q != "R":
+                free[q] = t + 70.0 if ops[i]["kind"] == "d" else end[i]
+            for s in after[i]:
+                left[s] -= 1
+                ready[s] = max(ready[s], end[i] + (HOP if ops[s]["q"] != q else 10.0))
+                if not left[s]:
+                    pend.setdefault(ops[s]["q"], []).append(s)
+        return start, end
+
+    prio = [0.0] * n
+    for i in range(n - 1, -1, -1):
+        prio[i] = ops[i]["cost"] + max([prio[s] + (0 if ops[s]["q"] == ops[i]["q"] else HOP) for s in succ[i]] or [0.0])
+    start, end = keep = lay(pred, succ, prio)
+    for _ in range(ROUNDS):
+        start, end = lay(pred, succ, lay(succ, pred, end)[1])
+        if max(end) < max(keep[1]):
+            keep = (start, end)
+    start, end = keep
+    order = sorted(range(n), key=lambda i: (start[i], i))
+    count, fin, know, qk, waits = {}, [None] * n, [None] * n, {}, [[] for _ in ops]
+    for i in order:
+        o = ops[i]
+        if o["kind"] == "c":
+            s = "q" + o["q"]
+            count[s] = count.get(s, 0) + 1
+            fin[i] = (s, count[s])
+        elif o["kind"] in "da":
+            fin[i] = (o["sem"], 16)
+    for i in order:
+        o = ops[i]
+        q = o["q"]
+        if q == "R":
+            know[i] = dict([fin[i]])
+            continue
+        k, need = qk.setdefault(q, {}), {}
+        for d in sorted(o["deps"], key=lambda d: -end[d]):
+            s, x = fin[d]
+            if (q == "P" and ops[d]["q"] == "P") or k.get(s, 0) >= x:
+                continue
+            need[s] = max(need.get(s, 0), x)
+            for s2, x2 in know[d].items():
+                k[s2] = max(k.get(s2, 0), x2)
+        waits[i] = sorted(need.items())
+        know[i] = dict(k)
+        if fin[i]:
+            know[i][fin[i][0]] = max(know[i].get(fin[i][0], 0), fin[i][1])
+    return ops, order, waits, fin, count, start, end
+
+
+def rank_program(g, core, T, topo):
+    rank = T.rank_of(core)
+    if rank is None:
+        return
+    if "s" not in CACHE:
+        CACHE["s"] = schedule()
+    ops, order, waits, fin, count, start, end = CACHE["s"]
+    eng = {"V": g.vector, "S": g.scalar, "P": g.tensor, "G": g, "D": g.sync}
+    n, sent, X = len(T.cores), [0], {}
+    peers = [T.cores[(rank + d) % n] for d in range(n)]
+
+    def send(dst, src, lo, hi, sem):
+        rid, pid, _ = topo.addr(peers[1])
+        sent[0] += len(topo.engines(core, peers[1]))
+        g.remote_dma_fused([RemoteDMATransfer(dst_ids=[DstId(rid=rid, pnc=pid)], dma_engine_mask=topo.mask(core, peers[1]), remote_sem=T.sem[sem],
+                                              srcs=[T[b][:, lo:hi] for b in src], dsts=[T[dst][:, lo:hi]], alu_op=1)], local_sem=T.sem.loc)
+
+    def stat():
+        for d in range(1, n):
+            rid, pid, _ = topo.addr(peers[d])
+            sent[0] += len(topo.engines(core, peers[d]))
+            g.remote_dma(T["st%d" % d][:], T.st0[:], T.sem["ar%d" % (d - 1)], T.sem.loc, pid, rid, topo.mask(core, peers[d]))
+    X["send"], X["stat"] = send, stat
+    arr = {}
+    for o in ops:
+        if o["kind"] == "a":
+            for d in o["deps"]:
+                arr.setdefault(d, o["sem"])
+    for i in order:
+        o = ops[i]
+        if o["q"] == "R":
+            continue
+        for s, x in waits[i]:
+            eng[o["q"]].wait_ge(T.sem[s], x)
+        X["ar"] = arr.get(i)
+        h = o["emit"](g, T, X)
+        if fin[i]:
+            h.then_inc(T.sem[fin[i][0]], 1 if o["kind"] == "c" else 16)
+    for s in sorted(count):
+        g.wait_ge(T.sem[s], count[s])
+    for o in ops:
+        if o["sem"]:
+            g.wait_ge(T.sem[o["sem"]], 16)
+    g.wait_ge(T.sem.loc, sent[0])

@@ -1,38 +1,40 @@
+import numpy as np
 from concourse.bass import DstId, RemoteDMATransfer
 from concourse.mybir import AluOpType as A, ActivationFunctionType as AF
 
 NV = 5
-CHUNKS = [(192, 256), (128, 192), (64, 128), (0, 64)]
-BATCHES = [(128, 256), (0, 128)]
+CHUNKS = [(192, 256, "SV-"), (128, 192, "SH-"), (64, 128, "SV-"), (0, 64, "SS-")]
+BATCHES = [(128, 256, "Vd"), (0, 128, "Vd")]
 FR = [(192, 256), (128, 192), (0, 128)]
-ROT, EPS, M2 = 167, 2.0 ** -13, 1.5 * 2.0 ** 32
-CYC, GATH, SCAT, HOP, REMOTE = 1.0, 1.55, 3.5, 60.0, 2200.0
-ROUNDS = 5
-BANKS = ["ba", "bb_", "bd", "bu", "bk0", "bk1", "bj0", "bj1"]
+ROT, EPS, QB, SIGN = 167, 2.0 ** -13, 98304.0, 1 << 23
+CYC, PCYC, GATH, SCAT, HOP, SAME, REMOTE, RATE = 0.85, 0.43, 1.55, 3.5, 170.0, 170.0, 2200.0, 450.0
+FV, FS, MN = 45.0, 65.0, 24.0
+ROUNDS, JITTER, SHARE, SEED = 4000, 6000.0, 0.02, 0
+BANKS = ["ba", "bb_", "bn0", "bn1", "bk0", "bk1", "bm", "bu"]
 SIZES = {
-    "bfloat16": "xw 4096 ff 4096 nd 4096 sf 4096 vv 4096 mk 1024 dw 2048 ib 128 inb 128 hib 128 onb 256 uw 128 l1 128 l2 128 lda 128 ldb 128 la 128 ka 256 "
-                "kb 256 m128 256 epb 256 qa 256 qb 256 s15 256 s14 256 mp 256 fk 256 ndk 256 rr 256 loc 16 st0 1024 st1 1024 st2 1024 st3 1024",
-    "float32": "cw 2048 ktab 1040 mtab 1040 otab 1040 wf 1 th2 16 onef 128 t1 128 blk 128 idf 128 upf 128 b8 128 diag 256 rst 256 mfw 256 m8 256 "
-               "d2 256 ss 256 ud 256 mg 256 acol 1 qt 512 lb0 256 lb1 256 lb2 256 lb3 256 lb4 256 lo0 256 lo1 256 lo2 256 lo3 256 lo4 256 "
-               "lk0 256 lk1 256 lk2 256 lk3 256 lk4 256",
+    "bfloat16": "xw 4096 ff 4096 fb 4096 pe 4096 sb 4096 mk 1024 dw 144 uwr 144 uw 128 ib 128 inb 128 hib 128 onb 256 l1 128 l2 128 la 128 "
+                "m128 128 m255 128 epb 256 qa 256 qb 256 pk 256 mp 256 fk 256 bk 256 rr 256 d2 256 n1k 16 tab 64 st0 1024 st1 1024 st2 1024 st3 1024",
+    "float32": "cwo 6144 wf 1 p15f 1 onef 144 t1 128 blk 128 idf 128 upf 128 b8 128 b8r 144 thf 256 rst 128 m8 256 ss 256 dl 256 yt4 256 yl4 256 acol 1 "
+               "diag 128 mfw 128 ud 256 lb0 256 lb1 256 lb2 256 lb3 256 lb4 256 lo0 256 lo1 256 lo2 256 lo3 256 lo4 256",
     "float16": "ta 128 tb 128 td 128 np 256 tb0 256 tb1 256 tb2 256 tb3 256 tb4 256 td0 256 td1 256 td2 256 td3 256 td4 256",
-    "int32": "cti 1024 lgi 256 tni 256 aai 256 bbi 256 wti 1 p15 256 ei 256 kai 256 rb 16 cb 16 pia 256 pib 256 kint 256 posi 16 us 256 r1 16 "
-             "cg 16 c3 16 n1k 16 k15 16 cod 16 cbv 16 cnt 16 c31 1",
-    "uint16": "fo 256 bo 256 posu 16 ru 16 cgu 16 c3u 16 codu 16"}
+    "int32": "cw 2048 lgi 256 tni 256 aai 256 bbi 256 thi 256 wti 1 p15 16 ei 128 kai 16 posb 16 rb 16 cb 16 cb4 16 pia 256 pib 256 kint 256 posi 16 xk 16 "
+             "us 256 u15 16 li 32 c3 16 cbv 16 cnt 16 c31 1",
+    "uint16": "fo 256 bo 256 posu 16 ml 16 ol 16 lu 32 c3u 16"}
 SCRATCH = {n: ("psum", [128, 512], "float32") for n in BANKS}
 for _d in SIZES:
     _l = SIZES[_d].split()
     for _i in range(0, len(_l), 2):
         SCRATCH[_l[_i]] = ("sbuf", [128, int(_l[_i + 1])], _d)
 SCRATCH["ab"] = ("sbuf", [128, 16, 16, 16], "bfloat16")
-SEMAPHORES = ["qV", "qS", "qP", "qG", "loc"] + ["dm%d" % i for i in range(20)] + ["ar%d" % i for i in range(20)]
+SCRATCH["kf"] = ("sbuf", [128, 16, 16], "float32")
+SEMAPHORES = ["qV", "qS", "qP", "qG", "loc"] + ["dm%d" % i for i in range(30)] + ["ar%d" % i for i in range(30)]
 CACHE = {}
 
 
 def program():
-    ops, acc, num = [], {}, {"d": 0, "a": 0}
+    ops, acc, num, first = [], {}, {"d": 0, "a": 0}, []
 
-    def add(q, cost, rd, wr, emit, kind="c", dep=()):
+    def add(q, cost, rd, wr, emit, kind="c", dep=(), nb=0, tag=""):
         deps, k = set(dep), len(ops)
         for w, lst in ((0, rd), (1, wr)):
             for b, lo, hi in lst:
@@ -51,18 +53,22 @@ def program():
         if kind in num:
             sem = ("dm%d" if kind == "d" else "ar%d") % num[kind]
             num[kind] += 1
-        ops.append({"q": q, "cost": cost, "deps": deps, "emit": emit, "kind": kind, "sem": sem})
+        ops.append({"q": q, "cost": cost, "deps": deps, "emit": emit, "kind": kind, "sem": sem, "nb": nb, "tag": tag or (wr[0][0] if wr else ""),
+                    "cls": k - first[0] if first else -k - 1})
         return k
 
     def vc(n, f=1.0):
-        return max(64.0, n * f) * CYC
+        return FV + max(MN, n * f) * CYC
 
     def ln(a):
         return -(-(a[2] - a[1]) // abs(a[3] if len(a) > 3 else 1))
 
+    def fast(*vs):
+        return 0.5 if all(SCRATCH[a[0]][2] in ("bfloat16", "float16", "uint16") for a in vs) else 1.0
+
     def view(T, a):
         if len(a) == 5:
-            return T[a[0]][0:a[4], a[1]:a[2]]
+            return T[a[0]][0:a[4], a[1]:a[2]:a[3]]
         if len(a) == 4 and a[3] == -1:
             return T[a[0]][:, a[2] - 1:(a[1] - 1 if a[1] else None):-1]
         return T[a[0]][:, a[1]:a[2]:a[3]] if len(a) == 4 else T[a[0]][:, a[1]:a[2]]
@@ -79,52 +85,69 @@ def program():
     def gtt(out, win, off, b, op):
         add("V", 50 + ln(out) * GATH * CYC, reg(win, off, b), reg(out), lambda g, T, X: g.vector.tensor_tensor(view(T, out), ind(T, win, off), view(T, b), op))
 
-    def ts(out, a, s1, o1, s2=None, o2=None, f=1.0):
+    def ts(out, a, s1, o1, s2=None, o2=None):
         def em(g, T, X):
             x1 = T[s1][:, 0:1] if isinstance(s1, str) else s1
             return g.vector.tensor_scalar(view(T, out), view(T, a), x1, s2, o1, o2) if o2 else g.vector.tensor_scalar(view(T, out), view(T, a), x1, None, o1)
-        add("V", vc(ln(out), f), reg(a) + ([(s1, 0, 1)] if isinstance(s1, str) else []), reg(out), em)
+        add("V", vc(ln(out), fast(out, a)), reg(a) + ([(s1, 0, 1)] if isinstance(s1, str) else []), reg(out), em)
 
     def cp(out, a):
-        add("V", vc(ln(out)), reg(a), reg(out), lambda g, T, X: g.vector.tensor_copy(view(T, out), view(T, a)))
+        add("V", vc(ln(out), fast(out, a)), reg(a), reg(out), lambda g, T, X: g.vector.tensor_copy(view(T, out), view(T, a)))
 
-    def ms(out, c, f=1.0):
-        add("V", vc(ln(out), f), [], reg(out), lambda g, T, X: g.vector.memset(view(T, out), c))
+    def ms(out, c):
+        add("V", vc(ln(out), fast(out)), [], reg(out), lambda g, T, X: g.vector.memset(view(T, out), c))
 
-    def scan(out, d0, d1, o0, o1, f=1.0):
-        add("V", vc(ln(out), f), reg(d0, d1), reg(out), lambda g, T, X: g.vector.tensor_tensor_scan(view(T, out), view(T, d0), view(T, d1), 0.0, o0, o1))
+    def scan(out, d0, d1, o0, o1):
+        add("V", vc(ln(out), fast(out, d0, d1)), reg(d0, d1), reg(out), lambda g, T, X: g.vector.tensor_tensor_scan(view(T, out), view(T, d0), view(T, d1), 0.0, o0, o1))
 
-    def act(out, a, scale=1.0, bias=0.0):
-        add("S", 20 + vc(ln(out)), reg(a), reg(out), lambda g, T, X: g.scalar.activation(view(T, out), view(T, a), AF.Identity, bias=bias, scale=scale))
+    def act(out, a, scale=1.0, bias=0.0, fn=AF.Identity):
+        add("S", FS - FV + vc(ln(out)), reg(a), reg(out), lambda g, T, X: g.scalar.activation(view(T, out), view(T, a), fn, bias=bias, scale=scale))
 
-    def gact(out, win, off):
-        add("S", 65 + ln(out) * GATH * CYC, reg(win, off), reg(out), lambda g, T, X: g.scalar.activation(view(T, out), ind(T, win, off), AF.Identity))
+    def gather(q, out, win, off):
+        if q == "H":
+            for e, i in (("V", 0), ("S", 1)):
+                gather(e, (out[0], out[1] + ln(out) // 2 * i, out[1] + ln(out) // 2 * (i + 1)), win, (off[0], off[1] + ln(off) // 2 * i, off[1] + ln(off) // 2 * (i + 1)))
+        elif q == "S":
+            add("S", 65 + ln(out) * GATH * CYC, reg(win, off), reg(out), lambda g, T, X: g.scalar.activation(view(T, out), ind(T, win, off), AF.Identity))
+        else:
+            add("V", 50 + ln(out) * GATH * CYC, reg(win, off), reg(out), lambda g, T, X: g.vector.tensor_copy(view(T, out), ind(T, win, off)))
 
-    def mm(bank, terms):
+    def mm(bank, terms, opens=True, closes=True):
         def em(g, T, X):
             for i, (o, lt, rh) in enumerate(terms):
-                last = g.tensor.matmul(view(T, o), view(T, lt), rh[1](T) if len(rh) == 2 else view(T, rh), i == 0, i == len(terms) - 1)
+                last = g.tensor.matmul(view(T, o), view(T, lt), rh[1](T) if len(rh) == 2 else view(T, rh), opens and i == 0, closes and i == len(terms) - 1)
             return last
         rd = []
         for o, lt, rh in terms:
             rd += reg(lt) + (rh[0] if len(rh) == 2 else reg(rh))
-        add("P", sum(max(64, ln(o)) * CYC * (4 if lt[0] == "b8" else 1) for o, lt, _ in terms), rd, [(bank, 0, 512)], em)
+        add("P", sum(max(64, ln(o)) * PCYC * (4 if SCRATCH[lt[0]][2] == "float32" else 1) for o, lt, _ in terms), rd, [(bank, 0, 512)], em)
 
     def sel(out, src, pattern, cmp, base, cm, parts=128):
-        add("G", 170 + 256 * CYC, reg(src), reg(out), lambda g, T, X: g.affine_select(T[out[0]][0:parts, 0:128], T[src[0]][0:parts, 0:128], pattern, cmp, 0.0, base, cm))
+        add("G", 170 + 2 * ln(out) * CYC, reg(src), reg(out),
+            lambda g, T, X: g.affine_select(T[out[0]][0:parts, out[1]:out[2]], T[src[0]][0:parts, src[1]:src[2]], pattern, cmp, 0.0, base, cm))
 
-    def iota(out, pattern, base, cm, flag=False):
-        add("G", 130 + 2 * ln(out) * CYC, [], reg(out), lambda g, T, X: (g.iota(view(T, out), pattern, base, cm, allow_small_or_imprecise_dtypes=True)
-                                                                     if flag else g.iota(view(T, out), pattern, base, cm)))
+    def iota(out, pattern, base, cm):
+        add("G", 130 + 2 * ln(out) * CYC, [], reg(out), lambda g, T, X: g.iota(view(T, out), pattern, base, cm))
 
     def dma(q, nbytes, rd, wr, fn):
-        add(q, 2000.0 + nbytes / 180.0, rd, wr, lambda g, T, X: fn(g.sync if q == "D" else g.scalar, T), kind="d")
+        add(q, 2000.0, rd, wr, lambda g, T, X: fn(g.sync if q == "D" else g.scalar, T), kind="d", nb=nbytes)
 
     def load(q, name, buf, lo, hi, c0, parts=128, size=4):
         dma(q, parts * (hi - lo) * size, [], [(buf, lo, hi)], lambda e, T: e.dma_start(T[buf][0:parts, lo:hi], T[name][:, c0:c0 + hi - lo]))
 
-    def store(q, name, c0, buf, lo, hi):
-        dma(q, 128 * (hi - lo) * 3, [(buf, lo, hi)], [], lambda e, T: e.dma_start(T[name][:, c0:c0 + hi - lo], T[buf][:, lo:hi]))
+    def store(q, name, c0, buf, lo, hi, size=4):
+        dma(q, 128 * (hi - lo) * size, [(buf, lo, hi)], [], lambda e, T: e.dma_start(T[name][:, c0:c0 + hi - lo], T[buf][:, lo:hi]))
+
+    def put(hop, dst, srcs, size):
+        k = add("G", 150.0, reg(*srcs), [], lambda g, T, X: X["put"](hop, lambda U: view(U, dst), [view(T, s) for s in srcs]), kind="s", tag="put")
+        add("R", REMOTE, [], reg(dst), None, kind="a", dep=(k,), nb=128 * ln(dst) * size * len(srcs))
+
+    def scatter(win, off, rd, fn):
+        add("V", 50 + 16 * ln(off) * SCAT * CYC, reg(off, *rd), reg(win), lambda g, T, X: fn(g.vector, T, ind(T, win, off)), tag="scatter")
+
+    def window(ib):
+        lo, hi = BATCHES[ib][:2]
+        return (16 * lo + 160, 16 * hi + 176) if 16 * hi + 176 <= 4096 else (0, 4096)
 
     load("D", "tn", "tni", 0, 256, 0)
     load("S", "lg", "lgi", 0, 256, 0)
@@ -134,198 +157,208 @@ def program():
     load("S", "xt", "xw", 0, ROT, 4096 - ROT, size=2)
     load("D", "sp", "st0", 0, 256, 0, size=2)
     load("S", "ep", "epb", 0, 256, 0, size=2)
-    load("D", "th", "pib", 0, 256, 0, 8)
+    load("D", "th", "thi", 0, 256, 0, 8)
     load("S", "wt", "wti", 0, 1, 0)
-    load("D", "ct", "cti", 0, 1024, 0)
-    ms(("onef", 0, 128), 1.0)
+    load("D", "ct", "cw", 0, 1024, 0)
+    ms(("onef", 0, 144), 1.0)
     one, blk, idf, b8 = ("onef", 0, 128), ("blk", 0, 128), ("idf", 0, 128), ("b8", 0, 128, 1, 8)
     sel(("t1", 0, 128), one, [[-16, 8], [0, 16]], A.is_ge, 0, 1)
     sel(blk, ("t1", 0, 128), [[16, 8], [0, 16]], A.is_ge, 15, -1)
     sel(("upf", 0, 128), blk, [[1, 128]], A.is_ge, 0, -1)
     sel(("t1", 0, 128), one, [[1, 128]], A.is_ge, 0, -16, 8)
     sel(b8[:3], ("t1", 0, 128), [[-1, 128]], A.is_ge, 15, 16, 8)
-    sel(("t1", 0, 128), blk, [[-1, 128]], A.is_gt, 0, 1)
     sel(idf, one, [[-1, 128]], A.is_equal, 0, 1)
-    iota(("p15", 0, 256), [[0, 256]], 0, 1)
-    iota(("ei", 0, 256), [[0, 16], [1, 16]], 0, 0)
-    iota(("us", 0, 256), [[256, 16], [0, 16]], 0, 0)
-    ms(("st0", 512, 1024), 1.0, 0.5)
-    ms(("l1", 0, 128, 1, 9), -255.0)
+    sel(("t1", 0, 128), blk, [[-1, 128]], A.is_gt, 0, 1)
+    sel(("b8r", 0, 144), ("onef", 0, 144), [[1, 144]], A.is_equal, -15, -16, 8)
+    iota(("p15", 0, 16), [[0, 16]], 0, 1)
+    iota(("ei", 0, 128), [[0, 8], [1, 16]], 0, 0)
+    ms(("st0", 512, 1024), 1.0)
+    ms(("l2", 0, 128, 1, 10), QB)
     ms(("l2", 0, 128, 1, 9), 9.0)
     ts(("ta", 0, 128), ("upf", 0, 128), 2.0, A.mult)
-    for n, k in (("l1", 2.0), ("l2", 2.0), ("ldb", 2.0), ("lda", -2.0)):
-        act((n, 0, 128, 1, 8), b8, scale=k)
+    act(("l2", 0, 128, 1, 8), b8, scale=2.0)
+    act(("l1", 0, 128, 1, 8), b8, scale=-2.0)
     ts(("tb", 0, 128), ("t1", 0, 128), -2.0, A.mult)
     ts(("td", 0, 128), blk, -2.0, A.mult)
-    for n, k in (("ib", 1.0), ("inb", -1.0), ("hib", 0.5)):
+    for n, k in (("inb", -1.0), ("ib", 1.0), ("hib", 0.5)):
         act((n, 0, 128), idf, scale=k)
     cp(("tb0", 0, 256), ("tni", 0, 256))
     cp(("lb0", 0, 256), ("lgi", 0, 256))
     cp(("st0", 512, 768, 1, 8), ("aai", 0, 256, 1, 8))
     cp(("st0", 768, 1024, 1, 8), ("bbi", 0, 256, 1, 8))
-    ms(("mk", 0, 1024), 1.0, 0.5)
+    ms(("mk", 0, 1024), 1.0)
     ms(("mk", 15, 1024, 16), 0.0)
-    ms(("dw", 0, 2048), 0.0, 0.5)
-    for r in range(16):
-        act(("dw", r * 128 + r, (r + 1) * 128, 16), ("blk", r, 128, 16), scale=4096.0)
+    ms(("pe", 0, 4096, 256), 0.0)
+    ms(("dw", 0, 144), 0.0)
+    ms(("uwr", 0, 144), 0.0)
+    act(("dw", 15, 143, 16), ("blk", 0, 128, 16), scale=2048.0)
     tt(("st0", 256, 512), ("st0", 0, 256), ("epb", 0, 256), A.subtract)
-    snd = add("G", 150.0, [("st0", 0, 1024)], [], lambda g, T, X: X["stat"](), kind="s")
     for d in range(1, 4):
-        add("R", REMOTE + 2000, [], [("st%d" % d, 0, 1024)], None, kind="a", dep=(snd,))
-    ms(("onb", 0, 256), 1.0, 0.5)
-    ts(("p15", 0, 256), ("p15", 0, 256), 15, A.bitwise_and)
-    ts(("kai", 0, 256), ("p15", 0, 256), 16.0, A.mult)
-    tt(("kai", 0, 256), ("kai", 0, 256), ("us", 0, 256), A.add)
-    cp(("ka", 0, 256), ("kai", 0, 256))
-    cp(("kb", 0, 256), ("ei", 0, 256))
-    tt(("diag", 0, 256), ("p15", 0, 256), ("ei", 0, 256), A.is_equal)
-    ms(("rst", 0, 256), -1e9)
-    ms(("rst", 0, 256, 16), 1e9)
-    ms(("mfw", 0, 256), 1.0)
-    ms(("mfw", 0, 256, 16), 0.0)
-    ms(("m128", 0, 256), -128.0, 0.5)
-    for i, (lo, hi) in enumerate(BATCHES):
-        ts(("rb", lo // 16, hi // 16), ("kai", lo, hi, 16), float(ROT - 160 * (i > 0)), A.add)
-    ts(("cb", 0, 16), ("kai", 0, 256, 16), 0.25, A.mult)
-    for nm, c in (("otab", 0), ("mtab", 0), ("ktab", 1)):
-        iota((nm, 0, 1040), [[0, 1040]], c, 0, True)
-    tt(("mtab", 0, 16), ("p15", 0, 16), ("ei", 0, 16), A.is_ge)
-    ts(("ktab", 0, 16), ("mtab", 0, 16), -1.0, A.mult, 1.0, A.add)
-    tt(("otab", 1024, 1040), ("p15", 0, 16), ("ei", 0, 16), A.is_equal)
-    ts(("otab", 1024, 1040), ("otab", 1024, 1040), 0.5, A.mult)
+        put(d, ("st%d" % d, 0, 1024), [("st0", 0, 1024)], 2)
+    ms(("onb", 0, 256), 1.0)
+    ms(("m128", 0, 128), -128.0)
+    ms(("m255", 0, 128), -255.0)
+    ms(("mfw", 0, 128), 1.0)
+    ms(("mfw", 0, 128, 16), 0.0)
+    ms(("rst", 0, 128), -1e9)
+    ms(("rst", 0, 128, 16), 1e9)
+    ms(("tab", 0, 64), 0.0)
+    ts(("p15", 0, 16), ("p15", 0, 16), 15, A.bitwise_and)
+    cp(("p15f", 0, 1), ("p15", 0, 1))
+    ts(("diag", 0, 128), ("ei", 0, 128), "p15f", A.is_equal)
+    ts(("kai", 0, 16), ("ei", 0, 16), 16.0, A.mult)
+    tt(("kai", 0, 16), ("kai", 0, 16), ("p15", 0, 16), A.add)
+    ts(("cb", 0, 16), ("kai", 0, 16), 4.0, A.mult)
+    for ib, (lo, hi, _) in enumerate(BATCHES):
+        c = ("kai", lo // 16, hi // 16)
+        ts(("rb",) + c[1:], c, 16.0, A.mult, float(ROT - window(ib)[0]), A.add)
+        ts(("posb",) + c[1:], c, 16.0, A.mult, float(-16 * lo), A.add)
+        ts(("cb4",) + c[1:], c, 4.0, A.mult, float(-4 * lo), A.add)
+    tt(("tab", 0, 16), ("p15", 0, 16), ("ei", 0, 16), A.is_ge)
+    tt(("tab", 33, 49), ("p15", 0, 16), ("ei", 0, 16), A.is_equal)
+    ts(("tab", 33, 49), ("tab", 33, 49), 0.5, A.mult)
     cp(("wf", 0, 1), ("wti", 0, 1))
     ts(("uw", 0, 128), blk, "wf", A.mult, -1.0, A.mult)
-    ts(("ss", 0, 256, 1, 8), ("pib", 0, 256, 1, 8), 4096.0, A.mult, 4095.0, A.add)
-    mm("bu", [(("bu", 0, 256), b8, ("ss", 0, 256, 1, 8))])
-    tt(("ud", 0, 256), ("bu", 0, 256), ("diag", 0, 256), A.mult)
-    scan(("mg", 0, 256), ("mfw", 0, 256), ("ud", 0, 256), A.mult, A.add)
-    cp(("th2", 0, 16), ("mg", 15, 256, 16))
-    cp(("cw", 0, 1024), ("cti", 0, 1024))
+    cp(("uwr", 15, 143, 16), ("uw", 0, 128, 16))
+    ts(("thf", 0, 256, 1, 8), ("thi", 0, 256, 1, 8), -2048.0, A.mult, -2048.0, A.add)
+    mm("bu", [(("bu", 0, 16), ("b8r", 15 - r, 143 - r, 1, 8), ("thf", r, 256, 16, 8)) for r in range(16)])
+    add("V", vc(16), [("bu", 0, 16), ("posb", 0, 16)], [("kf", 0, 256)], lambda g, T, X: g.vector.tensor_tensor(T.kf[:, :, 0], T.bu[:, 0:16], T.posb[:, 0:16], A.add))
+    for s in (1, 2, 4, 8):
+        add("V", vc(16 * s), [("kf", 0, 256)], [("kf", 0, 256)], lambda g, T, X, s=s: g.vector.tensor_scalar(T.kf[:, :, s:2 * s], T.kf[:, :, 0:s], float(s), None, A.add))
     I, NI, HI, xw = ("ib", 0, 128), ("inb", 0, 128), ("hib", 0, 128), ("xw", 0, 4096)
+    nd = [0]
     for v in range(NV):
-        L, Tn, st, Lo, Lk, To = "lb%d" % v, "tb%d" % v, "st%d" % (v % 4), "lo%d" % v, "lk%d" % v, "td%d" % v
+        L, Tn, st, Lo, To = "lb%d" % v, "tb%d" % v, "st%d" % (v % 4), "lo%d" % v, "td%d" % v
+        last = v == NV - 1
+        first[:] = [len(ops) - 1000 * last]
+        if last:
+            for ib, (lo, hi, _) in enumerate(BATCHES):
+                cp(("cwo", 1536 * ib, 1536 * ib + 4 * (hi - lo)), ("cw", 4 * lo, 4 * hi))
         for lo, hi in FR:
             act(("m8", lo, hi), (L, lo, hi), scale=0.125, bias=18.5 + EPS)
-        for nb, (bank, tri, q, pi, off, c0) in enumerate((("ba", "ta", "qa", "pia", "fo", 512), ("bb_", "tb", "qb", "pib", "bo", 768))):
-            for lo, hi in FR:
-                o1, o2, qt = (bank, lo, hi), (bank, 256 + lo, 256 + hi), ("qt", lo + 256 * nb, hi + 256 * nb)
-
-                def base(o, l):
-                    return ([(o, (tri, 0, 128), (Tn, lo, hi)), (o, (l, 0, 128, 1, 9), (st, c0 + lo, c0 + hi, 1, 9))]
-                            + ([(o, ("la", 0, 128, 1, 1), ("onb", lo, hi, 1, 1))] if nb and v else []))
-                mm(bank, base(o1, "l1"))
-                act(qt, o1, bias=M2)
-                act((q, lo, hi), qt, bias=-M2)
-                mm(bank, base(o2, "l2") + [(o2, NI, (q, lo, hi))])
-                tt((pi, lo, hi), o2, ("m8", lo, hi), A.mult)
+            for nb, (bank, tri, q, pi, off, c0) in enumerate((("ba", "ta", "qa", "pia", "fo", 512), ("bb_", "tb", "qb", "pib", "bo", 768))):
+                o = (bank, lo, hi)
+                base = ([(o, (tri, 0, 128), (Tn, lo, hi)), (o, ("l2", 0, 128, 1, 10), (st, c0 + lo, c0 + hi, 1, 10))]
+                        + ([(o, ("la", 0, 128, 1, 1), ("onb", lo, hi, 1, 1))] if nb and v else []))
+                mm(bank, base)
+                act((q, lo, hi), o, bias=-264.0)
+                mm(bank, base + [(o, NI, (q, lo, hi))])
+                tt((pi, lo, hi), o, ("m8", lo, hi), A.mult)
                 ts((pi, lo, hi), (pi, lo, hi), 4095, A.bitwise_and)
                 cp((off, lo, hi), (pi, lo, hi))
-        o = ("bd", 0, 256)
-        mm("bd", [(o, ("td", 0, 128), (Tn, 0, 256)), (o, ("lda", 0, 128, 1, 8), (st, 512, 768, 1, 8)), (o, ("ldb", 0, 128, 1, 8), (st, 768, 1024, 1, 8))]
-           + ([(o, ("la", 0, 128, 1, 1), ("onb", 0, 256, 1, 1))] if v else []) + [(o, NI, ("qb", 0, 256)), (o, I, ("qa", 0, 256))])
-        act(("d2", 0, 256), o)
-        for ic, (lo, hi) in enumerate(CHUNKS):
-            a, b, n = 16 * lo, 16 * hi, hi - lo
-            gact(("ff", a, b), xw, ("fo", lo, hi))
-            scan(("sf", a, b, -1), ("mk", 0, b - a, -1), ("ff", a, b, -1), A.mult, A.add, 0.5)
-            gtt(("nd", a, b), xw, ("bo", lo, hi), ("ff", a, b), A.subtract)
-            bj = "bj%d" % (ic & 1)
-            n15, n14, s15, s14, f1, f2 = ("nd", a + 15, b, 16), ("nd", a + 14, b, 16), ("s15", lo, hi), ("s14", lo, hi), (bj, 0, n), (bj, 256, 256 + n)
-            act(s15, n15)
-            act(s14, n14)
-            mm(bj, [(f1, I, (st, 256 + lo, 256 + hi)), (f1, I, ("sf", a, b, 16)), (f1, I, s15)])
-            act(n15, f1)
-            mm(bj, [(f2, I, (st, 256 + lo, 256 + hi)), (f2, I, ("sf", a, b, 16)), (f2, I, s15), (f2, I, s14), (f2, NI, n15)])
-            act(n14, f2)
-            scan(("vv", a, b, -1), ("mk", 0, b - a, -1), ("nd", a, b, -1), A.mult, A.add, 0.5)
-            act(n15, s15)
-            act(n14, s14)
-            c0, c1, r_ab = lo // 16, hi // 16, [("ab", a, b)]
-            add("S", 20 + vc(b - a), [("vv", a, b)], r_ab, lambda g, T, X, c0=c0, c1=c1, a=a, b=b: g.scalar.activation(T.ab[:, c0:c1], T.vv[:, a:b], AF.Abs))
-            add("V", vc(b - a, 0.5), r_ab, r_ab, lambda g, T, X, c0=c0, c1=c1: g.vector.tensor_scalar(T.ab[:, c0:c1], T.ab[:, c0:c1], 255.0, None, A.min))
-            ib = [i for i, (x, y) in enumerate(BATCHES) if x <= lo < y][0]
-            bk, d0 = "bk%d" % ib, lo - BATCHES[ib][0]
-            od = (bk, d0, d0 + n)
-
-            def dterm(r, c0=c0, c1=c1, r_ab=r_ab):
-                return (r_ab, lambda T: T.ab[:, c0:c1, r, :])
-            mm(bk, [(od, ("dw", r * 128, (r + 1) * 128), dterm(r)) for r in range(16)] + [(od, I, ("ka", d0, d0 + n)), (od, I, ("kb", d0, d0 + n))])
-        for ib, (lo, hi) in enumerate(BATCHES):
+        for ib, (lo, hi, pq) in enumerate(BATCHES):
+            bk = "bk%d" % (ib & 1)
+            o = ("bm", 256 + lo, 256 + hi)
+            mm("bm", [(o, ("td", 0, 128), (Tn, lo, hi)), (o, ("l1", 0, 128, 1, 8), (st, 512 + lo, 512 + hi, 1, 8)), (o, ("l2", 0, 128, 1, 8), (st, 768 + lo, 768 + hi, 1, 8))]
+               + ([(o, ("la", 0, 128, 1, 1), ("onb", lo, hi, 1, 1))] if v else []) + [(o, NI, ("qb", lo, hi)), (o, I, ("qa", lo, hi))])
+            act(("d2", lo, hi), o)
+            for cl, ch, who in CHUNKS:
+                if not lo <= cl < hi:
+                    continue
+                a, b, n, c0, c1 = 16 * cl, 16 * ch, ch - cl, cl // 16, ch // 16
+                gather(who[0], ("ff", a, b), xw, ("fo", cl, ch))
+                scan(("pe", a + 1, b), ("ff", a, b - 1), ("mk", 0, b - a - 1), A.add, A.mult)
+                gather(who[1], ("fb", a, b), xw, ("bo", cl, ch))
+                b15, o1, o2 = ("fb", a + 15, b, 16), ("ba", 256, 256 + n), ("ba", 384, 384 + n)
+                if who[2] == "a":
+                    mm("ba", [(o1, I, b15), (o1, I, (st, 256 + cl, 256 + ch))])
+                    mm("ba", [(o2, I, b15)])
+                    act(b15, o1)
+                scan(("sb", a, b, -1), ("mk", 0, b - a, -1), ("fb", a, b, -1), A.mult, A.add)
+                if who[2] == "a":
+                    act(b15, o2)
+                for h in (0, 1):
+                    bn = "bn%d" % h
+                    o = (bn, 0, 8 * n)
+                    mm(bn, [(o, I, ("pe", a + h, b, 2))] + [((bn, m, 8 * n, 8), I, (st, 256 + cl, 256 + ch)) for m in range(8) if who[2] != "a"], closes=False)
+                    mm(bn, [(o, I, ("sb", a + h, b, 2))], opens=False)
+                    add("S", FS - FV + vc(8 * n), [o], [("ab", a, b)], lambda g, T, X, c0=c0, c1=c1, h=h, o=o: g.scalar.activation(T.ab[:, c0:c1, :, h:16:2], view(T, o), AF.Abs))
+                add("V", vc(b - a, 0.5), [("ab", a, b)], [("ab", a, b)], lambda g, T, X, c0=c0, c1=c1: g.vector.tensor_scalar(T.ab[:, c0:c1], T.ab[:, c0:c1], 255.0, None, A.min))
+                od = (bk, cl - lo, ch - lo)
+                mm(bk, [(od, idf, ([("kf", cl, ch)], lambda T, c0=c0, c1=c1: T.kf[:, c0:c1]))], closes=False)
+                mm(bk, [(od, ("dw", 15 - r, 143 - r), ([("ab", a, b)], lambda T, r=r, c0=c0, c1=c1: T.ab[:, c0:c1, r, :])) for r in range(16)], opens=False)
             a, b, n, c0, c1 = 16 * lo, 16 * hi, hi - lo, lo // 16, hi // 16
 
             def sm(nm):
                 return (nm, c0, c1)
-            os_ = ("bd", 256 + lo, 256 + hi)
-            mm("bd", [(os_, I, (st, lo, hi)), (os_, I, ("sf", a, b, 16))])
-            act(("ss", lo, hi), os_)
-            scan(("kint", lo, hi), ("rst", 0, n), ("bk%d" % ib, 0, n), A.max, A.min)
-            key, u = ("kint", lo + 15, hi, 16), ("us", lo + 15, hi, 16)
-            ts(sm("posi"), key, 4095, A.bitwise_and)
+            os_, ou = ("bm", lo, hi), ("bu", c0, c1)
+            scan(("kint", lo, hi), ("rst", 0, n), (bk, 0, n), A.max, A.min)
+            key = ("kint", lo + 15, hi, 16)
+            ts(sm("posi"), key, 2047, A.bitwise_and)
             cp(sm("posu"), sm("posi"))
-            gtt(("np", lo, hi), ("sf", a, b), sm("posu"), ("ss", lo, hi), A.subtract)
-            ts(("mp", lo, hi), ("np", lo, hi), -255.0, A.max, f=0.5)
-            mm("bu", [(("bu", 0, n), ("uw", 0, 128), ("mp", lo, hi))])
-            tt(("ud", lo, hi), ("bu", 0, n), ("diag", lo, hi), A.mult)
-            scan(("us", lo, hi), ("mfw", 0, n), ("ud", lo, hi), A.mult, A.add)
-            ts(sm("r1"), u, 15, A.bitwise_and)
-            tt(sm("r1"), sm("r1"), sm("rb"), A.add)
-            if ib == 0:
-                ts(sm("r1"), sm("r1"), 4095, A.bitwise_and)
-            cp(sm("ru"), sm("r1"))
-            tt(sm("loc"), key, sm("th2"), A.is_le)
-            ts(sm("n1k"), sm("loc"), 1024.0, A.mult)
-            ts(sm("k15"), key, 15, A.bitwise_and)
-            tt(sm("cod"), sm("k15"), sm("n1k"), A.add)
-            cp(sm("codu"), sm("cod"))
-
-            def pair(dst, s1, s2):
-                k = add("G", 150.0, [(s1, lo, hi), (s2, lo, hi)], [], lambda g, T, X, lo=lo, hi=hi: X["send"](dst, (s1, s2), lo, hi, X["ar"]), kind="s")
-                add("R", REMOTE, [], [(dst, lo, hi)], None, kind="a", dep=(k,))
-            gtt((To, lo, hi), ("otab", 0, 1040), sm("codu"), ("d2", lo, hi), A.mult)
-            if v == NV - 1:
-                tt((To, lo, hi), (Tn, lo, hi), (To, lo, hi), A.add)
+            if pq[0] == "S":
+                gather("S", ("pk", lo, hi), ("pe", a, b), sm("posu"))
+                mm("bm", [(os_, I, (st, lo, hi)), (os_, I, ("pk", lo, hi))])
+                act(("mp", lo, hi), os_, scale=-1.0, bias=255.0, fn=AF.Relu)
             else:
-                pair("tb%d" % (v + 1), Tn, To)
-            gtt((Lk, lo, hi), ("ktab", 0, 1040), sm("codu"), (L, lo, hi), A.mult)
-            gact(("mg", lo, hi), ("mtab", 0, 1040), sm("codu"))
-            ts(sm("cg"), u, 1023, A.bitwise_and)
-            cp(sm("cgu"), sm("cg"))
-            gtt((Lo, lo, hi), ("cw", 0, 1024), sm("cgu"), ("mg", lo, hi), A.mult)
-            if v == NV - 1:
-                tt((Lk, lo, hi), (Lk, lo, hi), (Lo, lo, hi), A.add)
+                gtt(("pk", lo, hi), ("pe", a, b), sm("posu"), (st, lo, hi), A.add)
+                ts(("mp", lo, hi), ("pk", lo, hi), 255.0, A.min, -1.0, A.mult)
+            u = ("us", lo + 15, hi, 16)
+            if pq[1] == "r":
+                mm("bu", ([(ou, ("uw", 0, 128), ("m255", 0, c1 - c0))] if pq[0] == "S" else [])
+                   + [(ou, ("uwr", 15 - r, 143 - r), ("mp", lo + r, hi, 16)) for r in range(16)])
+                cp(u, ou)
             else:
-                pair("lb%d" % (v + 1), Lk, Lo)
-            gact(("fk", lo, hi), ("ff", a, b), sm("posu"))
-            gact(("ndk", lo, hi), ("nd", a, b), sm("posu"))
-            mm("bd", [(os_, I, ("fk", lo, hi)), (os_, HI, ("ndk", lo, hi))])
+                ou = ("bu", 0, n)
+                mm("bu", ([(ou, ("uw", 0, 128), ("m255", 0, n))] if pq[0] == "S" else []) + [(ou, ("uw", 0, 128), ("mp", lo, hi))])
+                tt(("ud", lo, hi), ou, ("diag", 0, n), A.mult)
+                scan(("us", lo, hi), ("mfw", 0, n), ("ud", lo, hi), A.mult, A.add)
+            cg, r1, both = ("li", 2 * c0, c0 + c1), ("li", c0 + c1, 2 * c1), (2 * c0, 2 * c1)
+            ts(cg, u, 1023, A.bitwise_and)
+            ts(sm("u15"), u, 15, A.bitwise_and)
+            tt(r1, sm("u15"), sm("rb"), A.add)
+            if window(ib)[1] == 4096:
+                ts(r1, r1, 4095, A.bitwise_and)
+            cp(("lu",) + both, ("li",) + both)
+            ts(sm("xk"), key, SIGN | 15, A.bitwise_and)
+            ts(sm("ol"), sm("xk"), float(1 - SIGN), A.add, 0.0, A.max)
+            ts(sm("ml"), sm("xk"), 16.0, A.min)
+            gtt((To, lo, hi), ("tab", 32, 64), sm("ol"), ("d2", lo, hi), A.mult)
+            if last:
+                tt(("pia", lo, hi), (Tn, lo, hi), (To, lo, hi), A.add)
+                ts(("pia", lo, hi), ("pia", lo, hi), 255, A.bitwise_and)
+                cp(("yt4", lo, hi), ("pia", lo, hi))
+                store("S", "yt", lo, "yt4", lo, hi)
+            else:
+                put(1, ("tb%d" % (v + 1), lo, hi), [(Tn, lo, hi), (To, lo, hi)], 2)
+            gtt(("dl", lo, hi), ("cw", 0, 1024), ("lu",) + cg[1:], (L, lo, hi), A.subtract)
+            gtt((Lo, lo, hi), ("tab", 0, 32), sm("ml"), ("dl", lo, hi), A.mult)
+            if last:
+                tt(("yl4", lo, hi), (L, lo, hi), (Lo, lo, hi), A.add)
+                store("D", "yl", lo, "yl4", lo, hi)
+            else:
+                put(1, ("lb%d" % (v + 1), lo, hi), [(L, lo, hi), (Lo, lo, hi)], 4)
+            gather("S", ("fk", lo, hi), ("ff", a, b), sm("posu"))
+            gather("S", ("bk", lo, hi), ("fb", a, b), sm("posu"))
+            mm("bm", [(os_, HI, ("fk", lo, hi)), (os_, HI, ("bk", lo, hi))])
             act(("rr", lo, hi), os_, bias=127.875)
-            wl, wh = (0, 4096) if ib == 0 else (a + 160, b + 176)
-            add("V", 50 + n * SCAT * CYC, reg(("rr", lo, hi), sm("ru"), ("m128", 0, n)), [("xw", wl, wh)],
-                lambda g, T, X, lo=lo, hi=hi, c0=c0, c1=c1, wl=wl, wh=wh: g.vector.tensor_tensor(T.xw[:, wl:wh].indirect(T.ru[:, c0:c1]), T.rr[:, lo:hi], T.m128[:, 0:hi - lo], A.add))
-        tt(("cbv", 0, 16), ("cb", 0, 16), ("n1k", 0, 16), A.add)
-        ts(("c3", 0, 16), ("us", 15, 256, 16), 3, A.bitwise_and)
-        tt(("c3", 0, 16), ("c3", 0, 16), ("cbv", 0, 16), A.add)
-        cp(("c3u", 0, 16), ("c3", 0, 16))
-        add("V", 50 + 256 * SCAT * CYC, [(L, 0, 256), ("c3u", 0, 16)], [("cw", 0, 2048)],
-            lambda g, T, X, L=L: g.vector.tensor_copy(T.cw[:, 0:2048].indirect(T.c3u[:, 0:16]), T[L][:, 0:256]))
-        if v < NV - 1:
-            mm("bu", [(("bu", 0, 16), ("onb", 0, 128), ("loc", 0, 16))])
+        for ib, (lo, hi, pq) in enumerate(BATCHES):
+            c0, c1 = lo // 16, hi // 16
+            scatter(("xw",) + window(ib), ("lu", c0 + c1, 2 * c1), [("rr", lo, hi), ("m128", 0, hi - lo)],
+                    lambda e, T, w, lo=lo, hi=hi: e.tensor_tensor(w, T.rr[:, lo:hi], T.m128[:, 0:hi - lo], A.add))
+        for ib, (lo, hi) in enumerate([b[:2] for b in BATCHES] if last else [(0, 256)]):
+            c0, c1 = lo // 16, hi // 16
+            ts(("n1k", c0, c1), ("kint", lo + 15, hi, 16), 0.0, A.is_lt, 1024.0, A.mult)
+            tt(("cbv", c0, c1), ("cb4" if last else "cb", c0, c1), ("n1k", c0, c1), A.add)
+            ts(("c3", c0, c1), ("us", lo + 15, hi, 16), 3, A.bitwise_and)
+            tt(("c3", c0, c1), ("c3", c0, c1), ("cbv", c0, c1), A.add)
+            cp(("c3u", c0, c1), ("c3", c0, c1))
+            scatter(("cwo", 1536 * ib, 1536 * ib + 1536) if last else ("cw", 0, 2048), ("c3u", c0, c1), [(L, lo, hi)],
+                    lambda e, T, w, L=L, lo=lo, hi=hi: e.tensor_copy(w, T[L][:, lo:hi]))
+            if last:
+                store("DS"[ib & 1], "yc", 4 * lo, "cwo", 1536 * ib, 1536 * ib + 4 * (hi - lo))
+        if not last:
+            mm("bu", [(("bu", 0, 16), ("onb", 0, 128), ("n1k", 0, 16))])
             scan(("cnt", 0, 16), ("onb", 0, 16), ("bu", 0, 16), A.mult, A.subtract)
-            ts(("c31", 0, 1), ("cnt", 15, 16), 31, A.bitwise_and)
+            ts(("c31", 0, 1), ("cnt", 15, 16), 10, A.arith_shift_right, 31, A.bitwise_and)
             cp(("acol", 0, 1), ("c31", 0, 1))
-            add("V", vc(128), [("acol", 0, 1), ("onb", 0, 128)], [("la", 0, 128)],
+            add("V", vc(64), [("acol", 0, 1), ("onb", 0, 128)], [("la", 0, 128)],
                 lambda g, T, X: g.vector.tensor_scalar(T.la[0:1, 0:128], T.onb[0:1, 0:128], T.acol[0:1, 0:1], 2.0, A.mult, A.mult))
-    cp(("pia", 0, 256), ("td4", 0, 256))
-    ts(("pia", 0, 256), ("pia", 0, 256), 255, A.bitwise_and)
-    cp(("mg", 0, 256), ("pia", 0, 256))
-    wl, wh = 16 * BATCHES[1][0] + 160, 16 * BATCHES[1][1] + 176
-    store("D", "yx", wh - ROT, "xw", wh, 4096)
-    store("S", "yx", 4096 - ROT, "xw", 0, wl)
-    store("S", "yt", 0, "mg", 0, 256)
-    store("D", "yx", 4096 - ROT + wl, "xw", wl, ROT)
-    store("D", "yx", 0, "xw", ROT, wh)
-    store("S", "yl", 0, "lk4", 0, 256)
-    store("D", "yc", 0, "cw", 0, 1024)
+    wl, wh = window(len(BATCHES) - 1)
+    store("D", "yx", wh - ROT, "xw", wh, 4096, 2)
+    store("S", "yx", 4096 - ROT, "xw", 0, wl, 2)
+    store("S", "yx", 4096 - ROT + wl, "xw", wl, ROT, 2)
+    store("D", "yx", 0, "xw", ROT, wh, 2)
     return ops
 
 
@@ -337,38 +370,50 @@ def schedule():
         for d in pred[i]:
             succ[d].append(i)
 
-    def lay(before, after, prio):
-        left, ready, free, start, end, pend = [len(p) for p in before], [0.0] * n, {}, [0.0] * n, [0.0] * n, {}
-        for i in range(n):
-            if not left[i]:
-                pend.setdefault(ops[i]["q"], []).append(i)
-        for _ in range(n):
-            best = None
-            for q, lst in pend.items():
-                if lst:
-                    t = max(free.get(q, 0.0), min(ready[i] for i in lst))
-                    if best is None or t < best[0]:
-                        best = (t, q, max((j for j in lst if ready[j] <= t), key=lambda j: (prio[j], -j)))
-            t, q, i = best
-            pend[q].remove(i)
-            start[i], end[i] = t, t + ops[i]["cost"]
-            if q != "R":
-                free[q] = t + 70.0 if ops[i]["kind"] == "d" else end[i]
-            for s in after[i]:
-                left[s] -= 1
-                ready[s] = max(ready[s], end[i] + (HOP if ops[s]["q"] != q else 10.0))
-                if not left[s]:
-                    pend.setdefault(ops[s]["q"], []).append(s)
+    que, cost, move = [o["q"] for o in ops], [o["cost"] for o in ops], [o["nb"] / RATE for o in ops]
+    hold = [70.0 if o["kind"] == "d" else 0.0 if o["q"] == "R" else o["cost"] for o in ops]
+    lags = [[[(d, SAME if que[d] == que[i] else HOP) for d in links[i]] for i in range(n)] for links in (pred, succ)]
+
+    def fit(busy, t, w):
+        k, hi = 0, len(busy)
+        while k < hi:
+            m = (k + hi) // 2
+            k, hi = (k, m) if busy[m][1] > t else (m + 1, hi)
+        while k < len(busy) and busy[k][0] < t + w:
+            t, k = max(t, busy[k][1]), k + 1
+        busy.insert(k, (t, t + w))
+        return t
+
+    def lay(key, back):
+        busy, start, end = {q: [] for q in set(que) | {"bytes"}}, [0.0] * n, [0.0] * n
+        for i in sorted(range(n), key=lambda j: key[j]):
+            t = max([end[d] + g for d, g in lags[back][i]] or [0.0])
+            if back:
+                t = (fit(busy["bytes"], t + cost[i], move[i]) + move[i] if move[i] else t + cost[i]) - hold[i]
+            start[i] = t = fit(busy[que[i]], t, hold[i]) if hold[i] else t
+            end[i] = t + hold[i] if back else (fit(busy["bytes"], t, move[i]) + move[i] if move[i] else t) + cost[i]
         return start, end
+
+    def both(key):
+        for i in range(n):
+            key[i] = max([key[i]] + [key[d] + 1e-3 for d in pred[i]])
+        end = lay(key, 0)[1]
+        end = lay([-x for x in end], 1)[1]
+        return lay([-x for x in end], 0)
 
     prio = [0.0] * n
     for i in range(n - 1, -1, -1):
-        prio[i] = ops[i]["cost"] + max([prio[s] + (0 if ops[s]["q"] == ops[i]["q"] else HOP) for s in succ[i]] or [0.0])
-    start, end = keep = lay(pred, succ, prio)
+        prio[i] = cost[i] + move[i] + max([prio[s] + HOP for s in succ[i]] or [0.0])
+    now = keep = both([-p for p in prio])
+    kinds = {}
+    kind = np.array([kinds.setdefault(o["cls"], len(kinds)) for o in ops])
+    rng = np.random.default_rng(SEED)
     for _ in range(ROUNDS):
-        start, end = lay(pred, succ, lay(succ, pred, end)[1])
-        if max(end) < max(keep[1]):
-            keep = (start, end)
+        shift = (rng.random(len(kinds)) < SHARE) * (rng.random(len(kinds)) - 0.5) * JITTER
+        new = both([float(x) for x in np.array(now[0]) + shift[kind]])
+        if max(new[1]) <= max(now[1]) + 200 * rng.random():
+            now = new
+            keep = min(keep, now, key=lambda x: max(x[1]))
     start, end = keep
     order = sorted(range(n), key=lambda i: (start[i], i))
     count, fin, know, qk, waits = {}, [None] * n, [None] * n, {}, [[] for _ in ops]
@@ -410,25 +455,18 @@ def rank_program(g, core, T, topo):
     ops, order, waits, fin, count, start, end = CACHE["s"]
     eng = {"V": g.vector, "S": g.scalar, "P": g.tensor, "G": g, "D": g.sync}
     n, sent, X = len(T.cores), [0], {}
-    peers = [T.cores[(rank + d) % n] for d in range(n)]
 
-    def send(dst, src, lo, hi, sem):
-        rid, pid, _ = topo.addr(peers[1])
-        sent[0] += len(topo.engines(core, peers[1]))
-        g.remote_dma_fused([RemoteDMATransfer(dst_ids=[DstId(rid=rid, pnc=pid)], dma_engine_mask=topo.mask(core, peers[1]), remote_sem=T.sem[sem],
-                                              srcs=[T[b][:, lo:hi] for b in src], dsts=[T[dst][:, lo:hi]], alu_op=1)], local_sem=T.sem.loc)
-
-    def stat():
-        for d in range(1, n):
-            rid, pid, _ = topo.addr(peers[d])
-            sent[0] += len(topo.engines(core, peers[d]))
-            g.remote_dma(T["st%d" % d][:], T.st0[:], T.sem["ar%d" % (d - 1)], T.sem.loc, pid, rid, topo.mask(core, peers[d]))
-    X["send"], X["stat"] = send, stat
-    arr = {}
-    for o in ops:
-        if o["kind"] == "a":
-            for d in o["deps"]:
-                arr.setdefault(d, o["sem"])
+    def put(hop, dst, srcs):
+        peer = T.cores[(rank + hop) % n]
+        rid, pid, _ = topo.addr(peer)
+        sent[0] += len(topo.engines(core, peer))
+        if len(srcs) == 1:
+            g.remote_dma(dst(T), srcs[0], T.sem[X["ar"]], T.sem.loc, pid, rid, topo.mask(core, peer))
+        else:
+            g.remote_dma_fused([RemoteDMATransfer(dst_ids=[DstId(rid=rid, pnc=pid)], dma_engine_mask=topo.mask(core, peer), remote_sem=T.sem[X["ar"]],
+                                                  srcs=srcs, dsts=[dst(T)], alu_op=1)], local_sem=T.sem.loc)
+    X["put"] = put
+    arr = {d: o["sem"] for o in ops if o["kind"] == "a" for d in o["deps"]}
     for i in order:
         o = ops[i]
         if o["q"] == "R":

@@ -3,23 +3,23 @@ from concourse.bass import DstId, RemoteDMATransfer
 from concourse.mybir import AluOpType as A, ActivationFunctionType as AF
 
 NV = 5
-CHUNKS = [(192, 256, "SV-"), (128, 192, "SH-"), (64, 128, "SV-"), (0, 64, "SS-")]
-BATCHES = [(128, 256, "Vd"), (0, 128, "Vd")]
-FR = [(192, 256), (128, 192), (0, 128)]
+CHUNKS = [(192, 256, "SV-"), (128, 192, "SH-"), (64, 128, "SV-"), (0, 64, "SHh")]
+BATCHES = [(128, 256, "Vr"), (0, 128, "Vr")]
+FR = [(128, 256, 0), (0, 128, 1)]
+ENG = {"fo": "VG", "bo": "VG", "posu": "VS", "ol": "VS", "ml": "VS", "ui": "VS", "lu": "VS", "n1k": "SS", "c3u": "GG"}
 ROT, EPS, QB, SIGN = 167, 2.0 ** -13, 98304.0, 1 << 23
-CYC, PCYC, GATH, SCAT, HOP, SAME, REMOTE, RATE = 0.85, 0.43, 1.55, 3.5, 170.0, 170.0, 2200.0, 450.0
-FV, FS, MN = 45.0, 65.0, 24.0
-ROUNDS, JITTER, SHARE, SEED = 4000, 6000.0, 0.02, 0
+CYC, PCYC, GATH, SCAT, WAKE, REMOTE, RATE, FV, FS, MN = 0.85, 0.43, 1.55, 3.5, 170.0, 2200.0, 450.0, 45.0, 65.0, 24.0
+ROUNDS, JITTER, SHARE, SEED = 3000, 6000.0, 0.02, 0
 BANKS = ["ba", "bb_", "bn0", "bn1", "bk0", "bk1", "bm", "bu"]
 SIZES = {
-    "bfloat16": "xw 4096 ff 4096 fb 4096 pe 4096 sb 4096 mk 1024 dw 144 uwr 144 uw 128 ib 128 inb 128 hib 128 onb 256 l1 128 l2 128 la 128 "
-                "m128 128 m255 128 epb 256 qa 256 qb 256 pk 256 mp 256 fk 256 bk 256 rr 256 d2 256 n1k 16 tab 64 st0 1024 st1 1024 st2 1024 st3 1024",
-    "float32": "cwo 6144 wf 1 p15f 1 onef 144 t1 128 blk 128 idf 128 upf 128 b8 128 b8r 144 thf 256 rst 128 m8 256 ss 256 dl 256 yt4 256 yl4 256 acol 1 "
+    "bfloat16": "xw 4096 ff 4096 fb 4096 pe 4096 sb 4096 mk 2048 dw 144 uwr 144 uwq 144 uw 128 uwp 128 ib 128 inb 128 hib 128 onb 256 l1 128 l2 128 la 128 "
+                "m128 128 m255 128 spb 256 epb 256 qa 256 qb 256 pk 256 mp 256 fk 256 bk 256 rr 256 d2 256 n1k 16 cb 16 cb4 16 nq 1 tab 96 "
+                "st0 1024 st1 1024 st2 1024 st3 1024",
+    "float32": "cwo 6144 wf 1 p15f 1 onef 144 t1 128 blk 128 idf 128 upf 128 b8 128 b8r 144 thf 256 rst 128 m8 256 dl 256 yt4 256 yl4 256 x2 1 cnt 16 "
                "diag 128 mfw 128 ud 256 lb0 256 lb1 256 lb2 256 lb3 256 lb4 256 lo0 256 lo1 256 lo2 256 lo3 256 lo4 256",
-    "float16": "ta 128 tb 128 td 128 np 256 tb0 256 tb1 256 tb2 256 tb3 256 tb4 256 td0 256 td1 256 td2 256 td3 256 td4 256",
-    "int32": "cw 2048 lgi 256 tni 256 aai 256 bbi 256 thi 256 wti 1 p15 16 ei 128 kai 16 posb 16 rb 16 cb 16 cb4 16 pia 256 pib 256 kint 256 posi 16 xk 16 "
-             "us 256 u15 16 li 32 c3 16 cbv 16 cnt 16 c31 1",
-    "uint16": "fo 256 bo 256 posu 16 ml 16 ol 16 lu 32 c3u 16"}
+    "float16": "ta 128 tb 128 td 128 ih 128 tb0 256 tb1 256 tb2 256 tb3 256 tb4 256 td0 256 td1 256 td2 256 td3 256 td4 256",
+    "int32": "cw 2048 lgi 256 tni 256 aai 256 bbi 256 thi 256 wti 1 p15 16 ei 128 kai 16 posb 16 rb 16 pi 512 kint 256 posi 16 xk 16 us 256 u15 16 li 32 c3 16",
+    "uint16": "fo 512 posu 16 ml 16 ol 16 lu 32 c3u 16"}
 SCRATCH = {n: ("psum", [128, 512], "float32") for n in BANKS}
 for _d in SIZES:
     _l = SIZES[_d].split()
@@ -91,9 +91,6 @@ def program():
             return g.vector.tensor_scalar(view(T, out), view(T, a), x1, s2, o1, o2) if o2 else g.vector.tensor_scalar(view(T, out), view(T, a), x1, None, o1)
         add("V", vc(ln(out), fast(out, a)), reg(a) + ([(s1, 0, 1)] if isinstance(s1, str) else []), reg(out), em)
 
-    def cp(out, a):
-        add("V", vc(ln(out), fast(out, a)), reg(a), reg(out), lambda g, T, X: g.vector.tensor_copy(view(T, out), view(T, a)))
-
     def ms(out, c):
         add("V", vc(ln(out), fast(out)), [], reg(out), lambda g, T, X: g.vector.memset(view(T, out), c))
 
@@ -102,6 +99,17 @@ def program():
 
     def act(out, a, scale=1.0, bias=0.0, fn=AF.Identity):
         add("S", FS - FV + vc(ln(out)), reg(a), reg(out), lambda g, T, X: g.scalar.activation(view(T, out), view(T, a), fn, bias=bias, scale=scale))
+
+    def sel(out, src, pattern, cmp, base, cm):
+        add("G", 170 + 2 * ln(out) * CYC, reg(src), reg(out), lambda g, T, X: g.affine_select(view(T, out), view(T, src), pattern, cmp, 0.0, base, cm))
+
+    def cp(out, a, q="V"):
+        if q == "V":
+            add("V", vc(ln(out), fast(out, a)), reg(a), reg(out), lambda g, T, X: g.vector.tensor_copy(view(T, out), view(T, a)))
+        elif q == "S":
+            act(out, a)
+        else:
+            sel(out, a, [[0, ln(out)]], A.is_ge, 0, 0)
 
     def gather(q, out, win, off):
         if q == "H":
@@ -121,10 +129,6 @@ def program():
         for o, lt, rh in terms:
             rd += reg(lt) + (rh[0] if len(rh) == 2 else reg(rh))
         add("P", sum(max(64, ln(o)) * PCYC * (4 if SCRATCH[lt[0]][2] == "float32" else 1) for o, lt, _ in terms), rd, [(bank, 0, 512)], em)
-
-    def sel(out, src, pattern, cmp, base, cm, parts=128):
-        add("G", 170 + 2 * ln(out) * CYC, reg(src), reg(out),
-            lambda g, T, X: g.affine_select(T[out[0]][0:parts, out[1]:out[2]], T[src[0]][0:parts, src[1]:src[2]], pattern, cmp, 0.0, base, cm))
 
     def iota(out, pattern, base, cm):
         add("G", 130 + 2 * ln(out) * CYC, [], reg(out), lambda g, T, X: g.iota(view(T, out), pattern, base, cm))
@@ -149,27 +153,32 @@ def program():
         lo, hi = BATCHES[ib][:2]
         return (16 * lo + 160, 16 * hi + 176) if 16 * hi + 176 <= 4096 else (0, 4096)
 
+    def spots(nb, cl, ch):
+        lo, hi = [p[:2] for p in FR if p[0] <= cl < p[1]][0]
+        return ("fo", lo + cl + nb * (hi - lo), lo + ch + nb * (hi - lo))
+
     load("D", "tn", "tni", 0, 256, 0)
     load("S", "lg", "lgi", 0, 256, 0)
     load("D", "aa", "aai", 0, 256, 0, 8)
     load("S", "bb", "bbi", 0, 256, 0, 8)
     load("D", "xt", "xw", ROT, 4096, 0, size=2)
     load("S", "xt", "xw", 0, ROT, 4096 - ROT, size=2)
-    load("D", "sp", "st0", 0, 256, 0, size=2)
+    load("D", "sp", "spb", 0, 256, 0, size=2)
     load("S", "ep", "epb", 0, 256, 0, size=2)
     load("D", "th", "thi", 0, 256, 0, 8)
     load("S", "wt", "wti", 0, 1, 0)
     load("D", "ct", "cw", 0, 1024, 0)
     ms(("onef", 0, 144), 1.0)
-    one, blk, idf, b8 = ("onef", 0, 128), ("blk", 0, 128), ("idf", 0, 128), ("b8", 0, 128, 1, 8)
+    one, blk, idf, b8, one8 = ("onef", 0, 128), ("blk", 0, 128), ("idf", 0, 128), ("b8", 0, 128, 1, 8), ("onef", 0, 128, 1, 8)
+    I, NI, HI, IH, xw = ("ib", 0, 128), ("inb", 0, 128), ("hib", 0, 128), ("ih", 0, 128), ("xw", 0, 4096)
     sel(("t1", 0, 128), one, [[-16, 8], [0, 16]], A.is_ge, 0, 1)
     sel(blk, ("t1", 0, 128), [[16, 8], [0, 16]], A.is_ge, 15, -1)
     sel(("upf", 0, 128), blk, [[1, 128]], A.is_ge, 0, -1)
-    sel(("t1", 0, 128), one, [[1, 128]], A.is_ge, 0, -16, 8)
-    sel(b8[:3], ("t1", 0, 128), [[-1, 128]], A.is_ge, 15, 16, 8)
+    sel(("thf", 0, 128, 1, 8), one8, [[1, 128]], A.is_ge, 0, -16)
+    sel(b8, ("thf", 0, 128, 1, 8), [[-1, 128]], A.is_ge, 15, 16)
     sel(idf, one, [[-1, 128]], A.is_equal, 0, 1)
     sel(("t1", 0, 128), blk, [[-1, 128]], A.is_gt, 0, 1)
-    sel(("b8r", 0, 144), ("onef", 0, 144), [[1, 144]], A.is_equal, -15, -16, 8)
+    sel(("b8r", 0, 144, 1, 8), ("onef", 0, 144, 1, 8), [[1, 144]], A.is_equal, -15, -16)
     iota(("p15", 0, 16), [[0, 16]], 0, 1)
     iota(("ei", 0, 128), [[0, 8], [1, 16]], 0, 0)
     ms(("st0", 512, 1024), 1.0)
@@ -180,72 +189,82 @@ def program():
     act(("l1", 0, 128, 1, 8), b8, scale=-2.0)
     ts(("tb", 0, 128), ("t1", 0, 128), -2.0, A.mult)
     ts(("td", 0, 128), blk, -2.0, A.mult)
-    for n, k in (("inb", -1.0), ("ib", 1.0), ("hib", 0.5)):
-        act((n, 0, 128), idf, scale=k)
+    for n, k in ((NI, -1.0), (I, 1.0), (HI, 0.5), (IH, 1.0)):
+        act(n, idf, scale=k)
     cp(("tb0", 0, 256), ("tni", 0, 256))
-    cp(("lb0", 0, 256), ("lgi", 0, 256))
+    cp(("lb0", 0, 256), ("lgi", 0, 256), "S")
     cp(("st0", 512, 768, 1, 8), ("aai", 0, 256, 1, 8))
-    cp(("st0", 768, 1024, 1, 8), ("bbi", 0, 256, 1, 8))
-    ms(("mk", 0, 1024), 1.0)
-    ms(("mk", 15, 1024, 16), 0.0)
+    cp(("st0", 768, 1024, 1, 8), ("bbi", 0, 256, 1, 8), "S")
+    width = 16 * max(c[1] - c[0] for c in CHUNKS)
+    ms(("mk", 0, width), 1.0)
+    ms(("mk", 15, width, 16), 0.0)
     ms(("pe", 0, 4096, 256), 0.0)
-    ms(("dw", 0, 144), 0.0)
-    ms(("uwr", 0, 144), 0.0)
+    for n in ("dw", "uwr", "uwq"):
+        ms((n, 0, 144), 0.0)
     act(("dw", 15, 143, 16), ("blk", 0, 128, 16), scale=2048.0)
-    tt(("st0", 256, 512), ("st0", 0, 256), ("epb", 0, 256), A.subtract)
+    act(("st0", 0, 256), ("spb", 0, 256), scale=-1.0, bias=255.0)
+    mm("bm", [(("bm", 0, 256), I, ("spb", 0, 256)), (("bm", 0, 256), NI, ("epb", 0, 256))])
+    act(("st0", 256, 512), ("bm", 0, 256))
     for d in range(1, 4):
         put(d, ("st%d" % d, 0, 1024), [("st0", 0, 1024)], 2)
     ms(("onb", 0, 256), 1.0)
     ms(("m128", 0, 128), -128.0)
     ms(("m255", 0, 128), -255.0)
-    ms(("mfw", 0, 128), 1.0)
-    ms(("mfw", 0, 128, 16), 0.0)
     ms(("rst", 0, 128), -1e9)
     ms(("rst", 0, 128, 16), 1e9)
-    ms(("tab", 0, 64), 0.0)
+    ms(("tab", 0, 96), 0.0)
     ts(("p15", 0, 16), ("p15", 0, 16), 15, A.bitwise_and)
-    cp(("p15f", 0, 1), ("p15", 0, 1))
-    ts(("diag", 0, 128), ("ei", 0, 128), "p15f", A.is_equal)
+    if any(b[2][1] == "d" for b in BATCHES):
+        ms(("mfw", 0, 128), 1.0)
+        ms(("mfw", 0, 128, 16), 0.0)
+        cp(("p15f", 0, 1), ("p15", 0, 1))
+        ts(("diag", 0, 128), ("ei", 0, 128), "p15f", A.is_equal)
     ts(("kai", 0, 16), ("ei", 0, 16), 16.0, A.mult)
     tt(("kai", 0, 16), ("kai", 0, 16), ("p15", 0, 16), A.add)
-    ts(("cb", 0, 16), ("kai", 0, 16), 4.0, A.mult)
+    act(("cb", 0, 16), ("kai", 0, 16), scale=4.0)
     for ib, (lo, hi, _) in enumerate(BATCHES):
         c = ("kai", lo // 16, hi // 16)
-        ts(("rb",) + c[1:], c, 16.0, A.mult, float(ROT - window(ib)[0]), A.add)
-        ts(("posb",) + c[1:], c, 16.0, A.mult, float(-16 * lo), A.add)
-        ts(("cb4",) + c[1:], c, 4.0, A.mult, float(-4 * lo), A.add)
-    tt(("tab", 0, 16), ("p15", 0, 16), ("ei", 0, 16), A.is_ge)
+        act(("rb",) + c[1:], c, scale=16.0, bias=float(ROT - window(ib)[0]))
+        act(("posb",) + c[1:], c, scale=16.0, bias=float(-16 * lo))
+        act(("cb4",) + c[1:], c, scale=4.0, bias=float(-4 * lo))
+    if "S" in ENG["ml"]:
+        tt(("u15", 0, 16), ("ei", 0, 16), ("p15", 0, 16), A.add)
+        ts(("tab", 1, 17), ("u15", 0, 16), 15.0, A.is_ge)
+    if "V" in ENG["ml"]:
+        tt(("tab", 64, 80), ("p15", 0, 16), ("ei", 0, 16), A.is_ge)
     tt(("tab", 33, 49), ("p15", 0, 16), ("ei", 0, 16), A.is_equal)
     ts(("tab", 33, 49), ("tab", 33, 49), 0.5, A.mult)
     cp(("wf", 0, 1), ("wti", 0, 1))
     ts(("uw", 0, 128), blk, "wf", A.mult, -1.0, A.mult)
-    cp(("uwr", 15, 143, 16), ("uw", 0, 128, 16))
-    ts(("thf", 0, 256, 1, 8), ("thi", 0, 256, 1, 8), -2048.0, A.mult, -2048.0, A.add)
+    act(("uwp", 0, 128), ("uw", 0, 128), scale=-1.0)
+    act(("uwr", 15, 143, 16), ("uw", 0, 128, 16))
+    act(("uwq", 15, 143, 16), ("uw", 0, 128, 16), scale=-1.0)
+    act(("thf", 0, 256, 1, 8), ("thi", 0, 256, 1, 8), scale=-2048.0, bias=-2048.0)
     mm("bu", [(("bu", 0, 16), ("b8r", 15 - r, 143 - r, 1, 8), ("thf", r, 256, 16, 8)) for r in range(16)])
     add("V", vc(16), [("bu", 0, 16), ("posb", 0, 16)], [("kf", 0, 256)], lambda g, T, X: g.vector.tensor_tensor(T.kf[:, :, 0], T.bu[:, 0:16], T.posb[:, 0:16], A.add))
     for s in (1, 2, 4, 8):
         add("V", vc(16 * s), [("kf", 0, 256)], [("kf", 0, 256)], lambda g, T, X, s=s: g.vector.tensor_scalar(T.kf[:, :, s:2 * s], T.kf[:, :, 0:s], float(s), None, A.add))
-    I, NI, HI, xw = ("ib", 0, 128), ("inb", 0, 128), ("hib", 0, 128), ("xw", 0, 4096)
-    nd = [0]
     for v in range(NV):
         L, Tn, st, Lo, To = "lb%d" % v, "tb%d" % v, "st%d" % (v % 4), "lo%d" % v, "td%d" % v
         last = v == NV - 1
         first[:] = [len(ops) - 1000 * last]
         if last:
             for ib, (lo, hi, _) in enumerate(BATCHES):
-                cp(("cwo", 1536 * ib, 1536 * ib + 4 * (hi - lo)), ("cw", 4 * lo, 4 * hi))
-        for lo, hi in FR:
+                cp(("cwo", 1536 * ib, 1536 * ib + 4 * (hi - lo)), ("cw", 4 * lo, 4 * hi), "G")
+        for ip, (lo, hi, joint) in enumerate(FR):
             act(("m8", lo, hi), (L, lo, hi), scale=0.125, bias=18.5 + EPS)
-            for nb, (bank, tri, q, pi, off, c0) in enumerate((("ba", "ta", "qa", "pia", "fo", 512), ("bb_", "tb", "qb", "pib", "bo", 768))):
-                o = (bank, lo, hi)
+            for nb, (bank, tri, q, c0) in enumerate((("ba", "ta", "qa", 512), ("bb_", "tb", "qb", 768))):
+                o, off = (bank, lo, hi), spots(nb, lo, hi)
                 base = ([(o, (tri, 0, 128), (Tn, lo, hi)), (o, ("l2", 0, 128, 1, 10), (st, c0 + lo, c0 + hi, 1, 10))]
                         + ([(o, ("la", 0, 128, 1, 1), ("onb", lo, hi, 1, 1))] if nb and v else []))
                 mm(bank, base)
                 act((q, lo, hi), o, bias=-264.0)
                 mm(bank, base + [(o, NI, (q, lo, hi))])
-                tt((pi, lo, hi), o, ("m8", lo, hi), A.mult)
-                ts((pi, lo, hi), (pi, lo, hi), 4095, A.bitwise_and)
-                cp((off, lo, hi), (pi, lo, hi))
+                tt(("pi",) + off[1:], o, ("m8", lo, hi), A.mult)
+                if nb or not joint:
+                    off = ("fo", 2 * lo, 2 * hi) if joint else off
+                    ts(("pi",) + off[1:], ("pi",) + off[1:], 4095, A.bitwise_and)
+                    cp(off, ("pi",) + off[1:], ENG["bo" if nb else "fo"][ip])
         for ib, (lo, hi, pq) in enumerate(BATCHES):
             bk = "bk%d" % (ib & 1)
             o = ("bm", 256 + lo, 256 + hi)
@@ -255,52 +274,67 @@ def program():
             for cl, ch, who in CHUNKS:
                 if not lo <= cl < hi:
                     continue
-                a, b, n, c0, c1 = 16 * cl, 16 * ch, ch - cl, cl // 16, ch // 16
-                gather(who[0], ("ff", a, b), xw, ("fo", cl, ch))
+                a, b = 16 * cl, 16 * ch
+                gather(who[0], ("ff", a, b), xw, spots(0, cl, ch))
                 scan(("pe", a + 1, b), ("ff", a, b - 1), ("mk", 0, b - a - 1), A.add, A.mult)
-                gather(who[1], ("fb", a, b), xw, ("bo", cl, ch))
-                b15, o1, o2 = ("fb", a + 15, b, 16), ("ba", 256, 256 + n), ("ba", 384, 384 + n)
-                if who[2] == "a":
-                    mm("ba", [(o1, I, b15), (o1, I, (st, 256 + cl, 256 + ch))])
-                    mm("ba", [(o2, I, b15)])
-                    act(b15, o1)
+                gather(who[1], ("fb", a, b), xw, spots(1, cl, ch))
                 scan(("sb", a, b, -1), ("mk", 0, b - a, -1), ("fb", a, b, -1), A.mult, A.add)
-                if who[2] == "a":
-                    act(b15, o2)
-                for h in (0, 1):
-                    bn = "bn%d" % h
-                    o = (bn, 0, 8 * n)
-                    mm(bn, [(o, I, ("pe", a + h, b, 2))] + [((bn, m, 8 * n, 8), I, (st, 256 + cl, 256 + ch)) for m in range(8) if who[2] != "a"], closes=False)
-                    mm(bn, [(o, I, ("sb", a + h, b, 2))], opens=False)
-                    add("S", FS - FV + vc(8 * n), [o], [("ab", a, b)], lambda g, T, X, c0=c0, c1=c1, h=h, o=o: g.scalar.activation(T.ab[:, c0:c1, :, h:16:2], view(T, o), AF.Abs))
-                add("V", vc(b - a, 0.5), [("ab", a, b)], [("ab", a, b)], lambda g, T, X, c0=c0, c1=c1: g.vector.tensor_scalar(T.ab[:, c0:c1], T.ab[:, c0:c1], 255.0, None, A.min))
+                for l in range(cl, ch, 64):
+                    u = min(l + 64, ch)
+                    for h in (0, 1):
+                        bn, half = "bn%d" % h, [("ab%d" % h, 16 * l, 16 * u)]
+                        o = (bn, 0, 8 * (u - l))
+                        mm(bn, [(o, I, ("pe", 16 * l + h, 16 * u, 2))] + [((bn, m, o[2], 8), I, (st, 256 + l, 256 + u)) for m in range(8)], closes=False)
+                        mm(bn, [(o, I, ("sb", 16 * l + h, 16 * u, 2))], opens=False)
+                        add("S", FS - FV + vc(o[2]), [o], half, lambda g, T, X, l=l, u=u, h=h, o=o: g.scalar.activation(T.ab[:, l // 16:u // 16, :, h:16:2], view(T, o), AF.Abs))
+                        if who[2] == "h":
+                            add("V", vc(o[2], 0.5), half, half, lambda g, T, X, l=l, u=u, h=h: g.vector.tensor_scalar(T.ab[:, l // 16:u // 16, :, h:16:2], T.ab[:, l // 16:u // 16, :, h:16:2], 255.0, None, A.min))
+                c0, c1, both = cl // 16, ch // 16, [("ab0", a, b), ("ab1", a, b)]
+                if who[2] != "h":
+                    add("V", vc(b - a, 0.5), both, both, lambda g, T, X, c0=c0, c1=c1: g.vector.tensor_scalar(T.ab[:, c0:c1], T.ab[:, c0:c1], 255.0, None, A.min))
                 od = (bk, cl - lo, ch - lo)
                 mm(bk, [(od, idf, ([("kf", cl, ch)], lambda T, c0=c0, c1=c1: T.kf[:, c0:c1]))], closes=False)
-                mm(bk, [(od, ("dw", 15 - r, 143 - r), ([("ab", a, b)], lambda T, r=r, c0=c0, c1=c1: T.ab[:, c0:c1, r, :])) for r in range(16)], opens=False)
+                mm(bk, [(od, ("dw", 15 - r, 143 - r), (both, lambda T, r=r, c0=c0, c1=c1: T.ab[:, c0:c1, r, :])) for r in range(16)], opens=False)
             a, b, n, c0, c1 = 16 * lo, 16 * hi, hi - lo, lo // 16, hi // 16
 
             def sm(nm):
                 return (nm, c0, c1)
-            os_, ou = ("bm", lo, hi), ("bu", c0, c1)
+            os_, ou, u = ("bm", lo, hi), ("bu", c0, c1) if pq[1] == "r" else ("bu", 0, n), ("us", lo + 15, hi, 16)
+
+            def weigh(res, full, x):
+                return [(ou, (res, 15 - r, 143 - r), (x, lo + r, hi, 16)) for r in range(16)] if pq[1] == "r" else [(ou, (full, 0, 128), (x, lo, hi))]
+            mm("bu", [(ou, ("uw", 0, 128), ("m255", 0, ln(ou)))] + (weigh("uwr", "uw", st) if pq[0] == "V" else []), closes=False)
             scan(("kint", lo, hi), ("rst", 0, n), (bk, 0, n), A.max, A.min)
             key = ("kint", lo + 15, hi, 16)
             ts(sm("posi"), key, 2047, A.bitwise_and)
-            cp(sm("posu"), sm("posi"))
+            cp(sm("posu"), sm("posi"), ENG["posu"][ib])
+            ts(sm("xk"), key, SIGN | 15, A.bitwise_and)
+            if last or ib == len(BATCHES) - 1:
+                cs, bc = ((c0, c1), bk) if last else ((0, 16), "bk0")
+                if ENG["n1k"][ib] == "S":
+                    act(("n1k",) + cs, ("xk",) + cs, scale=2.0 ** -13, bias=-0.002, fn=AF.Relu)
+                else:
+                    ts(("n1k",) + cs, ("kint", 16 * cs[0] + 15, 16 * cs[1], 16), 0.0, A.is_lt, 1024.0, A.mult)
+                if not last:
+                    mm(bc, [((bc, 256, 272), ("onb", 0, 128), ("n1k", 0, 16))])
+                    add("S", FS + 40, [(bc, 256, 272)], [("cnt", 0, 16), ("x2", 0, 1)],
+                        lambda g, T, X, bc=bc: g.scalar.activation(T.cnt[0:1, 0:16], T[bc][0:1, 256:272], AF.Identity, bias=896.0, scale=-2.0 / 1024, accum_out=T.x2[0:1, 0:1]))
+                    act(("nq", 0, 1, 1, 1), ("x2", 0, 1, 1, 1), scale=-1.0, bias=31.0)
+                    add("S", FS - FV + vc(128), [("x2", 0, 1), ("nq", 0, 1), ("onb", 0, 128)], [("la", 0, 128)],
+                        lambda g, T, X: g.scalar.activation(T.la[0:1, 0:128], T.onb[0:1, 0:128], AF.Identity, bias=T.nq[0:1, 0:1], scale=T.x2[0:1, 0:1]))
+                oc = (bc, 288 + cs[0], 288 + cs[1])
+                mm(bc, [(oc, I, ("n1k",) + cs), (oc, I, ("cb4" if last else "cb",) + cs)])
             if pq[0] == "S":
                 gather("S", ("pk", lo, hi), ("pe", a, b), sm("posu"))
-                mm("bm", [(os_, I, (st, lo, hi)), (os_, I, ("pk", lo, hi))])
-                act(("mp", lo, hi), os_, scale=-1.0, bias=255.0, fn=AF.Relu)
+                mm("bm", [(os_, I, (st, lo, hi)), (os_, NI, ("pk", lo, hi))])
+                act(("mp", lo, hi), os_, fn=AF.Relu)
+                mm("bu", weigh("uwr", "uw", "mp"), opens=False)
             else:
-                gtt(("pk", lo, hi), ("pe", a, b), sm("posu"), (st, lo, hi), A.add)
-                ts(("mp", lo, hi), ("pk", lo, hi), 255.0, A.min, -1.0, A.mult)
-            u = ("us", lo + 15, hi, 16)
+                gtt(("mp", lo, hi), ("pe", a, b), sm("posu"), (st, lo, hi), A.min)
+                mm("bu", weigh("uwq", "uwp", "mp"), opens=False)
             if pq[1] == "r":
-                mm("bu", ([(ou, ("uw", 0, 128), ("m255", 0, c1 - c0))] if pq[0] == "S" else [])
-                   + [(ou, ("uwr", 15 - r, 143 - r), ("mp", lo + r, hi, 16)) for r in range(16)])
-                cp(u, ou)
+                cp(u, ou, ENG["ui"][ib])
             else:
-                ou = ("bu", 0, n)
-                mm("bu", ([(ou, ("uw", 0, 128), ("m255", 0, n))] if pq[0] == "S" else []) + [(ou, ("uw", 0, 128), ("mp", lo, hi))])
                 tt(("ud", lo, hi), ou, ("diag", 0, n), A.mult)
                 scan(("us", lo, hi), ("mfw", 0, n), ("ud", lo, hi), A.mult, A.add)
             cg, r1, both = ("li", 2 * c0, c0 + c1), ("li", c0 + c1, 2 * c1), (2 * c0, 2 * c1)
@@ -309,54 +343,56 @@ def program():
             tt(r1, sm("u15"), sm("rb"), A.add)
             if window(ib)[1] == 4096:
                 ts(r1, r1, 4095, A.bitwise_and)
-            cp(("lu",) + both, ("li",) + both)
-            ts(sm("xk"), key, SIGN | 15, A.bitwise_and)
-            ts(sm("ol"), sm("xk"), float(1 - SIGN), A.add, 0.0, A.max)
-            ts(sm("ml"), sm("xk"), 16.0, A.min)
+            cp(("lu",) + both, ("li",) + both, ENG["lu"][ib])
+            for nm, k, c in (("ol", 1.0, 1.0 - SIGN), ("ml", -1.0, 16.0)):
+                if ENG[nm][ib] == "S":
+                    act(sm(nm), sm("xk"), scale=k, bias=c, fn=AF.Relu)
+                elif k > 0:
+                    ts(sm(nm), sm("xk"), c, A.add, 0.0, A.max)
+                else:
+                    ts(sm(nm), sm("xk"), c, A.min)
             gtt((To, lo, hi), ("tab", 32, 64), sm("ol"), ("d2", lo, hi), A.mult)
-            if last:
-                tt(("pia", lo, hi), (Tn, lo, hi), (To, lo, hi), A.add)
-                ts(("pia", lo, hi), ("pia", lo, hi), 255, A.bitwise_and)
-                cp(("yt4", lo, hi), ("pia", lo, hi))
-                store("S", "yt", lo, "yt4", lo, hi)
-            else:
+            if not last:
                 put(1, ("tb%d" % (v + 1), lo, hi), [(Tn, lo, hi), (To, lo, hi)], 2)
             gtt(("dl", lo, hi), ("cw", 0, 1024), ("lu",) + cg[1:], (L, lo, hi), A.subtract)
-            gtt((Lo, lo, hi), ("tab", 0, 32), sm("ml"), ("dl", lo, hi), A.mult)
-            if last:
-                tt(("yl4", lo, hi), (L, lo, hi), (Lo, lo, hi), A.add)
-                store("D", "yl", lo, "yl4", lo, hi)
-            else:
+            gtt((Lo, lo, hi), ("tab", 0, 32) if ENG["ml"][ib] == "S" else ("tab", 64, 96), sm("ml"), ("dl", lo, hi), A.mult)
+            if not last:
                 put(1, ("lb%d" % (v + 1), lo, hi), [(L, lo, hi), (Lo, lo, hi)], 4)
             gather("S", ("fk", lo, hi), ("ff", a, b), sm("posu"))
             gather("S", ("bk", lo, hi), ("fb", a, b), sm("posu"))
             mm("bm", [(os_, HI, ("fk", lo, hi)), (os_, HI, ("bk", lo, hi))])
             act(("rr", lo, hi), os_, bias=127.875)
+            if last:
+                o = ("ba", lo, hi)
+                mm("ba", [(o, IH, (Tn, lo, hi)), (o, IH, (To, lo, hi))])
+                act(("qa", lo, hi), o, bias=49024.5)
+                mm("ba", [(o, IH, (Tn, lo, hi)), (o, IH, (To, lo, hi)), (o, NI, ("qa", lo, hi))])
+                act(("yt4", lo, hi), o, bias=49152.0)
+                store("S", "yt", lo, "yt4", lo, hi)
+                o = ("bb_", lo, hi)
+                mm("bb_", [(o, idf, (L, lo, hi))], closes=False)
+                mm("bb_", [(o, idf, (Lo, lo, hi))], opens=False)
+                act(("yl4", lo, hi), o)
+                store("S", "yl", lo, "yl4", lo, hi)
+                c3s = [(ib, lo, hi)]
+            else:
+                c3s = [(ib, 0, 256)] if ib == len(BATCHES) - 1 else []
+            for ib, lo, hi in c3s:
+                c3 = ("c3", lo // 16, hi // 16)
+                ts(c3, ("us", lo + 15, hi, 16), 3, A.bitwise_and)
+                tt(c3, c3, oc, A.add)
+                cp(("c3u",) + c3[1:], c3, "V" if last else ENG["c3u"][ib])
+                scatter(("cwo", 1536 * ib, 1536 * ib + 1536) if last else ("cw", 0, 2048), ("c3u",) + c3[1:], [(L, lo, hi)],
+                        lambda e, T, w, L=L, lo=lo, hi=hi: e.tensor_copy(w, T[L][:, lo:hi]))
+                if last:
+                    store("D", "yc", 4 * lo, "cwo", 1536 * ib, 1536 * ib + 4 * (hi - lo))
         for ib, (lo, hi, pq) in enumerate(BATCHES):
             c0, c1 = lo // 16, hi // 16
             scatter(("xw",) + window(ib), ("lu", c0 + c1, 2 * c1), [("rr", lo, hi), ("m128", 0, hi - lo)],
                     lambda e, T, w, lo=lo, hi=hi: e.tensor_tensor(w, T.rr[:, lo:hi], T.m128[:, 0:hi - lo], A.add))
-        for ib, (lo, hi) in enumerate([b[:2] for b in BATCHES] if last else [(0, 256)]):
-            c0, c1 = lo // 16, hi // 16
-            ts(("n1k", c0, c1), ("kint", lo + 15, hi, 16), 0.0, A.is_lt, 1024.0, A.mult)
-            tt(("cbv", c0, c1), ("cb4" if last else "cb", c0, c1), ("n1k", c0, c1), A.add)
-            ts(("c3", c0, c1), ("us", lo + 15, hi, 16), 3, A.bitwise_and)
-            tt(("c3", c0, c1), ("c3", c0, c1), ("cbv", c0, c1), A.add)
-            cp(("c3u", c0, c1), ("c3", c0, c1))
-            scatter(("cwo", 1536 * ib, 1536 * ib + 1536) if last else ("cw", 0, 2048), ("c3u", c0, c1), [(L, lo, hi)],
-                    lambda e, T, w, L=L, lo=lo, hi=hi: e.tensor_copy(w, T[L][:, lo:hi]))
-            if last:
-                store("DS"[ib & 1], "yc", 4 * lo, "cwo", 1536 * ib, 1536 * ib + 4 * (hi - lo))
-        if not last:
-            mm("bu", [(("bu", 0, 16), ("onb", 0, 128), ("n1k", 0, 16))])
-            scan(("cnt", 0, 16), ("onb", 0, 16), ("bu", 0, 16), A.mult, A.subtract)
-            ts(("c31", 0, 1), ("cnt", 15, 16), 10, A.arith_shift_right, 31, A.bitwise_and)
-            cp(("acol", 0, 1), ("c31", 0, 1))
-            add("V", vc(64), [("acol", 0, 1), ("onb", 0, 128)], [("la", 0, 128)],
-                lambda g, T, X: g.vector.tensor_scalar(T.la[0:1, 0:128], T.onb[0:1, 0:128], T.acol[0:1, 0:1], 2.0, A.mult, A.mult))
     wl, wh = window(len(BATCHES) - 1)
     store("D", "yx", wh - ROT, "xw", wh, 4096, 2)
-    store("S", "yx", 4096 - ROT, "xw", 0, wl, 2)
+    store("D", "yx", 4096 - ROT, "xw", 0, wl, 2)
     store("S", "yx", 4096 - ROT + wl, "xw", wl, ROT, 2)
     store("D", "yx", 0, "xw", ROT, wh, 2)
     return ops
@@ -369,10 +405,9 @@ def schedule():
     for i in range(n):
         for d in pred[i]:
             succ[d].append(i)
-
     que, cost, move = [o["q"] for o in ops], [o["cost"] for o in ops], [o["nb"] / RATE for o in ops]
     hold = [70.0 if o["kind"] == "d" else 0.0 if o["q"] == "R" else o["cost"] for o in ops]
-    lags = [[[(d, SAME if que[d] == que[i] else HOP) for d in links[i]] for i in range(n)] for links in (pred, succ)]
+    lags = [[[(d, 0.0 if que[d] == que[i] == "P" else WAKE) for d in links[i]] for i in range(n)] for links in (pred, succ)]
 
     def fit(busy, t, w):
         k, hi = 0, len(busy)
@@ -403,7 +438,7 @@ def schedule():
 
     prio = [0.0] * n
     for i in range(n - 1, -1, -1):
-        prio[i] = cost[i] + move[i] + max([prio[s] + HOP for s in succ[i]] or [0.0])
+        prio[i] = cost[i] + move[i] + max([prio[s] + WAKE for s in succ[i]] or [0.0])
     now = keep = both([-p for p in prio])
     kinds = {}
     kind = np.array([kinds.setdefault(o["cls"], len(kinds)) for o in ops])

@@ -6,19 +6,19 @@ NV = 5
 CHUNKS = [(192, 256, "SV-"), (128, 192, "SH-"), (64, 128, "SV-"), (0, 64, "SHh")]
 BATCHES = [(128, 256, "Vr"), (0, 128, "Vr")]
 FR = [(128, 256, 0), (0, 128, 1)]
-ENG = {"fo": "VG", "bo": "VG", "posu": "VS", "ol": "VS", "ml": "VS", "ui": "VS", "lu": "VS", "n1k": "SS", "c3u": "GG"}
-ROT, EPS, QB, SIGN = 167, 2.0 ** -13, 98304.0, 1 << 23
+ENG = {"fo": "VG", "bo": "VG", "posu": "VS", "ol": "VS", "ml": "VS", "ui": "VS", "lu": "GS", "cg": "VS", "n1k": "SS", "yl": "SV", "ctl": "S"}
+ROT, C148, QB, SIGN = 167, 148.0 + 2.0 ** -10, 12288.0, 1 << 23
 CYC, PCYC, GATH, SCAT, WAKE, REMOTE, RATE, FV, FS, MN = 0.85, 0.43, 1.55, 3.5, 170.0, 2200.0, 450.0, 45.0, 65.0, 24.0
-ROUNDS, JITTER, SHARE, SEED = 3000, 6000.0, 0.02, 0
-BANKS = ["ba", "bb_", "bn0", "bn1", "bk0", "bk1", "bm", "bu"]
+ROUNDS, JITTER, SHARE, SLACK, AIM, COPY, SEED = 8000, 5000.0, 0.02, 800.0, 0.6, 0.03, 1
+BANKS = ["ba", "bb_", "bn0", "bn1", "bn2", "bk0", "bk1", "bu"]
 SIZES = {
     "bfloat16": "xw 4096 ff 4096 fb 4096 pe 4096 sb 4096 mk 2048 dw 144 uwr 144 uwq 144 uw 128 uwp 128 ib 128 inb 128 hib 128 onb 256 l1 128 l2 128 la 128 "
                 "m128 128 m255 128 spb 256 epb 256 qa 256 qb 256 pk 256 mp 256 fk 256 bk 256 rr 256 d2 256 n1k 16 cb 16 cb4 16 nq 1 tab 96 "
                 "st0 1024 st1 1024 st2 1024 st3 1024",
-    "float32": "cwo 6144 wf 1 p15f 1 onef 144 t1 128 blk 128 idf 128 upf 128 b8 128 b8r 144 thf 256 rst 128 m8 256 dl 256 yt4 256 yl4 256 x2 1 cnt 16 "
+    "float32": "cwo 6144 wf 1 p15f 1 onef 144 t1 128 blk 128 idf 128 upf 128 b8 128 b8r 144 thf 256 rst 128 c148 128 m80 256 m81 256 m82 256 m83 256 m84 256 cwf 2048 yt4 256 yl4 256 x2 1 cnt 16 "
                "diag 128 mfw 128 ud 256 lb0 256 lb1 256 lb2 256 lb3 256 lb4 256 lo0 256 lo1 256 lo2 256 lo3 256 lo4 256",
     "float16": "ta 128 tb 128 td 128 ih 128 tb0 256 tb1 256 tb2 256 tb3 256 tb4 256 td0 256 td1 256 td2 256 td3 256 td4 256",
-    "int32": "cw 2048 lgi 256 tni 256 aai 256 bbi 256 thi 256 wti 1 p15 16 ei 128 kai 16 posb 16 rb 16 pi 512 kint 256 posi 16 xk 16 us 256 u15 16 li 32 c3 16",
+    "int32": "cw 1024 dl 256 lgi 256 tni 256 aai 256 bbi 256 thi 256 wti 1 p15 16 ei 128 kai 16 posb 16 rb 16 pi 512 kint 256 posi 16 xk 16 us 256 u15 16 li 32 c3 16",
     "uint16": "fo 512 posu 16 ml 16 ol 16 lu 32 c3u 16"}
 SCRATCH = {n: ("psum", [128, 512], "float32") for n in BANKS}
 for _d in SIZES:
@@ -134,7 +134,7 @@ def program():
         add("G", 130 + 2 * ln(out) * CYC, [], reg(out), lambda g, T, X: g.iota(view(T, out), pattern, base, cm))
 
     def dma(q, nbytes, rd, wr, fn):
-        add(q, 2000.0, rd, wr, lambda g, T, X: fn(g.sync if q == "D" else g.scalar, T), kind="d", nb=nbytes)
+        add(q, 1500.0, rd, wr, lambda g, T, X: fn(g.sync if q == "D" else g.scalar, T), kind="d", nb=nbytes)
 
     def load(q, name, buf, lo, hi, c0, parts=128, size=4):
         dma(q, parts * (hi - lo) * size, [], [(buf, lo, hi)], lambda e, T: e.dma_start(T[buf][0:parts, lo:hi], T[name][:, c0:c0 + hi - lo]))
@@ -142,9 +142,10 @@ def program():
     def store(q, name, c0, buf, lo, hi, size=4):
         dma(q, 128 * (hi - lo) * size, [(buf, lo, hi)], [], lambda e, T: e.dma_start(T[name][:, c0:c0 + hi - lo], T[buf][:, lo:hi]))
 
-    def put(hop, dst, srcs, size):
-        k = add("G", 150.0, reg(*srcs), [], lambda g, T, X: X["put"](hop, lambda U: view(U, dst), [view(T, s) for s in srcs]), kind="s", tag="put")
-        add("R", REMOTE, [], reg(dst), None, kind="a", dep=(k,), nb=128 * ln(dst) * size * len(srcs))
+    def put(hop, size, *moves):
+        k = add("G", 150.0, reg(*[s for _, srcs in moves for s in srcs]), [],
+                lambda g, T, X: X["put"](hop, [(lambda U, d=d: view(U, d), [view(T, s) for s in srcs]) for d, srcs in moves]), kind="s", tag="put")
+        add("R", REMOTE, [], reg(*[d for d, _ in moves]), None, kind="a", dep=(k,), nb=sum(128 * ln(d) * size * len(srcs) for d, srcs in moves))
 
     def scatter(win, off, rd, fn):
         add("V", 50 + 16 * ln(off) * SCAT * CYC, reg(off, *rd), reg(win), lambda g, T, X: fn(g.vector, T, ind(T, win, off)), tag="scatter")
@@ -177,18 +178,19 @@ def program():
     sel(("thf", 0, 128, 1, 8), one8, [[1, 128]], A.is_ge, 0, -16)
     sel(b8, ("thf", 0, 128, 1, 8), [[-1, 128]], A.is_ge, 15, 16)
     sel(idf, one, [[-1, 128]], A.is_equal, 0, 1)
-    sel(("t1", 0, 128), blk, [[-1, 128]], A.is_gt, 0, 1)
     sel(("b8r", 0, 144, 1, 8), ("onef", 0, 144, 1, 8), [[1, 144]], A.is_equal, -15, -16)
     iota(("p15", 0, 16), [[0, 16]], 0, 1)
     iota(("ei", 0, 128), [[0, 8], [1, 16]], 0, 0)
     ms(("st0", 512, 1024), 1.0)
     ms(("l2", 0, 128, 1, 10), QB)
-    ms(("l2", 0, 128, 1, 9), 9.0)
-    ts(("ta", 0, 128), ("upf", 0, 128), 2.0, A.mult)
-    act(("l2", 0, 128, 1, 8), b8, scale=2.0)
-    act(("l1", 0, 128, 1, 8), b8, scale=-2.0)
-    ts(("tb", 0, 128), ("t1", 0, 128), -2.0, A.mult)
-    ts(("td", 0, 128), blk, -2.0, A.mult)
+    ms(("l2", 0, 128, 1, 9), 1.125)
+    ts(("ta", 0, 128), ("upf", 0, 128), 0.25, A.mult)
+    act(("l2", 0, 128, 1, 8), b8, scale=0.25)
+    act(("l1", 0, 128, 1, 8), b8, scale=-0.25)
+    ts(("td", 0, 128), blk, -0.25, A.mult)
+    tt(("tb", 0, 128), ("td", 0, 128), ("ta", 0, 128), A.add)
+    ms(("c148", 0, 128), C148)
+    act(("m80", 0, 256), ("lgi", 0, 256), bias=C148)
     for n, k in ((NI, -1.0), (I, 1.0), (HI, 0.5), (IH, 1.0)):
         act(n, idf, scale=k)
     cp(("tb0", 0, 256), ("tni", 0, 256))
@@ -203,15 +205,17 @@ def program():
         ms((n, 0, 144), 0.0)
     act(("dw", 15, 143, 16), ("blk", 0, 128, 16), scale=2048.0)
     act(("st0", 0, 256), ("spb", 0, 256), scale=-1.0, bias=255.0)
-    mm("bm", [(("bm", 0, 256), I, ("spb", 0, 256)), (("bm", 0, 256), NI, ("epb", 0, 256))])
-    act(("st0", 256, 512), ("bm", 0, 256))
+    mm("bk0", [(("bk0", 0, 256), I, ("spb", 0, 256)), (("bk0", 0, 256), NI, ("epb", 0, 256))])
+    act(("st0", 256, 512), ("bk0", 0, 256))
+    turn = [0]
     for d in range(1, 4):
-        put(d, ("st%d" % d, 0, 1024), [("st0", 0, 1024)], 2)
+        put(d, 2, (("st%d" % d, 0, 1024), [("st0", 0, 1024)]))
     ms(("onb", 0, 256), 1.0)
     ms(("m128", 0, 128), -128.0)
     ms(("m255", 0, 128), -255.0)
     ms(("rst", 0, 128), -1e9)
-    ms(("rst", 0, 128, 16), 1e9)
+    act(("rst", 0, 128, 16), ("onef", 0, 128, 16), scale=1e9, fn=AF.Silu)
+    ops[-1]["cost"] += 1300.0
     ms(("tab", 0, 96), 0.0)
     ts(("p15", 0, 16), ("p15", 0, 16), 15, A.bitwise_and)
     if any(b[2][1] == "d" for b in BATCHES):
@@ -233,7 +237,7 @@ def program():
     if "V" in ENG["ml"]:
         tt(("tab", 64, 80), ("p15", 0, 16), ("ei", 0, 16), A.is_ge)
     tt(("tab", 33, 49), ("p15", 0, 16), ("ei", 0, 16), A.is_equal)
-    ts(("tab", 33, 49), ("tab", 33, 49), 0.5, A.mult)
+    ts(("tab", 33, 49), ("tab", 33, 49), 4.0, A.mult)
     cp(("wf", 0, 1), ("wti", 0, 1))
     ts(("uw", 0, 128), blk, "wf", A.mult, -1.0, A.mult)
     act(("uwp", 0, 128), ("uw", 0, 128), scale=-1.0)
@@ -244,31 +248,32 @@ def program():
     add("V", vc(16), [("bu", 0, 16), ("posb", 0, 16)], [("kf", 0, 256)], lambda g, T, X: g.vector.tensor_tensor(T.kf[:, :, 0], T.bu[:, 0:16], T.posb[:, 0:16], A.add))
     for s in (1, 2, 4, 8):
         add("V", vc(16 * s), [("kf", 0, 256)], [("kf", 0, 256)], lambda g, T, X, s=s: g.vector.tensor_scalar(T.kf[:, :, s:2 * s], T.kf[:, :, 0:s], float(s), None, A.add))
+    cp(("cwf", 0, 1024), ("cw", 0, 1024), "G")
     for v in range(NV):
         L, Tn, st, Lo, To = "lb%d" % v, "tb%d" % v, "st%d" % (v % 4), "lo%d" % v, "td%d" % v
         last = v == NV - 1
         first[:] = [len(ops) - 1000 * last]
         if last:
             for ib, (lo, hi, _) in enumerate(BATCHES):
+                cp(("cw", 4 * lo, 4 * hi), ("cwf", 4 * lo, 4 * hi), "G")
                 cp(("cwo", 1536 * ib, 1536 * ib + 4 * (hi - lo)), ("cw", 4 * lo, 4 * hi), "G")
         for ip, (lo, hi, joint) in enumerate(FR):
-            act(("m8", lo, hi), (L, lo, hi), scale=0.125, bias=18.5 + EPS)
             for nb, (bank, tri, q, c0) in enumerate((("ba", "ta", "qa", 512), ("bb_", "tb", "qb", 768))):
                 o, off = (bank, lo, hi), spots(nb, lo, hi)
                 base = ([(o, (tri, 0, 128), (Tn, lo, hi)), (o, ("l2", 0, 128, 1, 10), (st, c0 + lo, c0 + hi, 1, 10))]
                         + ([(o, ("la", 0, 128, 1, 1), ("onb", lo, hi, 1, 1))] if nb and v else []))
                 mm(bank, base)
-                act((q, lo, hi), o, bias=-264.0)
+                act((q, lo, hi), o, bias=-33.0)
                 mm(bank, base + [(o, NI, (q, lo, hi))])
-                tt(("pi",) + off[1:], o, ("m8", lo, hi), A.mult)
+                tt(("pi",) + off[1:], o, ("m8%d" % v, lo, hi), A.mult)
                 if nb or not joint:
                     off = ("fo", 2 * lo, 2 * hi) if joint else off
                     ts(("pi",) + off[1:], ("pi",) + off[1:], 4095, A.bitwise_and)
                     cp(off, ("pi",) + off[1:], ENG["bo" if nb else "fo"][ip])
         for ib, (lo, hi, pq) in enumerate(BATCHES):
             bk = "bk%d" % (ib & 1)
-            o = ("bm", 256 + lo, 256 + hi)
-            mm("bm", [(o, ("td", 0, 128), (Tn, lo, hi)), (o, ("l1", 0, 128, 1, 8), (st, 512 + lo, 512 + hi, 1, 8)), (o, ("l2", 0, 128, 1, 8), (st, 768 + lo, 768 + hi, 1, 8))]
+            o = ("bk%d" % (1 - (ib & 1)), 320, 320 + hi - lo)
+            mm(o[0], [(o, ("td", 0, 128), (Tn, lo, hi)), (o, ("l1", 0, 128, 1, 8), (st, 512 + lo, 512 + hi, 1, 8)), (o, ("l2", 0, 128, 1, 8), (st, 768 + lo, 768 + hi, 1, 8))]
                + ([(o, ("la", 0, 128, 1, 1), ("onb", lo, hi, 1, 1))] if v else []) + [(o, NI, ("qb", lo, hi)), (o, I, ("qa", lo, hi))])
             act(("d2", lo, hi), o)
             for cl, ch, who in CHUNKS:
@@ -282,7 +287,8 @@ def program():
                 for l in range(cl, ch, 64):
                     u = min(l + 64, ch)
                     for h in (0, 1):
-                        bn, half = "bn%d" % h, [("ab%d" % h, 16 * l, 16 * u)]
+                        bn, half = "bn%d" % (turn[0] % 3), [("ab%d" % h, 16 * l, 16 * u)]
+                        turn[0] += 1
                         o = (bn, 0, 8 * (u - l))
                         mm(bn, [(o, I, ("pe", 16 * l + h, 16 * u, 2))] + [((bn, m, o[2], 8), I, (st, 256 + l, 256 + u)) for m in range(8)], closes=False)
                         mm(bn, [(o, I, ("sb", 16 * l + h, 16 * u, 2))], opens=False)
@@ -299,7 +305,7 @@ def program():
 
             def sm(nm):
                 return (nm, c0, c1)
-            os_, ou, u = ("bm", lo, hi), ("bu", c0, c1) if pq[1] == "r" else ("bu", 0, n), ("us", lo + 15, hi, 16)
+            os_, ou, u = (bk, 128, 128 + n), ("bu", c0, c1) if pq[1] == "r" else ("bu", 0, n), ("us", lo + 15, hi, 16)
 
             def weigh(res, full, x):
                 return [(ou, (res, 15 - r, 143 - r), (x, lo + r, hi, 16)) for r in range(16)] if pq[1] == "r" else [(ou, (full, 0, 128), (x, lo, hi))]
@@ -310,7 +316,7 @@ def program():
             cp(sm("posu"), sm("posi"), ENG["posu"][ib])
             ts(sm("xk"), key, SIGN | 15, A.bitwise_and)
             if last or ib == len(BATCHES) - 1:
-                cs, bc = ((c0, c1), bk) if last else ((0, 16), "bk0")
+                cs, bc = ((c0, c1), bk) if last else ((0, 16), "bk%d" % (1 - (ib & 1)))
                 if ENG["n1k"][ib] == "S":
                     act(("n1k",) + cs, ("xk",) + cs, scale=2.0 ** -13, bias=-0.002, fn=AF.Relu)
                 else:
@@ -318,15 +324,15 @@ def program():
                 if not last:
                     mm(bc, [((bc, 256, 272), ("onb", 0, 128), ("n1k", 0, 16))])
                     add("S", FS + 40, [(bc, 256, 272)], [("cnt", 0, 16), ("x2", 0, 1)],
-                        lambda g, T, X, bc=bc: g.scalar.activation(T.cnt[0:1, 0:16], T[bc][0:1, 256:272], AF.Identity, bias=896.0, scale=-2.0 / 1024, accum_out=T.x2[0:1, 0:1]))
-                    act(("nq", 0, 1, 1, 1), ("x2", 0, 1, 1, 1), scale=-1.0, bias=31.0)
+                        lambda g, T, X, bc=bc: g.scalar.activation(T.cnt[0:1, 0:16], T[bc][0:1, 256:272], AF.Identity, bias=112.0, scale=-0.25 / 1024, accum_out=T.x2[0:1, 0:1]))
+                    act(("nq", 0, 1, 1, 1), ("x2", 0, 1, 1, 1), scale=-1.0, bias=3.875)
                     add("S", FS - FV + vc(128), [("x2", 0, 1), ("nq", 0, 1), ("onb", 0, 128)], [("la", 0, 128)],
                         lambda g, T, X: g.scalar.activation(T.la[0:1, 0:128], T.onb[0:1, 0:128], AF.Identity, bias=T.nq[0:1, 0:1], scale=T.x2[0:1, 0:1]))
                 oc = (bc, 288 + cs[0], 288 + cs[1])
                 mm(bc, [(oc, I, ("n1k",) + cs), (oc, I, ("cb4" if last else "cb",) + cs)])
             if pq[0] == "S":
                 gather("S", ("pk", lo, hi), ("pe", a, b), sm("posu"))
-                mm("bm", [(os_, I, (st, lo, hi)), (os_, NI, ("pk", lo, hi))])
+                mm(bk, [(os_, I, (st, lo, hi)), (os_, NI, ("pk", lo, hi))])
                 act(("mp", lo, hi), os_, fn=AF.Relu)
                 mm("bu", weigh("uwr", "uw", "mp"), opens=False)
             else:
@@ -340,10 +346,13 @@ def program():
             cg, r1, both = ("li", 2 * c0, c0 + c1), ("li", c0 + c1, 2 * c1), (2 * c0, 2 * c1)
             ts(cg, u, 1023, A.bitwise_and)
             ts(sm("u15"), u, 15, A.bitwise_and)
-            tt(r1, sm("u15"), sm("rb"), A.add)
+            cp(("lu",) + cg[1:], cg, ENG["cg"][ib])
             if window(ib)[1] == 4096:
+                tt(r1, sm("u15"), sm("rb"), A.add)
                 ts(r1, r1, 4095, A.bitwise_and)
-            cp(("lu",) + both, ("li",) + both, ENG["lu"][ib])
+                cp(("lu",) + r1[1:], r1, ENG["lu"][ib])
+            else:
+                tt(("lu",) + r1[1:], sm("u15"), sm("rb"), A.add)
             for nm, k, c in (("ol", 1.0, 1.0 - SIGN), ("ml", -1.0, 16.0)):
                 if ENG[nm][ib] == "S":
                     act(sm(nm), sm("xk"), scale=k, bias=c, fn=AF.Relu)
@@ -353,14 +362,14 @@ def program():
                     ts(sm(nm), sm("xk"), c, A.min)
             gtt((To, lo, hi), ("tab", 32, 64), sm("ol"), ("d2", lo, hi), A.mult)
             if not last:
-                put(1, ("tb%d" % (v + 1), lo, hi), [(Tn, lo, hi), (To, lo, hi)], 2)
-            gtt(("dl", lo, hi), ("cw", 0, 1024), ("lu",) + cg[1:], (L, lo, hi), A.subtract)
+                put(1, 2, (("tb%d" % (v + 1), lo, hi), [(Tn, lo, hi), (To, lo, hi)]))
+            gtt(("dl", lo, hi), ("cwf", 0, 1024), ("lu",) + cg[1:], (L, lo, hi), A.subtract)
             gtt((Lo, lo, hi), ("tab", 0, 32) if ENG["ml"][ib] == "S" else ("tab", 64, 96), sm("ml"), ("dl", lo, hi), A.mult)
             if not last:
-                put(1, ("lb%d" % (v + 1), lo, hi), [(L, lo, hi), (Lo, lo, hi)], 4)
+                put(1, 4, (("m8%d" % (v + 1), lo, hi), [(L, lo, hi), (Lo, lo, hi), ("c148", 0, n)]), (("lb%d" % (v + 1), lo, hi), [(L, lo, hi), (Lo, lo, hi)]))
             gather("S", ("fk", lo, hi), ("ff", a, b), sm("posu"))
             gather("S", ("bk", lo, hi), ("fb", a, b), sm("posu"))
-            mm("bm", [(os_, HI, ("fk", lo, hi)), (os_, HI, ("bk", lo, hi))])
+            mm(bk, [(os_, HI, ("fk", lo, hi)), (os_, HI, ("bk", lo, hi))])
             act(("rr", lo, hi), os_, bias=127.875)
             if last:
                 o = ("ba", lo, hi)
@@ -370,9 +379,12 @@ def program():
                 act(("yt4", lo, hi), o, bias=49152.0)
                 store("S", "yt", lo, "yt4", lo, hi)
                 o = ("bb_", lo, hi)
-                mm("bb_", [(o, idf, (L, lo, hi))], closes=False)
-                mm("bb_", [(o, idf, (Lo, lo, hi))], opens=False)
-                act(("yl4", lo, hi), o)
+                mm("bb_", [(o, idf, (L, lo, hi))], closes=ENG["yl"][ib] == "V")
+                if ENG["yl"][ib] == "V":
+                    tt(("yl4", lo, hi), o, (Lo, lo, hi), A.add)
+                else:
+                    mm("bb_", [(o, idf, (Lo, lo, hi))], opens=False)
+                    act(("yl4", lo, hi), o)
                 store("S", "yl", lo, "yl4", lo, hi)
                 c3s = [(ib, lo, hi)]
             else:
@@ -380,10 +392,13 @@ def program():
             for ib, lo, hi in c3s:
                 c3 = ("c3", lo // 16, hi // 16)
                 ts(c3, ("us", lo + 15, hi, 16), 3, A.bitwise_and)
-                tt(c3, c3, oc, A.add)
-                cp(("c3u",) + c3[1:], c3, "V" if last else ENG["c3u"][ib])
-                scatter(("cwo", 1536 * ib, 1536 * ib + 1536) if last else ("cw", 0, 2048), ("c3u",) + c3[1:], [(L, lo, hi)],
-                        lambda e, T, w, L=L, lo=lo, hi=hi: e.tensor_copy(w, T[L][:, lo:hi]))
+                tt(("c3u",) + c3[1:], c3, oc, A.add)
+                if last or ENG["ctl"] == "V":
+                    scatter(("cwo", 1536 * ib, 1536 * ib + 1536) if last else ("cwf", 0, 2048), ("c3u",) + c3[1:], [(L, lo, hi)],
+                            lambda e, T, w, L=L, lo=lo, hi=hi: e.tensor_copy(w, T[L][:, lo:hi]))
+                else:
+                    add("S", 65 + 256 * SCAT * CYC, [("c3u", 0, 16), (L, 0, 256)], [("cwf", 0, 2048)],
+                        lambda g, T, X, L=L: g.scalar.activation(T.cwf[:, 0:2048].indirect(T.c3u[:, 0:16]), T[L][:, 0:256], AF.Silu), tag="scatter")
                 if last:
                     store("D", "yc", 4 * lo, "cwo", 1536 * ib, 1536 * ib + 4 * (hi - lo))
         for ib, (lo, hi, pq) in enumerate(BATCHES):
@@ -443,11 +458,39 @@ def schedule():
     kinds = {}
     kind = np.array([kinds.setdefault(o["cls"], len(kinds)) for o in ops])
     rng = np.random.default_rng(SEED)
-    for _ in range(ROUNDS):
+
+    def blocked(start, end):
+        before, last, pairs = {}, {}, []
+        for i in sorted(range(n), key=lambda j: start[j]):
+            before[i], last[que[i]] = last.get(que[i]), i
+        i = max(range(n), key=lambda j: end[j])
+        while i is not None:
+            tight = [d for d, g in lags[0][i] if end[d] + g > start[i] - 1.0]
+            if not tight and before[i] is not None and hold[i]:
+                pairs.append((i, before[i]))
+            i = tight[0] if tight else before[i] if hold[i] else None
+        return pairs
+    pairs = blocked(*now)
+    heads = [i for i in range(n) if ops[i]["cls"] == 0]
+    rows = [np.arange(h, h + heads[1] - heads[0]) for h in heads]
+    lead = [o["tag"] for o in ops[heads[0]:]].index("ff")
+    for k in range(ROUNDS):
         shift = (rng.random(len(kinds)) < SHARE) * (rng.random(len(kinds)) - 0.5) * JITTER
-        new = both([float(x) for x in np.array(now[0]) + shift[kind]])
-        if max(new[1]) <= max(now[1]) + 200 * rng.random():
+        if pairs and rng.random() < AIM:
+            i, j = pairs[int(rng.integers(len(pairs)))]
+            shift[:] = 0.0
+            shift[kind[i] if rng.random() < 0.5 else kind[j]] = now[0][i] - now[0][j] + rng.random() ** 2 * JITTER
+            shift[kind[i]] *= -1.0
+        key = np.array(now[0]) + shift[kind]
+        if rng.random() < COPY:
+            t0 = [now[0][row[lead]] for row in rows]
+            a = int(rng.integers(len(rows)))
+            for b, row in enumerate(rows):
+                key[row] = key[rows[a]] - t0[a] + t0[b]
+        new = both([float(x) for x in key])
+        if max(new[1]) <= max(now[1]) + SLACK * (1.0 - k / ROUNDS) * rng.random():
             now = new
+            pairs = blocked(*now)
             keep = min(keep, now, key=lambda x: max(x[1]))
     start, end = keep
     order = sorted(range(n), key=lambda i: (start[i], i))
@@ -491,15 +534,13 @@ def rank_program(g, core, T, topo):
     eng = {"V": g.vector, "S": g.scalar, "P": g.tensor, "G": g, "D": g.sync}
     n, sent, X = len(T.cores), [0], {}
 
-    def put(hop, dst, srcs):
+    def put(hop, moves):
         peer = T.cores[(rank + hop) % n]
         rid, pid, _ = topo.addr(peer)
-        sent[0] += len(topo.engines(core, peer))
-        if len(srcs) == 1:
-            g.remote_dma(dst(T), srcs[0], T.sem[X["ar"]], T.sem.loc, pid, rid, topo.mask(core, peer))
-        else:
-            g.remote_dma_fused([RemoteDMATransfer(dst_ids=[DstId(rid=rid, pnc=pid)], dma_engine_mask=topo.mask(core, peer), remote_sem=T.sem[X["ar"]],
-                                                  srcs=srcs, dsts=[dst(T)], alu_op=1)], local_sem=T.sem.loc)
+        es = topo.engines(core, peer)
+        sent[0] += len(es)
+        g.remote_dma_fused([RemoteDMATransfer(dst_ids=[DstId(rid=rid, pnc=pid)], dma_engine_mask=sum(1 << e for e in es[i::len(moves)]), remote_sem=T.sem[X["ar"]],
+                                              srcs=srcs, dsts=[dst(T)], alu_op=int(len(srcs) > 1)) for i, (dst, srcs) in enumerate(moves)], local_sem=T.sem.loc)
     X["put"] = put
     arr = {d: o["sem"] for o in ops if o["kind"] == "a" for d in o["deps"]}
     for i in order:

import numpy as np
from concourse.bass import DstId, RemoteDMATransfer
from concourse.mybir import AluOpType as A, ActivationFunctionType as AF

NV = 5
CHUNKS = [(192, 256, "SV-"), (128, 192, "SH-"), (64, 128, "SV-"), (0, 64, "SHh")]
BATCHES = [(128, 256, "Vr"), (0, 128, "Vr")]
FR = [(128, 256, 0), (0, 128, 1)]
ENG = {"fo": "VG", "bo": "VG", "posu": "VS", "ol": "VS", "ml": "VS", "ui": "VS", "lu": "GS", "cg": "VS", "n1k": "SS", "yl": "SV", "ctl": "S"}
ROT, C148, QB, SIGN = 167, 148.0 + 2.0 ** -10, 12288.0, 1 << 23
CYC, PCYC, GATH, SCAT, WAKE, REMOTE, RATE, FV, FS, MN = 0.85, 0.43, 1.55, 3.5, 170.0, 2200.0, 450.0, 45.0, 65.0, 24.0
ROUNDS, JITTER, SHARE, SLACK, AIM, COPY, SEED = 8000, 5000.0, 0.02, 800.0, 0.6, 0.03, 1
BANKS = ["ba", "bb_", "bn0", "bn1", "bn2", "bk0", "bk1", "bu"]
SIZES = {
    "bfloat16": "xw 4096 ff 4096 fb 4096 pe 4096 sb 4096 mk 2048 dw 144 uwr 144 uwq 144 uw 128 uwp 128 ib 128 inb 128 hib 128 onb 256 l1 128 l2 128 la 128 "
                "m128 128 m255 128 spb 256 epb 256 qa 256 qb 256 pk 256 mp 256 fk 256 bk 256 rr 256 d2 256 n1k 16 cb 16 cb4 16 nq 1 tab 96 "
                "st0 1024 st1 1024 st2 1024 st3 1024",
    "float32": "cwo 6144 wf 1 p15f 1 onef 144 t1 128 blk 128 idf 128 upf 128 b8 128 b8r 144 thf 256 rst 128 c148 128 m80 256 m81 256 m82 256 m83 256 m84 256 cwf 2048 yt4 256 yl4 256 x2 1 cnt 16 "
               "diag 128 mfw 128 ud 256 lb0 256 lb1 256 lb2 256 lb3 256 lb4 256 lo0 256 lo1 256 lo2 256 lo3 256 lo4 256",
    "float16": "ta 128 tb 128 td 128 ih 128 tb0 256 tb1 256 tb2 256 tb3 256 tb4 256 td0 256 td1 256 td2 256 td3 256 td4 256",
    "int32": "cw 1024 dl 256 lgi 256 tni 256 aai 256 bbi 256 thi 256 wti 1 p15 16 ei 128 kai 16 posb 16 rb 16 pi 512 kint 256 posi 16 xk 16 us 256 u15 16 li 32 c3 16",
    "uint16": "fo 512 posu 16 ml 16 ol 16 lu 32 c3u 16"}
SCRATCH = {n: ("psum", [128, 512], "float32") for n in BANKS}
for _d in SIZES:
    _l = SIZES[_d].split()
    for _i in range(0, len(_l), 2):
        SCRATCH[_l[_i]] = ("sbuf", [128, int(_l[_i + 1])], _d)
SCRATCH["ab"] = ("sbuf", [128, 16, 16, 16], "bfloat16")
SCRATCH["kf"] = ("sbuf", [128, 16, 16], "float32")
SEMAPHORES = ["qV", "qS", "qP", "qG", "loc"] + ["dm%d" % i for i in range(30)] + ["ar%d" % i for i in range(30)]
CACHE = {}


def program():
    ops, acc, num, first = [], {}, {"d": 0, "a": 0}, []

    def add(q, cost, rd, wr, emit, kind="c", dep=(), nb=0, tag=""):
        deps, k = set(dep), len(ops)
        for w, lst in ((0, rd), (1, wr)):
            for b, lo, hi in lst:
                for o, l, h, ow in acc.get(b, ()):
                    if b in BANKS:
                        if ops[o]["q"] != q or w or ow:
                            deps.add(o)
                    elif (w or ow) and l < hi and lo < h:
                        deps.add(o)
        for b, lo, hi in wr:
            acc[b] = [e for e in acc.get(b, ()) if not (b in BANKS or (lo <= e[1] and e[2] <= hi))] + [(k, lo, hi, 1)]
        for b, lo, hi in rd:
            acc.setdefault(b, []).append((k, lo, hi, 0))
        deps.discard(k)
        sem = None
        if kind in num:
            sem = ("dm%d" if kind == "d" else "ar%d") % num[kind]
            num[kind] += 1
        ops.append({"q": q, "cost": cost, "deps": deps, "emit": emit, "kind": kind, "sem": sem, "nb": nb, "tag": tag or (wr[0][0] if wr else ""),
                    "cls": k - first[0] if first else -k - 1})
        return k

    def vc(n, f=1.0):
        return FV + max(MN, n * f) * CYC

    def ln(a):
        return -(-(a[2] - a[1]) // abs(a[3] if len(a) > 3 else 1))

    def fast(*vs):
        return 0.5 if all(SCRATCH[a[0]][2] in ("bfloat16", "float16", "uint16") for a in vs) else 1.0

    def view(T, a):
        if len(a) == 5:
            return T[a[0]][0:a[4], a[1]:a[2]:a[3]]
        if len(a) == 4 and a[3] == -1:
            return T[a[0]][:, a[2] - 1:(a[1] - 1 if a[1] else None):-1]
        return T[a[0]][:, a[1]:a[2]:a[3]] if len(a) == 4 else T[a[0]][:, a[1]:a[2]]

    def reg(*vs):
        return [a[:3] for a in vs]

    def ind(T, win, off):
        return view(T, win).indirect(view(T, off))

    def tt(out, a, b, op):
        add("V", vc(ln(out), 1.0 if a[0] in BANKS or b[0] in BANKS else 2.0), reg(a, b), reg(out), lambda g, T, X: g.vector.tensor_tensor(view(T, out), view(T, a), view(T, b), op))

    def gtt(out, win, off, b, op):
        add("V", 50 + ln(out) * GATH * CYC, reg(win, off, b), reg(out), lambda g, T, X: g.vector.tensor_tensor(view(T, out), ind(T, win, off), view(T, b), op))

    def ts(out, a, s1, o1, s2=None, o2=None):
        def em(g, T, X):
            x1 = T[s1][:, 0:1] if isinstance(s1, str) else s1
            return g.vector.tensor_scalar(view(T, out), view(T, a), x1, s2, o1, o2) if o2 else g.vector.tensor_scalar(view(T, out), view(T, a), x1, None, o1)
        add("V", vc(ln(out), fast(out, a)), reg(a) + ([(s1, 0, 1)] if isinstance(s1, str) else []), reg(out), em)

    def ms(out, c):
        add("V", vc(ln(out), fast(out)), [], reg(out), lambda g, T, X: g.vector.memset(view(T, out), c))

    def scan(out, d0, d1, o0, o1):
        add("V", vc(ln(out), fast(out, d0, d1)), reg(d0, d1), reg(out), lambda g, T, X: g.vector.tensor_tensor_scan(view(T, out), view(T, d0), view(T, d1), 0.0, o0, o1))

    def act(out, a, scale=1.0, bias=0.0, fn=AF.Identity):
        add("S", FS - FV + vc(ln(out)), reg(a), reg(out), lambda g, T, X: g.scalar.activation(view(T, out), view(T, a), fn, bias=bias, scale=scale))

    def sel(out, src, pattern, cmp, base, cm):
        add("G", 170 + 2 * ln(out) * CYC, reg(src), reg(out), lambda g, T, X: g.affine_select(view(T, out), view(T, src), pattern, cmp, 0.0, base, cm))

    def cp(out, a, q="V"):
        if q == "V":
            add("V", vc(ln(out), fast(out, a)), reg(a), reg(out), lambda g, T, X: g.vector.tensor_copy(view(T, out), view(T, a)))
        elif q == "S":
            act(out, a)
        else:
            sel(out, a, [[0, ln(out)]], A.is_ge, 0, 0)

    def gather(q, out, win, off):
        if q == "H":
            for e, i in (("V", 0), ("S", 1)):
                gather(e, (out[0], out[1] + ln(out) // 2 * i, out[1] + ln(out) // 2 * (i + 1)), win, (off[0], off[1] + ln(off) // 2 * i, off[1] + ln(off) // 2 * (i + 1)))
        elif q == "S":
            add("S", 65 + ln(out) * GATH * CYC, reg(win, off), reg(out), lambda g, T, X: g.scalar.activation(view(T, out), ind(T, win, off), AF.Identity))
        else:
            add("V", 50 + ln(out) * GATH * CYC, reg(win, off), reg(out), lambda g, T, X: g.vector.tensor_copy(view(T, out), ind(T, win, off)))

    def mm(bank, terms, opens=True, closes=True):
        def em(g, T, X):
            for i, (o, lt, rh) in enumerate(terms):
                last = g.tensor.matmul(view(T, o), view(T, lt), rh[1](T) if len(rh) == 2 else view(T, rh), opens and i == 0, closes and i == len(terms) - 1)
            return last
        rd = []
        for o, lt, rh in terms:
            rd += reg(lt) + (rh[0] if len(rh) == 2 else reg(rh))
        add("P", sum(max(64, ln(o)) * PCYC * (4 if SCRATCH[lt[0]][2] == "float32" else 1) for o, lt, _ in terms), rd, [(bank, 0, 512)], em)

    def iota(out, pattern, base, cm):
        add("G", 130 + 2 * ln(out) * CYC, [], reg(out), lambda g, T, X: g.iota(view(T, out), pattern, base, cm))

    def dma(q, nbytes, rd, wr, fn):
        add(q, 1500.0, rd, wr, lambda g, T, X: fn(g.sync if q == "D" else g.scalar, T), kind="d", nb=nbytes)

    def load(q, name, buf, lo, hi, c0, parts=128, size=4):
        dma(q, parts * (hi - lo) * size, [], [(buf, lo, hi)], lambda e, T: e.dma_start(T[buf][0:parts, lo:hi], T[name][:, c0:c0 + hi - lo]))

    def store(q, name, c0, buf, lo, hi, size=4):
        dma(q, 128 * (hi - lo) * size, [(buf, lo, hi)], [], lambda e, T: e.dma_start(T[name][:, c0:c0 + hi - lo], T[buf][:, lo:hi]))

    def put(hop, size, *moves):
        k = add("G", 150.0, reg(*[s for _, srcs in moves for s in srcs]), [],
                lambda g, T, X: X["put"](hop, [(lambda U, d=d: view(U, d), [view(T, s) for s in srcs]) for d, srcs in moves]), kind="s", tag="put")
        add("R", REMOTE, [], reg(*[d for d, _ in moves]), None, kind="a", dep=(k,), nb=sum(128 * ln(d) * size * len(srcs) for d, srcs in moves))

    def scatter(win, off, rd, fn):
        add("V", 50 + 16 * ln(off) * SCAT * CYC, reg(off, *rd), reg(win), lambda g, T, X: fn(g.vector, T, ind(T, win, off)), tag="scatter")

    def window(ib):
        lo, hi = BATCHES[ib][:2]
        return (16 * lo + 160, 16 * hi + 176) if 16 * hi + 176 <= 4096 else (0, 4096)

    def spots(nb, cl, ch):
        lo, hi = [p[:2] for p in FR if p[0] <= cl < p[1]][0]
        return ("fo", lo + cl + nb * (hi - lo), lo + ch + nb * (hi - lo))

    load("D", "tn", "tni", 0, 256, 0)
    load("S", "lg", "lgi", 0, 256, 0)
    load("D", "aa", "aai", 0, 256, 0, 8)
    load("S", "bb", "bbi", 0, 256, 0, 8)
    load("D", "xt", "xw", ROT, 4096, 0, size=2)
    load("S", "xt", "xw", 0, ROT, 4096 - ROT, size=2)
    load("D", "sp", "spb", 0, 256, 0, size=2)
    load("S", "ep", "epb", 0, 256, 0, size=2)
    load("D", "th", "thi", 0, 256, 0, 8)
    load("S", "wt", "wti", 0, 1, 0)
    load("D", "ct", "cw", 0, 1024, 0)
    ms(("onef", 0, 144), 1.0)
    one, blk, idf, b8, one8 = ("onef", 0, 128), ("blk", 0, 128), ("idf", 0, 128), ("b8", 0, 128, 1, 8), ("onef", 0, 128, 1, 8)
    I, NI, HI, IH, xw = ("ib", 0, 128), ("inb", 0, 128), ("hib", 0, 128), ("ih", 0, 128), ("xw", 0, 4096)
    sel(("t1", 0, 128), one, [[-16, 8], [0, 16]], A.is_ge, 0, 1)
    sel(blk, ("t1", 0, 128), [[16, 8], [0, 16]], A.is_ge, 15, -1)
    sel(("upf", 0, 128), blk, [[1, 128]], A.is_ge, 0, -1)
    sel(("thf", 0, 128, 1, 8), one8, [[1, 128]], A.is_ge, 0, -16)
    sel(b8, ("thf", 0, 128, 1, 8), [[-1, 128]], A.is_ge, 15, 16)
    sel(idf, one, [[-1, 128]], A.is_equal, 0, 1)
    sel(("b8r", 0, 144, 1, 8), ("onef", 0, 144, 1, 8), [[1, 144]], A.is_equal, -15, -16)
    iota(("p15", 0, 16), [[0, 16]], 0, 1)
    iota(("ei", 0, 128), [[0, 8], [1, 16]], 0, 0)
    ms(("st0", 512, 1024), 1.0)
    ms(("l2", 0, 128, 1, 10), QB)
    ms(("l2", 0, 128, 1, 9), 1.125)
    ts(("ta", 0, 128), ("upf", 0, 128), 0.25, A.mult)
    act(("l2", 0, 128, 1, 8), b8, scale=0.25)
    act(("l1", 0, 128, 1, 8), b8, scale=-0.25)
    ts(("td", 0, 128), blk, -0.25, A.mult)
    tt(("tb", 0, 128), ("td", 0, 128), ("ta", 0, 128), A.add)
    ms(("c148", 0, 128), C148)
    act(("m80", 0, 256), ("lgi", 0, 256), bias=C148)
    for n, k in ((NI, -1.0), (I, 1.0), (HI, 0.5), (IH, 1.0)):
        act(n, idf, scale=k)
    cp(("tb0", 0, 256), ("tni", 0, 256))
    cp(("lb0", 0, 256), ("lgi", 0, 256), "S")
    cp(("st0", 512, 768, 1, 8), ("aai", 0, 256, 1, 8))
    cp(("st0", 768, 1024, 1, 8), ("bbi", 0, 256, 1, 8), "S")
    width = 16 * max(c[1] - c[0] for c in CHUNKS)
    ms(("mk", 0, width), 1.0)
    ms(("mk", 15, width, 16), 0.0)
    ms(("pe", 0, 4096, 256), 0.0)
    for n in ("dw", "uwr", "uwq"):
        ms((n, 0, 144), 0.0)
    act(("dw", 15, 143, 16), ("blk", 0, 128, 16), scale=2048.0)
    act(("st0", 0, 256), ("spb", 0, 256), scale=-1.0, bias=255.0)
    mm("bk0", [(("bk0", 0, 256), I, ("spb", 0, 256)), (("bk0", 0, 256), NI, ("epb", 0, 256))])
    act(("st0", 256, 512), ("bk0", 0, 256))
    turn = [0]
    for d in range(1, 4):
        put(d, 2, (("st%d" % d, 0, 1024), [("st0", 0, 1024)]))
    ms(("onb", 0, 256), 1.0)
    ms(("m128", 0, 128), -128.0)
    ms(("m255", 0, 128), -255.0)
    ms(("rst", 0, 128), -1e9)
    act(("rst", 0, 128, 16), ("onef", 0, 128, 16), scale=1e9, fn=AF.Silu)
    ops[-1]["cost"] += 1300.0
    ms(("tab", 0, 96), 0.0)
    ts(("p15", 0, 16), ("p15", 0, 16), 15, A.bitwise_and)
    if any(b[2][1] == "d" for b in BATCHES):
        ms(("mfw", 0, 128), 1.0)
        ms(("mfw", 0, 128, 16), 0.0)
        cp(("p15f", 0, 1), ("p15", 0, 1))
        ts(("diag", 0, 128), ("ei", 0, 128), "p15f", A.is_equal)
    ts(("kai", 0, 16), ("ei", 0, 16), 16.0, A.mult)
    tt(("kai", 0, 16), ("kai", 0, 16), ("p15", 0, 16), A.add)
    act(("cb", 0, 16), ("kai", 0, 16), scale=4.0)
    for ib, (lo, hi, _) in enumerate(BATCHES):
        c = ("kai", lo // 16, hi // 16)
        act(("rb",) + c[1:], c, scale=16.0, bias=float(ROT - window(ib)[0]))
        act(("posb",) + c[1:], c, scale=16.0, bias=float(-16 * lo))
        act(("cb4",) + c[1:], c, scale=4.0, bias=float(-4 * lo))
    if "S" in ENG["ml"]:
        tt(("u15", 0, 16), ("ei", 0, 16), ("p15", 0, 16), A.add)
        ts(("tab", 1, 17), ("u15", 0, 16), 15.0, A.is_ge)
    if "V" in ENG["ml"]:
        tt(("tab", 64, 80), ("p15", 0, 16), ("ei", 0, 16), A.is_ge)
    tt(("tab", 33, 49), ("p15", 0, 16), ("ei", 0, 16), A.is_equal)
    ts(("tab", 33, 49), ("tab", 33, 49), 4.0, A.mult)
    cp(("wf", 0, 1), ("wti", 0, 1))
    ts(("uw", 0, 128), blk, "wf", A.mult, -1.0, A.mult)
    act(("uwp", 0, 128), ("uw", 0, 128), scale=-1.0)
    act(("uwr", 15, 143, 16), ("uw", 0, 128, 16))
    act(("uwq", 15, 143, 16), ("uw", 0, 128, 16), scale=-1.0)
    act(("thf", 0, 256, 1, 8), ("thi", 0, 256, 1, 8), scale=-2048.0, bias=-2048.0)
    mm("bu", [(("bu", 0, 16), ("b8r", 15 - r, 143 - r, 1, 8), ("thf", r, 256, 16, 8)) for r in range(16)])
    add("V", vc(16), [("bu", 0, 16), ("posb", 0, 16)], [("kf", 0, 256)], lambda g, T, X: g.vector.tensor_tensor(T.kf[:, :, 0], T.bu[:, 0:16], T.posb[:, 0:16], A.add))
    for s in (1, 2, 4, 8):
        add("V", vc(16 * s), [("kf", 0, 256)], [("kf", 0, 256)], lambda g, T, X, s=s: g.vector.tensor_scalar(T.kf[:, :, s:2 * s], T.kf[:, :, 0:s], float(s), None, A.add))
    cp(("cwf", 0, 1024), ("cw", 0, 1024), "G")
    for v in range(NV):
        L, Tn, st, Lo, To = "lb%d" % v, "tb%d" % v, "st%d" % (v % 4), "lo%d" % v, "td%d" % v
        last = v == NV - 1
        first[:] = [len(ops) - 1000 * last]
        if last:
            for ib, (lo, hi, _) in enumerate(BATCHES):
                cp(("cw", 4 * lo, 4 * hi), ("cwf", 4 * lo, 4 * hi), "G")
                cp(("cwo", 1536 * ib, 1536 * ib + 4 * (hi - lo)), ("cw", 4 * lo, 4 * hi), "G")
        for ip, (lo, hi, joint) in enumerate(FR):
            for nb, (bank, tri, q, c0) in enumerate((("ba", "ta", "qa", 512), ("bb_", "tb", "qb", 768))):
                o, off = (bank, lo, hi), spots(nb, lo, hi)
                base = ([(o, (tri, 0, 128), (Tn, lo, hi)), (o, ("l2", 0, 128, 1, 10), (st, c0 + lo, c0 + hi, 1, 10))]
                        + ([(o, ("la", 0, 128, 1, 1), ("onb", lo, hi, 1, 1))] if nb and v else []))
                mm(bank, base)
                act((q, lo, hi), o, bias=-33.0)
                mm(bank, base + [(o, NI, (q, lo, hi))])
                tt(("pi",) + off[1:], o, ("m8%d" % v, lo, hi), A.mult)
                if nb or not joint:
                    off = ("fo", 2 * lo, 2 * hi) if joint else off
                    ts(("pi",) + off[1:], ("pi",) + off[1:], 4095, A.bitwise_and)
                    cp(off, ("pi",) + off[1:], ENG["bo" if nb else "fo"][ip])
        for ib, (lo, hi, pq) in enumerate(BATCHES):
            bk = "bk%d" % (ib & 1)
            o = ("bk%d" % (1 - (ib & 1)), 320, 320 + hi - lo)
            mm(o[0], [(o, ("td", 0, 128), (Tn, lo, hi)), (o, ("l1", 0, 128, 1, 8), (st, 512 + lo, 512 + hi, 1, 8)), (o, ("l2", 0, 128, 1, 8), (st, 768 + lo, 768 + hi, 1, 8))]
               + ([(o, ("la", 0, 128, 1, 1), ("onb", lo, hi, 1, 1))] if v else []) + [(o, NI, ("qb", lo, hi)), (o, I, ("qa", lo, hi))])
            act(("d2", lo, hi), o)
            for cl, ch, who in CHUNKS:
                if not lo <= cl < hi:
                    continue
                a, b = 16 * cl, 16 * ch
                gather(who[0], ("ff", a, b), xw, spots(0, cl, ch))
                scan(("pe", a + 1, b), ("ff", a, b - 1), ("mk", 0, b - a - 1), A.add, A.mult)
                gather(who[1], ("fb", a, b), xw, spots(1, cl, ch))
                scan(("sb", a, b, -1), ("mk", 0, b - a, -1), ("fb", a, b, -1), A.mult, A.add)
                for l in range(cl, ch, 64):
                    u = min(l + 64, ch)
                    for h in (0, 1):
                        bn, half = "bn%d" % (turn[0] % 3), [("ab%d" % h, 16 * l, 16 * u)]
                        turn[0] += 1
                        o = (bn, 0, 8 * (u - l))
                        mm(bn, [(o, I, ("pe", 16 * l + h, 16 * u, 2))] + [((bn, m, o[2], 8), I, (st, 256 + l, 256 + u)) for m in range(8)], closes=False)
                        mm(bn, [(o, I, ("sb", 16 * l + h, 16 * u, 2))], opens=False)
                        add("S", FS - FV + vc(o[2]), [o], half, lambda g, T, X, l=l, u=u, h=h, o=o: g.scalar.activation(T.ab[:, l // 16:u // 16, :, h:16:2], view(T, o), AF.Abs))
                        if who[2] == "h":
                            add("V", vc(o[2], 0.5), half, half, lambda g, T, X, l=l, u=u, h=h: g.vector.tensor_scalar(T.ab[:, l // 16:u // 16, :, h:16:2], T.ab[:, l // 16:u // 16, :, h:16:2], 255.0, None, A.min))
                c0, c1, both = cl // 16, ch // 16, [("ab0", a, b), ("ab1", a, b)]
                if who[2] != "h":
                    add("V", vc(b - a, 0.5), both, both, lambda g, T, X, c0=c0, c1=c1: g.vector.tensor_scalar(T.ab[:, c0:c1], T.ab[:, c0:c1], 255.0, None, A.min))
                od = (bk, cl - lo, ch - lo)
                mm(bk, [(od, idf, ([("kf", cl, ch)], lambda T, c0=c0, c1=c1: T.kf[:, c0:c1]))], closes=False)
                mm(bk, [(od, ("dw", 15 - r, 143 - r), (both, lambda T, r=r, c0=c0, c1=c1: T.ab[:, c0:c1, r, :])) for r in range(16)], opens=False)
            a, b, n, c0, c1 = 16 * lo, 16 * hi, hi - lo, lo // 16, hi // 16

            def sm(nm):
                return (nm, c0, c1)
            os_, ou, u = (bk, 128, 128 + n), ("bu", c0, c1) if pq[1] == "r" else ("bu", 0, n), ("us", lo + 15, hi, 16)

            def weigh(res, full, x):
                return [(ou, (res, 15 - r, 143 - r), (x, lo + r, hi, 16)) for r in range(16)] if pq[1] == "r" else [(ou, (full, 0, 128), (x, lo, hi))]
            mm("bu", [(ou, ("uw", 0, 128), ("m255", 0, ln(ou)))] + (weigh("uwr", "uw", st) if pq[0] == "V" else []), closes=False)
            scan(("kint", lo, hi), ("rst", 0, n), (bk, 0, n), A.max, A.min)
            key = ("kint", lo + 15, hi, 16)
            ts(sm("posi"), key, 2047, A.bitwise_and)
            cp(sm("posu"), sm("posi"), ENG["posu"][ib])
            ts(sm("xk"), key, SIGN | 15, A.bitwise_and)
            if last or ib == len(BATCHES) - 1:
                cs, bc = ((c0, c1), bk) if last else ((0, 16), "bk%d" % (1 - (ib & 1)))
                if ENG["n1k"][ib] == "S":
                    act(("n1k",) + cs, ("xk",) + cs, scale=2.0 ** -13, bias=-0.002, fn=AF.Relu)
                else:
                    ts(("n1k",) + cs, ("kint", 16 * cs[0] + 15, 16 * cs[1], 16), 0.0, A.is_lt, 1024.0, A.mult)
                if not last:
                    mm(bc, [((bc, 256, 272), ("onb", 0, 128), ("n1k", 0, 16))])
                    add("S", FS + 40, [(bc, 256, 272)], [("cnt", 0, 16), ("x2", 0, 1)],
                        lambda g, T, X, bc=bc: g.scalar.activation(T.cnt[0:1, 0:16], T[bc][0:1, 256:272], AF.Identity, bias=112.0, scale=-0.25 / 1024, accum_out=T.x2[0:1, 0:1]))
                    act(("nq", 0, 1, 1, 1), ("x2", 0, 1, 1, 1), scale=-1.0, bias=3.875)
                    add("S", FS - FV + vc(128), [("x2", 0, 1), ("nq", 0, 1), ("onb", 0, 128)], [("la", 0, 128)],
                        lambda g, T, X: g.scalar.activation(T.la[0:1, 0:128], T.onb[0:1, 0:128], AF.Identity, bias=T.nq[0:1, 0:1], scale=T.x2[0:1, 0:1]))
                oc = (bc, 288 + cs[0], 288 + cs[1])
                mm(bc, [(oc, I, ("n1k",) + cs), (oc, I, ("cb4" if last else "cb",) + cs)])
            if pq[0] == "S":
                gather("S", ("pk", lo, hi), ("pe", a, b), sm("posu"))
                mm(bk, [(os_, I, (st, lo, hi)), (os_, NI, ("pk", lo, hi))])
                act(("mp", lo, hi), os_, fn=AF.Relu)
                mm("bu", weigh("uwr", "uw", "mp"), opens=False)
            else:
                gtt(("mp", lo, hi), ("pe", a, b), sm("posu"), (st, lo, hi), A.min)
                mm("bu", weigh("uwq", "uwp", "mp"), opens=False)
            if pq[1] == "r":
                cp(u, ou, ENG["ui"][ib])
            else:
                tt(("ud", lo, hi), ou, ("diag", 0, n), A.mult)
                scan(("us", lo, hi), ("mfw", 0, n), ("ud", lo, hi), A.mult, A.add)
            cg, r1, both = ("li", 2 * c0, c0 + c1), ("li", c0 + c1, 2 * c1), (2 * c0, 2 * c1)
            ts(cg, u, 1023, A.bitwise_and)
            ts(sm("u15"), u, 15, A.bitwise_and)
            cp(("lu",) + cg[1:], cg, ENG["cg"][ib])
            if window(ib)[1] == 4096:
                tt(r1, sm("u15"), sm("rb"), A.add)
                ts(r1, r1, 4095, A.bitwise_and)
                cp(("lu",) + r1[1:], r1, ENG["lu"][ib])
            else:
                tt(("lu",) + r1[1:], sm("u15"), sm("rb"), A.add)
            for nm, k, c in (("ol", 1.0, 1.0 - SIGN), ("ml", -1.0, 16.0)):
                if ENG[nm][ib] == "S":
                    act(sm(nm), sm("xk"), scale=k, bias=c, fn=AF.Relu)
                elif k > 0:
                    ts(sm(nm), sm("xk"), c, A.add, 0.0, A.max)
                else:
                    ts(sm(nm), sm("xk"), c, A.min)
            gtt((To, lo, hi), ("tab", 32, 64), sm("ol"), ("d2", lo, hi), A.mult)
            if not last:
                put(1, 2, (("tb%d" % (v + 1), lo, hi), [(Tn, lo, hi), (To, lo, hi)]))
            gtt(("dl", lo, hi), ("cwf", 0, 1024), ("lu",) + cg[1:], (L, lo, hi), A.subtract)
            gtt((Lo, lo, hi), ("tab", 0, 32) if ENG["ml"][ib] == "S" else ("tab", 64, 96), sm("ml"), ("dl", lo, hi), A.mult)
            if not last:
                put(1, 4, (("m8%d" % (v + 1), lo, hi), [(L, lo, hi), (Lo, lo, hi), ("c148", 0, n)]), (("lb%d" % (v + 1), lo, hi), [(L, lo, hi), (Lo, lo, hi)]))
            gather("S", ("fk", lo, hi), ("ff", a, b), sm("posu"))
            gather("S", ("bk", lo, hi), ("fb", a, b), sm("posu"))
            mm(bk, [(os_, HI, ("fk", lo, hi)), (os_, HI, ("bk", lo, hi))])
            act(("rr", lo, hi), os_, bias=127.875)
            if last:
                o = ("ba", lo, hi)
                mm("ba", [(o, IH, (Tn, lo, hi)), (o, IH, (To, lo, hi))])
                act(("qa", lo, hi), o, bias=49024.5)
                mm("ba", [(o, IH, (Tn, lo, hi)), (o, IH, (To, lo, hi)), (o, NI, ("qa", lo, hi))])
                act(("yt4", lo, hi), o, bias=49152.0)
                store("S", "yt", lo, "yt4", lo, hi)
                o = ("bb_", lo, hi)
                mm("bb_", [(o, idf, (L, lo, hi))], closes=ENG["yl"][ib] == "V")
                if ENG["yl"][ib] == "V":
                    tt(("yl4", lo, hi), o, (Lo, lo, hi), A.add)
                else:
                    mm("bb_", [(o, idf, (Lo, lo, hi))], opens=False)
                    act(("yl4", lo, hi), o)
                store("S", "yl", lo, "yl4", lo, hi)
                c3s = [(ib, lo, hi)]
            else:
                c3s = [(ib, 0, 256)] if ib == len(BATCHES) - 1 else []
            for ib, lo, hi in c3s:
                c3 = ("c3", lo // 16, hi // 16)
                ts(c3, ("us", lo + 15, hi, 16), 3, A.bitwise_and)
                tt(("c3u",) + c3[1:], c3, oc, A.add)
                if last or ENG["ctl"] == "V":
                    scatter(("cwo", 1536 * ib, 1536 * ib + 1536) if last else ("cwf", 0, 2048), ("c3u",) + c3[1:], [(L, lo, hi)],
                            lambda e, T, w, L=L, lo=lo, hi=hi: e.tensor_copy(w, T[L][:, lo:hi]))
                else:
                    add("S", 65 + 256 * SCAT * CYC, [("c3u", 0, 16), (L, 0, 256)], [("cwf", 0, 2048)],
                        lambda g, T, X, L=L: g.scalar.activation(T.cwf[:, 0:2048].indirect(T.c3u[:, 0:16]), T[L][:, 0:256], AF.Silu), tag="scatter")
                if last:
                    store("D", "yc", 4 * lo, "cwo", 1536 * ib, 1536 * ib + 4 * (hi - lo))
        for ib, (lo, hi, pq) in enumerate(BATCHES):
            c0, c1 = lo // 16, hi // 16
            scatter(("xw",) + window(ib), ("lu", c0 + c1, 2 * c1), [("rr", lo, hi), ("m128", 0, hi - lo)],
                    lambda e, T, w, lo=lo, hi=hi: e.tensor_tensor(w, T.rr[:, lo:hi], T.m128[:, 0:hi - lo], A.add))
    wl, wh = window(len(BATCHES) - 1)
    store("D", "yx", wh - ROT, "xw", wh, 4096, 2)
    store("D", "yx", 4096 - ROT, "xw", 0, wl, 2)
    store("S", "yx", 4096 - ROT + wl, "xw", wl, ROT, 2)
    store("D", "yx", 0, "xw", ROT, wh, 2)
    return ops


def schedule():
    ops = program()
    n = len(ops)
    pred, succ = [sorted(o["deps"]) for o in ops], [[] for _ in ops]
    for i in range(n):
        for d in pred[i]:
            succ[d].append(i)
    que, cost, move = [o["q"] for o in ops], [o["cost"] for o in ops], [o["nb"] / RATE for o in ops]
    hold = [70.0 if o["kind"] == "d" else 0.0 if o["q"] == "R" else o["cost"] for o in ops]
    lags = [[[(d, 0.0 if que[d] == que[i] == "P" else WAKE) for d in links[i]] for i in range(n)] for links in (pred, succ)]

    def fit(busy, t, w):
        k, hi = 0, len(busy)
        while k < hi:
            m = (k + hi) // 2
            k, hi = (k, m) if busy[m][1] > t else (m + 1, hi)
        while k < len(busy) and busy[k][0] < t + w:
            t, k = max(t, busy[k][1]), k + 1
        busy.insert(k, (t, t + w))
        return t

    def lay(key, back):
        busy, start, end = {q: [] for q in set(que) | {"bytes"}}, [0.0] * n, [0.0] * n
        for i in sorted(range(n), key=lambda j: key[j]):
            t = max([end[d] + g for d, g in lags[back][i]] or [0.0])
            if back:
                t = (fit(busy["bytes"], t + cost[i], move[i]) + move[i] if move[i] else t + cost[i]) - hold[i]
            start[i] = t = fit(busy[que[i]], t, hold[i]) if hold[i] else t
            end[i] = t + hold[i] if back else (fit(busy["bytes"], t, move[i]) + move[i] if move[i] else t) + cost[i]
        return start, end

    def both(key):
        for i in range(n):
            key[i] = max([key[i]] + [key[d] + 1e-3 for d in pred[i]])
        end = lay(key, 0)[1]
        end = lay([-x for x in end], 1)[1]
        return lay([-x for x in end], 0)

    prio = [0.0] * n
    for i in range(n - 1, -1, -1):
        prio[i] = cost[i] + move[i] + max([prio[s] + WAKE for s in succ[i]] or [0.0])
    now = keep = both([-p for p in prio])
    kinds = {}
    kind = np.array([kinds.setdefault(o["cls"], len(kinds)) for o in ops])
    rng = np.random.default_rng(SEED)

    def blocked(start, end):
        before, last, pairs = {}, {}, []
        for i in sorted(range(n), key=lambda j: start[j]):
            before[i], last[que[i]] = last.get(que[i]), i
        i = max(range(n), key=lambda j: end[j])
        while i is not None:
            tight = [d for d, g in lags[0][i] if end[d] + g > start[i] - 1.0]
            if not tight and before[i] is not None and hold[i]:
                pairs.append((i, before[i]))
            i = tight[0] if tight else before[i] if hold[i] else None
        return pairs
    pairs = blocked(*now)
    heads = [i for i in range(n) if ops[i]["cls"] == 0]
    rows = [np.arange(h, h + heads[1] - heads[0]) for h in heads]
    lead = [o["tag"] for o in ops[heads[0]:]].index("ff")
    for k in range(ROUNDS):
        shift = (rng.random(len(kinds)) < SHARE) * (rng.random(len(kinds)) - 0.5) * JITTER
        if pairs and rng.random() < AIM:
            i, j = pairs[int(rng.integers(len(pairs)))]
            shift[:] = 0.0
            shift[kind[i] if rng.random() < 0.5 else kind[j]] = now[0][i] - now[0][j] + rng.random() ** 2 * JITTER
            shift[kind[i]] *= -1.0
        key = np.array(now[0]) + shift[kind]
        if rng.random() < COPY:
            t0 = [now[0][row[lead]] for row in rows]
            a = int(rng.integers(len(rows)))
            for b, row in enumerate(rows):
                key[row] = key[rows[a]] - t0[a] + t0[b]
        new = both([float(x) for x in key])
        if max(new[1]) <= max(now[1]) + SLACK * (1.0 - k / ROUNDS) * rng.random():
            now = new
            pairs = blocked(*now)
            keep = min(keep, now, key=lambda x: max(x[1]))
    start, end = keep
    order = sorted(range(n), key=lambda i: (start[i], i))
    count, fin, know, qk, waits = {}, [None] * n, [None] * n, {}, [[] for _ in ops]
    for i in order:
        o = ops[i]
        if o["kind"] == "c":
            s = "q" + o["q"]
            count[s] = count.get(s, 0) + 1
            fin[i] = (s, count[s])
        elif o["kind"] in "da":
            fin[i] = (o["sem"], 16)
    for i in order:
        o = ops[i]
        q = o["q"]
        if q == "R":
            know[i] = dict([fin[i]])
            continue
        k, need = qk.setdefault(q, {}), {}
        for d in sorted(o["deps"], key=lambda d: -end[d]):
            s, x = fin[d]
            if (q == "P" and ops[d]["q"] == "P") or k.get(s, 0) >= x:
                continue
            need[s] = max(need.get(s, 0), x)
            for s2, x2 in know[d].items():
                k[s2] = max(k.get(s2, 0), x2)
        waits[i] = sorted(need.items())
        know[i] = dict(k)
        if fin[i]:
            know[i][fin[i][0]] = max(know[i].get(fin[i][0], 0), fin[i][1])
    return ops, order, waits, fin, count, start, end


def rank_program(g, core, T, topo):
    rank = T.rank_of(core)
    if rank is None:
        return
    if "s" not in CACHE:
        CACHE["s"] = schedule()
    ops, order, waits, fin, count, start, end = CACHE["s"]
    eng = {"V": g.vector, "S": g.scalar, "P": g.tensor, "G": g, "D": g.sync}
    n, sent, X = len(T.cores), [0], {}

    def put(hop, moves):
        peer = T.cores[(rank + hop) % n]
        rid, pid, _ = topo.addr(peer)
        es = topo.engines(core, peer)
        sent[0] += len(es)
        g.remote_dma_fused([RemoteDMATransfer(dst_ids=[DstId(rid=rid, pnc=pid)], dma_engine_mask=sum(1 << e for e in es[i::len(moves)]), remote_sem=T.sem[X["ar"]],
                                              srcs=srcs, dsts=[dst(T)], alu_op=int(len(srcs) > 1)) for i, (dst, srcs) in enumerate(moves)], local_sem=T.sem.loc)
    X["put"] = put
    arr = {d: o["sem"] for o in ops if o["kind"] == "a" for d in o["deps"]}
    for i in order:
        o = ops[i]
        if o["q"] == "R":
            continue
        for s, x in waits[i]:
            eng[o["q"]].wait_ge(T.sem[s], x)
        X["ar"] = arr.get(i)
        h = o["emit"](g, T, X)
        if fin[i]:
            h.then_inc(T.sem[fin[i][0]], 1 if o["kind"] == "c" else 16)
    for s in sorted(count):
        g.wait_ge(T.sem[s], count[s])
    for o in ops:
        if o["sem"]:
            g.wait_ge(T.sem[o["sem"]], 16)
    g.wait_ge(T.sem.loc, sent[0])
